import numpy as np
import ml_dtypes


def mxq(x, axis, fmt="e4m3"):
    dtype, down = {"e4m3": (ml_dtypes.float8_e4m3fn, 7), "e5m2": (ml_dtypes.float8_e5m2, 14)}[fmt]
    v = np.moveaxis(np.asarray(x, np.float32).astype(ml_dtypes.bfloat16).astype(np.float64), axis, -1)
    blocks = v.reshape(v.shape[:-1] + (-1, 32))
    amax = np.abs(blocks).max(-1, keepdims=True)
    byte = np.maximum(np.where(amax > 0, np.frexp(amax)[1] - 1 + 127, 0) - down, 1)
    scale = np.exp2(byte - 127.0)
    codes = (blocks / scale).astype(np.float32).astype(dtype).astype(np.float64)
    return np.moveaxis((codes * scale).reshape(v.shape), -1, axis)


WIDE = False


def mx_kscale(k):
    if not WIDE:
        return np.ones(k)
    levels = np.array([10, -10, 5, -5, 0])
    if k % 512:
        return np.exp2(np.random.permutation(np.resize(levels, k // 32))).repeat(32)
    a = np.empty((k // 512, 16))
    for p in range(k // 512):
        a[p, :8] = np.random.permutation(np.resize(levels, 8))
        for g in range(8):
            far = levels[np.abs(levels - a[p, g]) >= 10]
            a[p, g + 8] = far[np.random.randint(len(far))]
    return np.exp2(a.ravel()).repeat(32)


def f64(x):
    return np.asarray(x).astype(np.float64)


def striped(idx):
    return np.tile(idx.reshape(-1, 16).T, (8, 1)).astype(np.uint16)


def unstriped(offs):
    return offs[:16].T.reshape(-1).astype(np.int64)


E2M1 = np.array([0.0, 0.5, 1.0, 1.5, 2.0, 3.0, 4.0, 6.0, -0.0, -0.5, -1.0, -1.5, -2.0, -3.0, -4.0, -6.0])


def pack_weight(w, fmt):
    k, n = w.shape
    w = f64(np.asarray(w, np.float32).astype(ml_dtypes.bfloat16)).reshape(k // 32, 32, n)
    amax = np.abs(w).max(1)
    if fmt == "e4m3":
        byte = np.frexp(amax)[1] - 1 + 127 - 7
    else:
        mant, ex = np.frexp(amax / 6.0)
        byte = np.where(mant > 0.5, ex, ex - 1) + 127
    byte = np.clip(np.where(amax > 0, byte, 1), 1, 254)
    scaled = (w * np.exp2(127.0 - byte)[:, None, :]).reshape(k, n).astype(np.float32)
    by_word = np.ascontiguousarray(scaled.reshape(k // 512, 128, 4, n).transpose(0, 1, 3, 2))
    if fmt == "e4m3":
        words = by_word.astype(ml_dtypes.float8_e4m3fn).view(np.uint8)
    else:
        c = by_word.astype(ml_dtypes.float4_e2m1fn).view(np.uint8) & 0xF
        words = (c[..., 0::2] | (c[..., 1::2] << 4)).reshape(k // 512, 128, 2 * n)
    return np.ascontiguousarray(words), np.ascontiguousarray(byte.astype(np.uint8).reshape(k // 512, 16, n))


def unpack_weight(words, scales, fmt):
    g, _, n = scales.shape
    words = np.ascontiguousarray(words).reshape(g, 128, n, -1)
    if fmt == "e4m3":
        vals = words.view(ml_dtypes.float8_e4m3fn).astype(np.float64)
    else:
        nib = np.empty((g, 128, n, 4), np.uint8)
        nib[..., 0::2] = words & 0xF
        nib[..., 1::2] = words >> 4
        vals = E2M1[nib]
    vals = vals * np.repeat(np.exp2(scales.astype(np.float64) - 127.0), 8, axis=1)[..., None]
    return vals.transpose(0, 1, 3, 2).reshape(g * 512, n)


def gelu(v):
    return 0.5 * v * (1.0 + np.tanh(np.sqrt(2.0 / np.pi) * (v + 0.044715 * v**3)))


K, H, N, T, S, T2, P = 1536, 1024, 384, 4096, 1024, 2048, 1024

def setup_inputs():
    n = np.random.standard_normal
    s = mx_kscale(K)[:, None]
    u = mx_kscale(H)[:, None]
    tab_words, tab_scales = pack_weight(n((K, T)) * s, "e4m3")
    w4_words, w4_scales = pack_weight(n((K, H)) / np.sqrt(K) / s * u.T, "e2m1")
    w8_words, w8_scales = pack_weight(n((H, N)) / np.sqrt(H) / u, "e4m3")
    return {
        "tab_words": tab_words, "tab_scales": tab_scales,
        "offs": striped(np.random.permutation(T)[:S]),
        "offs2": striped(np.random.permutation(T2)[:S]),
        "offs3": striped(np.random.permutation(T2)[:P]),
        "w4_words": w4_words, "w4_scales": w4_scales,
        "w8_words": w8_words, "w8_scales": w8_scales,
        "wv": (1.5 * n((H, N)) / np.sqrt(H) / u).astype(np.float32),
        "page0": (n((H, T2)) * u).astype(np.float32),
        "wgs": np.exp(0.3 * n((128, S))).astype(np.float32),
        "gin": (np.exp(0.3 * n(H)) / u[:, 0]).astype(np.float32),
        "gout": (np.exp(0.3 * n(H)) * u[:, 0]).astype(np.float32),
    }

def reference(tab_words, tab_scales, offs, offs2, offs3, w4_words, w4_scales,
              w8_words, w8_scales, wv, page0, wgs, gin, gout):
    v = unpack_weight(tab_words, tab_scales, "e4m3")[:, unstriped(offs)]
    w4 = unpack_weight(w4_words, w4_scales, "e2m1")
    w8 = unpack_weight(w8_words, w8_scales, "e4m3")
    h = w4.T @ v
    page = f64(page0).copy()
    page[:, unstriped(offs2)] = np.tile(f64(wgs), (H // 128, 1)) * h
    x = page[:, unstriped(offs3)]
    a = f64(gin)[:, None] * x
    ge = 0.5 * a * (1.0 + np.tanh(np.sqrt(2.0 / np.pi) * (a + 0.044715 * a * a * a)))
    z = f64(gout)[:, None] * ge
    value = mxq(f64(wv), 0, "e4m3").T @ mxq(z, 0, "e4m3")
    gate = w8.T @ mxq(x, 0, "e4m3")
    return value * (1.0 / (1.0 + np.exp(-gate)))

@@ -1,0 +1,303 @@
+from contextlib import ExitStack
+
+import concourse.mybir as mybir
+
+K, H, N, T, S, T2, M = 1536, 1024, 384, 4096, 1024, 2048, 1024
+FLOPS = 2 * K * H * S + 4 * H * N * M
+
+F32 = mybir.dt.float32
+BF16 = mybir.dt.bfloat16
+I32 = mybir.dt.int32
+U32 = mybir.dt.uint32
+U16 = mybir.dt.uint16
+U8 = mybir.dt.uint8
+FP8X4 = mybir.dt.float8_e4m3fn_x4
+FP4X4 = mybir.dt.float4_e2m1fn_x4
+ACT = mybir.ActivationFunctionType
+ALU = mybir.AluOpType
+
+P = 128
+PACK = 4
+KP = K // (P * PACK)
+RP = H // (P * PACK)
+HALF = 512
+NT = N // P
+QUADS = 4
+
+
+def tile_list_dialogue_reply_ranker_kernel(tc, tab_words, tab_scales, offs, offs2, offs3, w4_words, w4_scales,
+                                                    w8_words, w8_scales, wv, page0, wgs, gin, gout, out):
+    nc = tc.nc
+    with ExitStack() as ctx:
+        keep = ctx.enter_context(tc.tile_pool(name="keep", bufs=1))
+        ring = ctx.enter_context(tc.tile_pool(name="ring", bufs=2))
+        psum = ctx.enter_context(tc.psum_pool(name="psum", bufs=1))
+
+        def bank(b):
+            return psum.tile([P, HALF], F32, name="bank%d" % b)
+
+        def cols(h):
+            return slice(h * HALF, (h + 1) * HALF)
+
+        def entries(lst, h):
+            return lst[:, h * HALF // 16:(h + 1) * HALF // 16]
+
+        list1 = keep.tile([P, S // 16], U16)
+        list2 = keep.tile([P, S // 16], U16)
+        list3 = keep.tile([P, M // 16], U16)
+        nc.sync.dma_start(list1[:], offs)
+        nc.sync.dma_start(list2[:], offs2)
+
+        ts_win = keep.tile([P, T], U8, align_bytes=64)
+        w4s_raw = keep.tile([P, KP, H], U8, align_bytes=64)
+        ts_moved = keep.tile([P, KP - 1, S], U8, align_bytes=64)
+        w8_sc = keep.tile([P, RP, N], U8, align_bytes=64)
+        nc.vector.memset(ts_win[:].bitcast(I32), 0)
+        nc.vector.memset(w4s_raw[:].bitcast(I32), 0)
+        nc.vector.memset(ts_moved[:].bitcast(I32), 0)
+        nc.vector.memset(w8_sc[:].bitcast(I32), 0)
+
+        w4_raw = keep.tile([P, KP, 2 * H], U8, align_bytes=64)
+        nc.sync.dma_start(w4_raw[:].bitcast(I32), w4_words.rearrange("a p c -> p a c").bitcast(I32))
+        tabs = []
+        for a in range(KP):
+            tab = ring.tile([P, T], I32, name="tab%d" % a, tag="big", bufs=3, align_bytes=64)
+            nc.sync.dma_start(tab[:], tab_words[a].rearrange("p t i -> p (t i)").bitcast(I32))
+            tabs.append(tab)
+        for q in range(QUADS):
+            nc.gpsimd.dma_start(ts_win[32 * q:32 * q + 4 * KP, :].bitcast(I32),
+                                tab_scales[:, 4 * q:4 * q + 4, :].bitcast(I32))
+        for q in range(QUADS):
+            nc.gpsimd.dma_start(w4s_raw[32 * q:32 * q + 4, :, :].bitcast(I32),
+                                w4_scales[:, 4 * q:4 * q + 4, :].rearrange("a r c -> r a c").bitcast(I32))
+
+        page_rows = page0.rearrange("(b p t) c -> b t p c", p=P, t=PACK)
+        pages = {}
+
+        def load_page(i):
+            pages[i] = ring.tile([P, T2], F32, name="page%d" % i, tag="page", bufs=4)
+            nc.sync.dma_start(pages[i][:], page_rows[i // PACK, i % PACK])
+
+        wgs_rows = wgs.rearrange("(q t) j -> q t j", t=PACK)
+        wgs_first = keep.tile([P, S], F32)
+        wgs_rest = keep.tile([P, PACK - 1, S], F32)
+        load_page(0)
+        for h in range(2):
+            for q in (0, 2, 1, 3):
+                nc.sync.dma_start(wgs_first[32 * q:32 * q + 32, cols(h)], wgs_rows[:, 0, cols(h)])
+        nc.sync.dma_start(list3[:], offs3)
+        load_page(1)
+        for q in (0, 2, 1, 3):
+            nc.sync.dma_start(wgs_rest[32 * q:32 * q + 32, :, :], wgs_rows[:, 1:, :])
+        gin_t = keep.tile([P, RP, PACK], F32)
+        gout_t = keep.tile([P, RP, PACK], F32)
+        nc.sync.dma_start(gin_t[:], gin.rearrange("(b p t) -> p b t", p=P, t=PACK))
+        nc.sync.dma_start(gout_t[:], gout.rearrange("(b p t) -> p b t", p=P, t=PACK))
+        load_page(2)
+        load_page(3)
+
+        ts_got = keep.tile([P, S], U8, align_bytes=64)
+        nc.vector.tensor_copy(ts_got[:], ts_win[:].indirect(list1[:]))
+        for a in range(1, KP):
+            for q in range(QUADS):
+                first = 32 * q + 4 * a
+                nc.gpsimd.dma_start(ts_moved[32 * q:32 * q + 4, a - 1, :].bitcast(I32), ts_got[first:first + 4, :].bitcast(I32))
+        v_scales = [ts_got[:]] + [ts_moved[:, a - 1, :] for a in range(1, KP)]
+
+        w4_codes = keep.tile([P, RP, KP, 2 * HALF], U8, align_bytes=64)
+        w4_sc = keep.tile([P, RP, KP, HALF], U8, align_bytes=64)
+        for b in range(RP):
+            nc.vector.tensor_copy(
+                w4_codes[:, b].bitcast(U16).rearrange("p a (t m) -> p a t m", t=PACK),
+                w4_raw[:].bitcast(U16)[:, :, cols(b)].rearrange("p a (m t) -> p a t m", t=PACK))
+            nc.vector.tensor_copy(
+                w4_sc[:, b].rearrange("p a (t m) -> p a t m", t=PACK),
+                w4s_raw[:, :, cols(b)].rearrange("p a (m t) -> p a t m", t=PACK))
+
+        v_codes = keep.tile([P, KP, S], U32, align_bytes=64)
+        for a in range(KP - 1):
+            nc.vector.tensor_copy(v_codes[:, a, :], tabs[a][:].bitcast(U32).indirect(list1[:]))
+        for h in range(2):
+            nc.vector.tensor_copy(v_codes[:, KP - 1, cols(h)], tabs[KP - 1][:].bitcast(U32).indirect(entries(list1, h)))
+
+        x_f32 = [ring.tile([P, PACK, M], F32, name="x_f32_0", tag="big", bufs=3, align_bytes=64)]
+        wv_raw = ring.tile([P, RP, PACK, N], F32, name="wv_raw", tag="big", bufs=3, align_bytes=64)
+        x_f32.append(ring.tile([P, PACK, M], F32, name="x_f32_1", tag="big", bufs=3, align_bytes=64))
+        nc.sync.dma_start(wv_raw[:], wv.rearrange("(b p j) n -> p b j n", p=P, j=PACK))
+        w8_codes = keep.tile([P, RP, N], U32, align_bytes=64)
+        nc.sync.dma_start(w8_codes[:].bitcast(I32), w8_words.rearrange("b p c i -> p b (c i)").bitcast(I32))
+        for q in range(QUADS):
+            nc.sync.dma_start(w8_sc[32 * q:32 * q + 4, :, :].bitcast(I32),
+                              w8_scales[:, 4 * q:4 * q + 4, :].rearrange("b r c -> r b c").bitcast(I32))
+
+        staged = {}
+
+        def project(i):
+            b, t = divmod(i, PACK)
+            staged[i] = ring.tile([P, S], F32, name="staged%d" % i, tag="staged")
+            for h in range(2):
+                acc = bank(6 + h)
+                for a in range(KP):
+                    nc.tensor.matmul_mx(
+                        out=acc[:],
+                        lhsT=w4_codes[:, b, a, 2 * P * t:2 * P * (t + 1)].bitcast(FP4X4),
+                        lhsT_scale=w4_sc[:, b, a, P * t:P * (t + 1)],
+                        rhs=v_codes[:, a, cols(h)].bitcast(FP8X4),
+                        rhs_scale=v_scales[a][:, cols(h)],
+                        start=(a == 0), stop=(a == KP - 1))
+                nc.scalar.copy(staged[i][:, cols(h)], acc[:])
+
+        def scatter(i):
+            t = i % PACK
+            weight = wgs_first[:] if t == 0 else wgs_rest[:, t - 1, :]
+            if i == 0:
+                for h in range(2):
+                    nc.vector.tensor_tensor(pages[i][:].indirect(entries(list2, h)), staged[i][:, cols(h)],
+                                            weight[:, cols(h)], ALU.mult)
+            else:
+                nc.vector.tensor_tensor(pages[i][:].indirect(list2[:]), staged[i][:], weight, ALU.mult)
+
+        def fetch(i):
+            b, t = divmod(i, PACK)
+            if i == RP * PACK - 1:
+                for h in range(2):
+                    nc.vector.tensor_copy(x_f32[b][:, t, cols(h)], pages[i][:].indirect(entries(list3, h)))
+            else:
+                nc.vector.tensor_copy(x_f32[b][:, t, :], pages[i][:].indirect(list3[:]))
+            if i + 4 < RP * PACK:
+                load_page(i + 4)
+
+        x_bf = {}
+        z_bf = {}
+        for b in range(RP):
+            for h in range(2):
+                x_bf[b, h] = keep.tile([P, HALF, PACK], BF16, name="x_bf%d%d" % (b, h), align_bytes=64)
+                z_bf[b, h] = keep.tile([P, HALF, PACK], BF16, name="z_bf%d%d" % (b, h), align_bytes=64)
+
+        def gelu_half(i, h):
+            b, t = divmod(i, PACK)
+            ge = ring.tile([P, HALF], F32, name="ge", bufs=3)
+            nc.scalar.activation(ge[:], x_f32[b][:, t, cols(h)], ACT.Gelu_apprx_tanh, scale=gin_t[:, b, t:t + 1])
+            nc.scalar.activation(z_bf[b, h][:, :, t], ge[:], ACT.Copy, scale=gout_t[:, b, t:t + 1])
+
+        def weave_x(copy, b, h, t0, t1):
+            copy(x_bf[b, h][:, :, t0:t1].rearrange("p (c i) t -> p c t i", i=4),
+                 x_f32[b][:, t0:t1, cols(h)].rearrange("p t (c i) -> p c t i", i=4))
+
+        x_codes = keep.tile([P, RP, M], U32, align_bytes=64)
+        z_codes = keep.tile([P, RP, M], U32, align_bytes=64)
+        x_sc = keep.tile([P, RP, M], U8, align_bytes=64)
+        z_sc = keep.tile([P, RP, M], U8, align_bytes=64)
+
+        def quantize(codes, scales, src, b, h):
+            nc.vector.quantize_mx(out=codes[:, b, cols(h)].bitcast(FP8X4), scales=scales[:, b, cols(h)],
+                                  in_=src[b, h][:].rearrange("p m t -> p (m t)"))
+
+        wv_bf = keep.tile([P, RP * N * PACK], BF16, align_bytes=64)
+        wv_codes = keep.tile([P, RP * N], U32, align_bytes=64)
+        wv_sc = keep.tile([P, RP * N], U8, align_bytes=64)
+
+        def weave_wv():
+            for b in range(RP):
+                nc.scalar.activation(
+                    wv_bf[:, b * N * PACK:(b + 1) * N * PACK].rearrange("p (c i j) -> p c j i", i=4, j=PACK),
+                    wv_raw[:, b].rearrange("p j (c i) -> p c j i", i=4), ACT.Copy, scale=0.5)
+
+        def quantize_wv():
+            for c0, c1 in ((0, 512), (512, RP * N)):
+                nc.vector.quantize_mx(out=wv_codes[:, c0:c1].bitcast(FP8X4), scales=wv_sc[:, c0:c1],
+                                      in_=wv_bf[:, PACK * c0:PACK * c1])
+
+        def gate_pass(acc, n, b, h):
+            nc.tensor.matmul_mx(out=acc[:], lhsT=w8_codes[:, b, P * n:P * (n + 1)].bitcast(FP8X4),
+                                lhsT_scale=w8_sc[:, b, P * n:P * (n + 1)],
+                                rhs=x_codes[:, b, cols(h)].bitcast(FP8X4), rhs_scale=x_sc[:, b, cols(h)],
+                                start=(b == 0), stop=(b == RP - 1))
+
+        def value_pass(acc, n, b, h):
+            c0 = b * N + P * n
+            nc.tensor.matmul_mx(out=acc[:], lhsT=wv_codes[:, c0:c0 + P].bitcast(FP8X4), lhsT_scale=wv_sc[:, c0:c0 + P],
+                                rhs=z_codes[:, b, cols(h)].bitcast(FP8X4), rhs_scale=z_sc[:, b, cols(h)],
+                                start=(b == 0), stop=(b == RP - 1))
+
+        last = RP * PACK - 1
+        project(0)
+        project(1)
+        scatter(0)
+        for i in range(1, last):
+            project(i + 1)
+            scatter(i)
+            fetch(i - 1)
+            for h in range(2):
+                gelu_half(i - 1, h)
+            if i == 2:
+                weave_wv()
+            if i == 3:
+                quantize_wv()
+            if i == PACK:
+                for h in range(2):
+                    weave_x(nc.scalar.copy, 0, h, 0, PACK)
+            if i == PACK + 1:
+                for h in range(2):
+                    quantize(z_codes, z_sc, z_bf, 0, h)
+                quantize(x_codes, x_sc, x_bf, 0, 0)
+        fetch(last - 1)
+        for h in range(2):
+            weave_x(nc.scalar.copy, 1, h, 0, 2)
+        for h in range(2):
+            gelu_half(last - 1, h)
+
+        gate = {}
+        value = {}
+        for n in range(NT):
+            gate[n, 0] = bank(n)
+            gate_pass(gate[n, 0], n, 0, 0)
+            value[n, 0] = bank(NT + n)
+            value_pass(value[n, 0], n, 0, 0)
+        scatter(last)
+        quantize(x_codes, x_sc, x_bf, 0, 1)
+        for n in range(2):
+            gate[n, 1] = bank(6 + n)
+            gate_pass(gate[n, 1], n, 0, 1)
+        fetch(last)
+        for h in range(2):
+            gelu_half(last, h)
+        for h in range(2):
+            weave_x(nc.vector.tensor_copy, 1, h, 2, PACK)
+        quantize(x_codes, x_sc, x_bf, 1, 0)
+        quantize(z_codes, z_sc, z_bf, 1, 0)
+        quantize(x_codes, x_sc, x_bf, 1, 1)
+        quantize(z_codes, z_sc, z_bf, 1, 1)
+
+        th = {}
+
+        def squash(n, h):
+            th[n, h] = ring.tile([P, HALF], F32, name="th", bufs=3)
+            nc.scalar.activation(th[n, h][:], gate[n, h][:], ACT.Tanh, scale=0.5)
+
+        def finish(n, h):
+            res = ring.tile([P, HALF], F32, name="res", bufs=6)
+            nc.vector.scalar_tensor_tensor(out=res[:], in0=th[n, h][:], scalar=1.0, in1=value[n, h][:],
+                                           op0=ALU.add, op1=ALU.mult)
+            nc.sync.dma_start(out[P * n:P * (n + 1), cols(h)], res[:])
+
+        for n in range(NT):
+            gate_pass(gate[n, 0], n, 1, 0)
+        for n in range(NT):
+            value_pass(value[n, 0], n, 1, 0)
+        for n in range(2):
+            gate_pass(gate[n, 1], n, 1, 1)
+        for n in range(NT):
+            squash(n, 0)
+        gate[2, 1] = bank(0)
+        for b in range(RP):
+            gate_pass(gate[2, 1], 2, b, 1)
+        for n in range(NT):
+            finish(n, 0)
+        for n in range(NT):
+            value[n, 1] = bank(1 + n)
+            for b in range(RP):
+                value_pass(value[n, 1], n, b, 1)
+        for n in range(NT):
+            squash(n, 1)
+            finish(n, 1)

@@ -47,84 +47,91 @@ def tile_list_dialogue_reply_ranker_kernel(tc, tab_words, tab_scales, offs, offs
         list3 = keep.tile([P, M // 16], U16)
         nc.sync.dma_start(list1[:], offs)
         nc.sync.dma_start(list2[:], offs2)
+        nc.sync.dma_start(list3[:], offs3)
 
-        ts_win = keep.tile([P, T], U8, align_bytes=64)
-        w4s_raw = keep.tile([P, KP, H], U8, align_bytes=64)
-        ts_moved = keep.tile([P, KP - 1, S], U8, align_bytes=64)
-        w8_sc = keep.tile([P, RP, N], U8, align_bytes=64)
-        nc.vector.memset(ts_win[:].bitcast(I32), 0)
-        nc.vector.memset(w4s_raw[:].bitcast(I32), 0)
-        nc.vector.memset(ts_moved[:].bitcast(I32), 0)
-        nc.vector.memset(w8_sc[:].bitcast(I32), 0)
-
-        w4_raw = keep.tile([P, KP, 2 * H], U8, align_bytes=64)
-        nc.sync.dma_start(w4_raw[:].bitcast(I32), w4_words.rearrange("a p c -> p a c").bitcast(I32))
         tabs = []
-        for a in range(KP):
-            tab = ring.tile([P, T], I32, name="tab%d" % a, tag="big", bufs=3, align_bytes=64)
+
+        def load_table(pool, a):
+            tab = pool.tile([P, T], I32, name="tab%d" % a, align_bytes=64)
             nc.sync.dma_start(tab[:], tab_words[a].rearrange("p t i -> p (t i)").bitcast(I32))
             tabs.append(tab)
-        for q in range(QUADS):
-            nc.gpsimd.dma_start(ts_win[32 * q:32 * q + 4 * KP, :].bitcast(I32),
-                                tab_scales[:, 4 * q:4 * q + 4, :].bitcast(I32))
-        for q in range(QUADS):
-            nc.gpsimd.dma_start(w4s_raw[32 * q:32 * q + 4, :, :].bitcast(I32),
-                                w4_scales[:, 4 * q:4 * q + 4, :].rearrange("a r c -> r a c").bitcast(I32))
 
+        def fetch_table(a, dst, offsets):
+            nc.vector.tensor_copy(dst, tabs[a][:].bitcast(U32).indirect(offsets))
+
+        row_first = (32, 48, 112)
+
+        def load_scale_rows(tile, scales):
+            rows = scales.rearrange("a q c -> (a q) c").bitcast(I32)
+            nc.scalar.dma_start(tile[32:64, :].bitcast(I32), rows[0:32, :])
+            nc.scalar.dma_start(tile[112:128, :].bitcast(I32), rows[32:48, :])
+            nc.vector.memset(tile[0:32, :].bitcast(I32), 0)
+            nc.vector.memset(tile[64:112, :].bitcast(I32), 0)
+
+        w4_raw = keep.tile([P, KP, 2 * H], U8, tag="tab2", align_bytes=64)
+        nc.sync.dma_start(w4_raw[:].bitcast(I32), w4_words.rearrange("a p c -> p a c").bitcast(I32))
+        load_table(keep, 0)
+        w4s_raw = keep.tile([P, H], U8, align_bytes=64)
+        ts_got = keep.tile([P, S], U8, align_bytes=64)
+        with tc.tile_pool(name="scale_window", bufs=1) as window_pool:
+            ts_win = window_pool.tile([P, T], U8, offset=T, align_bytes=64)
+            load_scale_rows(ts_win, tab_scales)
+            load_scale_rows(w4s_raw, w4_scales)
+            nc.vector.tensor_copy(ts_got[:], ts_win[:].indirect(list1[:]))
+        planes = keep.tile([P, KP, S + H], U8, align_bytes=64)
+        nc.gpsimd.memset(planes[:].bitcast(I32), 0)
+
+        w4_pool = ctx.enter_context(tc.tile_pool(name="w4_pool", bufs=1))
+        w4_codes = w4_pool.tile([P, RP, KP, 2 * HALF], U8, align_bytes=64)
+        v_codes = [keep.tile([P, S], U32, name="v_codes%d" % a, align_bytes=64) for a in range(KP)]
+        with tc.tile_pool(name="second_pass", bufs=1) as second_pool:
+            load_table(second_pool, 1)
+            scale_rows = keep.tile([P, S + H], U8, align_bytes=64)
+            nc.vector.tensor_copy(scale_rows[:, S:].rearrange("p (b t m) -> p b t m", b=RP, t=PACK),
+                                  w4s_raw[:].rearrange("p (b m t) -> p b t m", b=RP, t=PACK))
+            nc.vector.tensor_copy(scale_rows[:, :S].bitcast(I32), ts_got[:].bitcast(I32))
+            for a in range(KP):
+                for q in range(QUADS):
+                    first = row_first[a] + 4 * q
+                    nc.scalar.dma_start(planes[32 * q:32 * q + 4, a, :].bitcast(I32),
+                                        scale_rows[first:first + 4, :].bitcast(I32))
+            for b in range(RP):
+                nc.vector.tensor_copy(
+                    w4_codes[:, b].bitcast(U16).rearrange("p a (t m) -> p a t m", t=PACK),
+                    w4_raw[:].bitcast(U16)[:, :, cols(b)].rearrange("p a (m t) -> p a t m", t=PACK))
+            load_table(keep, 2)
+            for a in range(KP - 1):
+                fetch_table(a, v_codes[a][:], list1[:])
+        for h in range(2):
+            fetch_table(KP - 1, v_codes[KP - 1][:, cols(h)], entries(list1, h))
+
+        held = ctx.enter_context(tc.tile_pool(name="held", bufs=1))
         page_rows = page0.rearrange("(b p t) c -> b t p c", p=P, t=PACK)
         pages = {}
 
         def load_page(i):
-            pages[i] = ring.tile([P, T2], F32, name="page%d" % i, tag="page", bufs=4)
+            pages[i] = held.tile([P, T2], F32, name="page%d" % i, tag="page%d" % (i % 4), align_bytes=64)
             nc.sync.dma_start(pages[i][:], page_rows[i // PACK, i % PACK])
 
         wgs_rows = wgs.rearrange("(q t) j -> q t j", t=PACK)
-        wgs_first = keep.tile([P, S], F32)
-        wgs_rest = keep.tile([P, PACK - 1, S], F32)
-        load_page(0)
-        for h in range(2):
+        weights = [held.tile([P, S], F32, name="wgs%d" % t, align_bytes=64) for t in range(PACK)]
+        gin_t = held.tile([P, RP, PACK], F32)
+        gout_t = held.tile([P, RP, PACK], F32)
+        for t in range(PACK):
+            load_page(t)
             for q in (0, 2, 1, 3):
-                nc.sync.dma_start(wgs_first[32 * q:32 * q + 32, cols(h)], wgs_rows[:, 0, cols(h)])
-        nc.sync.dma_start(list3[:], offs3)
-        load_page(1)
-        for q in (0, 2, 1, 3):
-            nc.sync.dma_start(wgs_rest[32 * q:32 * q + 32, :, :], wgs_rows[:, 1:, :])
-        gin_t = keep.tile([P, RP, PACK], F32)
-        gout_t = keep.tile([P, RP, PACK], F32)
-        nc.sync.dma_start(gin_t[:], gin.rearrange("(b p t) -> p b t", p=P, t=PACK))
-        nc.sync.dma_start(gout_t[:], gout.rearrange("(b p t) -> p b t", p=P, t=PACK))
-        load_page(2)
-        load_page(3)
+                nc.sync.dma_start(weights[t][32 * q:32 * q + 32, :], wgs_rows[:, t, :])
+            if t == 1:
+                nc.sync.dma_start(gin_t[:], gin.rearrange("(b p t) -> p b t", p=P, t=PACK))
+                nc.sync.dma_start(gout_t[:], gout.rearrange("(b p t) -> p b t", p=P, t=PACK))
 
-        ts_got = keep.tile([P, S], U8, align_bytes=64)
-        nc.vector.tensor_copy(ts_got[:], ts_win[:].indirect(list1[:]))
-        for a in range(1, KP):
-            for q in range(QUADS):
-                first = 32 * q + 4 * a
-                nc.gpsimd.dma_start(ts_moved[32 * q:32 * q + 4, a - 1, :].bitcast(I32), ts_got[first:first + 4, :].bitcast(I32))
-        v_scales = [ts_got[:]] + [ts_moved[:, a - 1, :] for a in range(1, KP)]
-
-        w4_codes = keep.tile([P, RP, KP, 2 * HALF], U8, align_bytes=64)
-        w4_sc = keep.tile([P, RP, KP, HALF], U8, align_bytes=64)
-        for b in range(RP):
-            nc.vector.tensor_copy(
-                w4_codes[:, b].bitcast(U16).rearrange("p a (t m) -> p a t m", t=PACK),
-                w4_raw[:].bitcast(U16)[:, :, cols(b)].rearrange("p a (m t) -> p a t m", t=PACK))
-            nc.vector.tensor_copy(
-                w4_sc[:, b].rearrange("p a (t m) -> p a t m", t=PACK),
-                w4s_raw[:, :, cols(b)].rearrange("p a (m t) -> p a t m", t=PACK))
-
-        v_codes = keep.tile([P, KP, S], U32, align_bytes=64)
-        for a in range(KP - 1):
-            nc.vector.tensor_copy(v_codes[:, a, :], tabs[a][:].bitcast(U32).indirect(list1[:]))
-        for h in range(2):
-            nc.vector.tensor_copy(v_codes[:, KP - 1, cols(h)], tabs[KP - 1][:].bitcast(U32).indirect(entries(list1, h)))
-
-        x_f32 = [ring.tile([P, PACK, M], F32, name="x_f32_0", tag="big", bufs=3, align_bytes=64)]
-        wv_raw = ring.tile([P, RP, PACK, N], F32, name="wv_raw", tag="big", bufs=3, align_bytes=64)
-        x_f32.append(ring.tile([P, PACK, M], F32, name="x_f32_1", tag="big", bufs=3, align_bytes=64))
+        x_f32 = [keep.tile([P, PACK, M], F32, name="x_f32_0", tag="tab0", align_bytes=64),
+                 keep.tile([P, PACK, M], F32, name="x_f32_1", tag="tab2", align_bytes=64)]
+        wv_raw = held.tile([P, RP, PACK, N], F32)
         nc.sync.dma_start(wv_raw[:], wv.rearrange("(b p j) n -> p b j n", p=P, j=PACK))
-        w8_codes = keep.tile([P, RP, N], U32, align_bytes=64)
+        w8_sc = held.tile([P, RP, N], U8, align_bytes=64)
+        nc.gpsimd.memset(w8_sc[:].bitcast(I32), 0)
+        w8_codes = held.tile([P, RP, N], U32, align_bytes=64)
         nc.sync.dma_start(w8_codes[:].bitcast(I32), w8_words.rearrange("b p c i -> p b (c i)").bitcast(I32))
         for q in range(QUADS):
             nc.sync.dma_start(w8_sc[32 * q:32 * q + 4, :, :].bitcast(I32),
@@ -134,22 +141,22 @@ def tile_list_dialogue_reply_ranker_kernel(tc, tab_words, tab_scales, offs, offs
 
         def project(i):
             b, t = divmod(i, PACK)
-            staged[i] = ring.tile([P, S], F32, name="staged%d" % i, tag="staged")
+            staged[i] = keep.tile([P, S], F32, name="staged%d" % i, align_bytes=64)
             for h in range(2):
                 acc = bank(6 + h)
                 for a in range(KP):
                     nc.tensor.matmul_mx(
                         out=acc[:],
                         lhsT=w4_codes[:, b, a, 2 * P * t:2 * P * (t + 1)].bitcast(FP4X4),
-                        lhsT_scale=w4_sc[:, b, a, P * t:P * (t + 1)],
-                        rhs=v_codes[:, a, cols(h)].bitcast(FP8X4),
-                        rhs_scale=v_scales[a][:, cols(h)],
+                        lhsT_scale=planes[:, a, S + P * i:S + P * (i + 1)],
+                        rhs=v_codes[a][:, cols(h)].bitcast(FP8X4),
+                        rhs_scale=planes[:, a, cols(h)],
                         start=(a == 0), stop=(a == KP - 1))
                 nc.scalar.copy(staged[i][:, cols(h)], acc[:])
 
         def scatter(i):
             t = i % PACK
-            weight = wgs_first[:] if t == 0 else wgs_rest[:, t - 1, :]
+            weight = weights[t][:]
             if i == 0:
                 for h in range(2):
                     nc.vector.tensor_tensor(pages[i][:].indirect(entries(list2, h)), staged[i][:, cols(h)],
@@ -174,36 +181,42 @@ def tile_list_dialogue_reply_ranker_kernel(tc, tab_words, tab_scales, offs, offs
                 x_bf[b, h] = keep.tile([P, HALF, PACK], BF16, name="x_bf%d%d" % (b, h), align_bytes=64)
                 z_bf[b, h] = keep.tile([P, HALF, PACK], BF16, name="z_bf%d%d" % (b, h), align_bytes=64)
 
+        z_rows = {}
+
         def gelu_half(i, h):
             b, t = divmod(i, PACK)
+            if b not in z_rows:
+                z_rows[b] = keep.tile([P, PACK, M], BF16, name="z_rows%d" % b, align_bytes=64)
             ge = ring.tile([P, HALF], F32, name="ge", bufs=3)
             nc.scalar.activation(ge[:], x_f32[b][:, t, cols(h)], ACT.Gelu_apprx_tanh, scale=gin_t[:, b, t:t + 1])
-            nc.scalar.activation(z_bf[b, h][:, :, t], ge[:], ACT.Copy, scale=gout_t[:, b, t:t + 1])
+            dst = z_bf[b, h][:, :, t] if i == last else z_rows[b][:, t, cols(h)]
+            nc.scalar.activation(dst, ge[:], ACT.Copy, scale=gout_t[:, b, t:t + 1])
 
-        def weave_x(copy, b, h, t0, t1):
-            copy(x_bf[b, h][:, :, t0:t1].rearrange("p (c i) t -> p c t i", i=4),
-                 x_f32[b][:, t0:t1, cols(h)].rearrange("p t (c i) -> p c t i", i=4))
+        def weave(copy, dst, src, b, h, t0=0, t1=PACK):
+            copy(dst[b, h][:, :, t0:t1].rearrange("p (c i) t -> p c t i", i=4),
+                 src[b][:, t0:t1, cols(h)].rearrange("p t (c i) -> p c t i", i=4))
 
-        x_codes = keep.tile([P, RP, M], U32, align_bytes=64)
-        z_codes = keep.tile([P, RP, M], U32, align_bytes=64)
+        x_codes = {}
+        z_codes = {}
         x_sc = keep.tile([P, RP, M], U8, align_bytes=64)
         z_sc = keep.tile([P, RP, M], U8, align_bytes=64)
 
         def quantize(codes, scales, src, b, h):
-            nc.vector.quantize_mx(out=codes[:, b, cols(h)].bitcast(FP8X4), scales=scales[:, b, cols(h)],
+            nc.vector.quantize_mx(out=codes[b, h].bitcast(FP8X4), scales=scales[:, b, cols(h)],
                                   in_=src[b, h][:].rearrange("p m t -> p (m t)"))
 
-        wv_bf = keep.tile([P, RP * N * PACK], BF16, align_bytes=64)
-        wv_codes = keep.tile([P, RP * N], U32, align_bytes=64)
+        wv_bf = keep.tile([P, RP * N * PACK], BF16, tag="spare", align_bytes=64)
+        wv_q = {}
         wv_sc = keep.tile([P, RP * N], U8, align_bytes=64)
 
-        def weave_wv():
-            for b in range(RP):
-                nc.scalar.activation(
-                    wv_bf[:, b * N * PACK:(b + 1) * N * PACK].rearrange("p (c i j) -> p c j i", i=4, j=PACK),
-                    wv_raw[:, b].rearrange("p j (c i) -> p c j i", i=4), ACT.Copy, scale=0.5)
+        def weave_wv(b):
+            nc.scalar.activation(
+                wv_bf[:, b * N * PACK:(b + 1) * N * PACK].rearrange("p (c i j) -> p c j i", i=4, j=PACK),
+                wv_raw[:, b].rearrange("p j (c i) -> p c j i", i=4), ACT.Copy, scale=0.5)
 
         def quantize_wv():
+            wv_codes = keep.tile([P, RP * N], U32, tag="staged%d" % last, align_bytes=64)
+            wv_q[0] = wv_codes
             for c0, c1 in ((0, 512), (512, RP * N)):
                 nc.vector.quantize_mx(out=wv_codes[:, c0:c1].bitcast(FP8X4), scales=wv_sc[:, c0:c1],
                                       in_=wv_bf[:, PACK * c0:PACK * c1])
@@ -211,13 +224,13 @@ def tile_list_dialogue_reply_ranker_kernel(tc, tab_words, tab_scales, offs, offs
         def gate_pass(acc, n, b, h):
             nc.tensor.matmul_mx(out=acc[:], lhsT=w8_codes[:, b, P * n:P * (n + 1)].bitcast(FP8X4),
                                 lhsT_scale=w8_sc[:, b, P * n:P * (n + 1)],
-                                rhs=x_codes[:, b, cols(h)].bitcast(FP8X4), rhs_scale=x_sc[:, b, cols(h)],
+                                rhs=x_codes[b, h].bitcast(FP8X4), rhs_scale=x_sc[:, b, cols(h)],
                                 start=(b == 0), stop=(b == RP - 1))
 
         def value_pass(acc, n, b, h):
             c0 = b * N + P * n
-            nc.tensor.matmul_mx(out=acc[:], lhsT=wv_codes[:, c0:c0 + P].bitcast(FP8X4), lhsT_scale=wv_sc[:, c0:c0 + P],
-                                rhs=z_codes[:, b, cols(h)].bitcast(FP8X4), rhs_scale=z_sc[:, b, cols(h)],
+            nc.tensor.matmul_mx(out=acc[:], lhsT=wv_q[0][:, c0:c0 + P].bitcast(FP8X4), lhsT_scale=wv_sc[:, c0:c0 + P],
+                                rhs=z_codes[b, h].bitcast(FP8X4), rhs_scale=z_sc[:, b, cols(h)],
                                 start=(b == 0), stop=(b == RP - 1))
 
         last = RP * PACK - 1
@@ -230,65 +243,82 @@ def tile_list_dialogue_reply_ranker_kernel(tc, tab_words, tab_scales, offs, offs
             fetch(i - 1)
             for h in range(2):
                 gelu_half(i - 1, h)
-            if i == 2:
-                weave_wv()
-            if i == 3:
-                quantize_wv()
-            if i == PACK:
+            if i in (2, 3):
+                weave_wv(i - 2)
+            if i == 4:
                 for h in range(2):
-                    weave_x(nc.scalar.copy, 0, h, 0, PACK)
-            if i == PACK + 1:
+                    weave(nc.scalar.copy, x_bf, x_f32, 0, h)
+            if i == 5:
                 for h in range(2):
-                    quantize(z_codes, z_sc, z_bf, 0, h)
-                quantize(x_codes, x_sc, x_bf, 0, 0)
+                    weave(nc.scalar.copy, z_bf, z_rows, 0, h)
+            if i == 6:
+                for h in range(2):
+                    weave(nc.scalar.copy, x_bf, x_f32, 1, h, 0, 2)
+
+        def code_tiles(pool, b, h, tag):
+            both = pool.tile([P, 2, HALF], U32, name="codes%d%d" % (b, h), tag=tag, align_bytes=64)
+            x_codes[b, h] = both[:, 0, :]
+            z_codes[b, h] = both[:, 1, :]
+
         fetch(last - 1)
-        for h in range(2):
-            weave_x(nc.scalar.copy, 1, h, 0, 2)
+        code_tiles(held, 0, 0, "wgs%d" % (PACK - 2))
+        quantize(x_codes, x_sc, x_bf, 0, 0)
+        quantize(z_codes, z_sc, z_bf, 0, 0)
         for h in range(2):
             gelu_half(last - 1, h)
+            weave(nc.scalar.copy, z_bf, z_rows, 1, h, 0, PACK - 1)
+
+        scatter(last)
+        quantize_wv()
+        fetch(last)
+        code_tiles(held, 0, 1, "page%d" % (last % 4))
+        code_tiles(keep, 1, 0, "codes10")
+        code_tiles(keep, 1, 1, "codes11")
+        for h in range(2):
+            gelu_half(last, h)
+        quantize(x_codes, x_sc, x_bf, 0, 1)
+        weave(nc.vector.tensor_copy, x_bf, x_f32, 1, 0, 2, PACK)
+        quantize(z_codes, z_sc, z_bf, 0, 1)
+        quantize(x_codes, x_sc, x_bf, 1, 0)
+        weave(nc.vector.tensor_copy, x_bf, x_f32, 1, 1, 2, PACK)
+        quantize(z_codes, z_sc, z_bf, 1, 0)
+        quantize(x_codes, x_sc, x_bf, 1, 1)
+        quantize(z_codes, z_sc, z_bf, 1, 1)
 
         gate = {}
         value = {}
         for n in range(NT):
             gate[n, 0] = bank(n)
             gate_pass(gate[n, 0], n, 0, 0)
+        for n in range(NT):
             value[n, 0] = bank(NT + n)
             value_pass(value[n, 0], n, 0, 0)
-        scatter(last)
-        quantize(x_codes, x_sc, x_bf, 0, 1)
         for n in range(2):
             gate[n, 1] = bank(6 + n)
             gate_pass(gate[n, 1], n, 0, 1)
-        fetch(last)
-        for h in range(2):
-            gelu_half(last, h)
-        for h in range(2):
-            weave_x(nc.vector.tensor_copy, 1, h, 2, PACK)
-        quantize(x_codes, x_sc, x_bf, 1, 0)
-        quantize(z_codes, z_sc, z_bf, 1, 0)
-        quantize(x_codes, x_sc, x_bf, 1, 1)
-        quantize(z_codes, z_sc, z_bf, 1, 1)
 
         th = {}
 
         def squash(n, h):
-            th[n, h] = ring.tile([P, HALF], F32, name="th", bufs=3)
+            if h == 0:
+                th[n, h] = held.tile([P, HALF], F32, name="th", tag="wgs%d" % (0, 1, 3)[n], align_bytes=64)
+            else:
+                th[n, h] = held.tile([P, HALF], F32, name="th", tag="page%d" % n, align_bytes=64)
             nc.scalar.activation(th[n, h][:], gate[n, h][:], ACT.Tanh, scale=0.5)
 
         def finish(n, h):
-            res = ring.tile([P, HALF], F32, name="res", bufs=6)
+            res = keep.tile([P, HALF], F32, name="res", tag="staged%d" % (NT * h + n), align_bytes=64)
             nc.vector.scalar_tensor_tensor(out=res[:], in0=th[n, h][:], scalar=1.0, in1=value[n, h][:],
                                            op0=ALU.add, op1=ALU.mult)
             nc.sync.dma_start(out[P * n:P * (n + 1), cols(h)], res[:])
 
         for n in range(NT):
             gate_pass(gate[n, 0], n, 1, 0)
+            squash(n, 0)
         for n in range(NT):
             value_pass(value[n, 0], n, 1, 0)
         for n in range(2):
             gate_pass(gate[n, 1], n, 1, 1)
-        for n in range(NT):
-            squash(n, 0)
         gate[2, 1] = bank(0)
         for b in range(RP):
             gate_pass(gate[2, 1], 2, b, 1)

@@ -117,10 +117,17 @@ def tile_list_dialogue_reply_ranker_kernel(tc, tab_words, tab_scales, offs, offs
         weights = [held.tile([P, S], F32, name="wgs%d" % t, align_bytes=64) for t in range(PACK)]
         gin_t = held.tile([P, RP, PACK], F32)
         gout_t = held.tile([P, RP, PACK], F32)
-        for t in range(PACK):
-            load_page(t)
+
+        def load_weights(t, part):
             for q in (0, 2, 1, 3):
-                nc.sync.dma_start(weights[t][32 * q:32 * q + 32, :], wgs_rows[:, t, :])
+                nc.sync.dma_start(weights[t][32 * q:32 * q + 32, part], wgs_rows[:, t, part])
+
+        load_weights(0, cols(0))
+        load_page(0)
+        load_weights(0, cols(1))
+        for t in range(1, PACK):
+            load_page(t)
+            load_weights(t, slice(0, S))
             if t == 1:
                 nc.sync.dma_start(gin_t[:], gin.rearrange("(b p t) -> p b t", p=P, t=PACK))
                 nc.sync.dma_start(gout_t[:], gout.rearrange("(b p t) -> p b t", p=P, t=PACK))

@@ -23,6 +23,7 @@ RP = H // (P * PACK)
 HALF = 512
 NT = N // P
 QUADS = 4
+EARLY = 2 * P
 
 
 def tile_list_dialogue_reply_ranker_kernel(tc, tab_words, tab_scales, offs, offs2, offs3, w4_words, w4_scales,
@@ -46,8 +47,6 @@ def tile_list_dialogue_reply_ranker_kernel(tc, tab_words, tab_scales, offs, offs
         list2 = keep.tile([P, S // 16], U16)
         list3 = keep.tile([P, M // 16], U16)
         nc.sync.dma_start(list1[:], offs)
-        nc.sync.dma_start(list2[:], offs2)
-        nc.sync.dma_start(list3[:], offs3)
 
         tabs = []
 
@@ -63,49 +62,55 @@ def tile_list_dialogue_reply_ranker_kernel(tc, tab_words, tab_scales, offs, offs
 
         def load_scale_rows(tile, scales):
             rows = scales.rearrange("a q c -> (a q) c").bitcast(I32)
-            nc.scalar.dma_start(tile[32:64, :].bitcast(I32), rows[0:32, :])
-            nc.scalar.dma_start(tile[112:128, :].bitcast(I32), rows[32:48, :])
+            nc.sync.dma_start(tile[32:64, :].bitcast(I32), rows[0:32, :])
+            nc.sync.dma_start(tile[112:128, :].bitcast(I32), rows[32:48, :])
             nc.vector.memset(tile[0:32, :].bitcast(I32), 0)
             nc.vector.memset(tile[64:112, :].bitcast(I32), 0)
 
-        w4_raw = keep.tile([P, KP, 2 * H], U8, tag="tab2", align_bytes=64)
-        nc.sync.dma_start(w4_raw[:].bitcast(I32), w4_words.rearrange("a p c -> p a c").bitcast(I32))
-        load_table(keep, 0)
-        w4s_raw = keep.tile([P, H], U8, align_bytes=64)
-        ts_got = keep.tile([P, S], U8, align_bytes=64)
-        with tc.tile_pool(name="scale_window", bufs=1) as window_pool:
-            ts_win = window_pool.tile([P, T], U8, offset=T, align_bytes=64)
-            load_scale_rows(ts_win, tab_scales)
-            load_scale_rows(w4s_raw, w4_scales)
-            nc.vector.tensor_copy(ts_got[:], ts_win[:].indirect(list1[:]))
-        planes = keep.tile([P, KP, S + H], U8, align_bytes=64)
-        nc.gpsimd.memset(planes[:].bitcast(I32), 0)
-
-        w4_pool = ctx.enter_context(tc.tile_pool(name="w4_pool", bufs=1))
-        w4_codes = w4_pool.tile([P, RP, KP, 2 * HALF], U8, align_bytes=64)
-        v_codes = [keep.tile([P, S], U32, name="v_codes%d" % a, align_bytes=64) for a in range(KP)]
-        with tc.tile_pool(name="second_pass", bufs=1) as second_pool:
-            load_table(second_pool, 1)
-            scale_rows = keep.tile([P, S + H], U8, align_bytes=64)
-            nc.vector.tensor_copy(scale_rows[:, S:].rearrange("p (b t m) -> p b t m", b=RP, t=PACK),
-                                  w4s_raw[:].rearrange("p (b m t) -> p b t m", b=RP, t=PACK))
-            nc.vector.tensor_copy(scale_rows[:, :S].bitcast(I32), ts_got[:].bitcast(I32))
+        def move_scale_rows(queues, dst, part):
             for a in range(KP):
                 for q in range(QUADS):
                     first = row_first[a] + 4 * q
-                    nc.scalar.dma_start(planes[32 * q:32 * q + 4, a, :].bitcast(I32),
-                                        scale_rows[first:first + 4, :].bitcast(I32))
-            for b in range(RP):
-                nc.vector.tensor_copy(
-                    w4_codes[:, b].bitcast(U16).rearrange("p a (t m) -> p a t m", t=PACK),
-                    w4_raw[:].bitcast(U16)[:, :, cols(b)].rearrange("p a (m t) -> p a t m", t=PACK))
-            load_table(keep, 2)
+                    queue = queues[(QUADS * a + q) * len(queues) // (KP * QUADS)]
+                    queue.dma_start(dst[32 * q:32 * q + 4, a, :].bitcast(I32),
+                                    scale_rows[first:first + 4, part].bitcast(I32))
+
+        w4s_raw = keep.tile([P, H], U8, align_bytes=64)
+        ts_got = keep.tile([P, S], U8, tag="w4", align_bytes=64)
+        scale_rows = keep.tile([P, S + H], U8, align_bytes=64)
+        planes = keep.tile([P, KP, S + EARLY], U8, align_bytes=64)
+        v_codes = [keep.tile([P, S], U32, name="v_codes%d" % a, align_bytes=64) for a in range(KP)]
+        w4_raw = keep.tile([P, KP, 2 * HALF], U8, tag="tab2", align_bytes=64)
+        with tc.tile_pool(name="early", bufs=1) as early:
+            ts_win = early.tile([P, T], U8, align_bytes=64)
+            load_scale_rows(ts_win, tab_scales)
+            load_scale_rows(w4s_raw, w4_scales)
+            w4_rows = w4_words.rearrange("a p c -> p a c")
+            nc.sync.dma_start(w4_raw[:].bitcast(I32), w4_rows[:, :, :2 * HALF].bitcast(I32))
+            load_table(keep, 0)
+            nc.sync.dma_start(list2[:], offs2)
+            nc.sync.dma_start(list3[:], offs3)
+            load_table(early, 1)
+            nc.gpsimd.memset(planes[:].bitcast(I32), 0)
+            nc.vector.tensor_copy(ts_got[:], ts_win[:].indirect(list1[:]))
+            by_slice = scale_rows[:, S:].rearrange("p (b t m) -> p b t m", b=RP, t=PACK)
+            as_given = w4s_raw[:].rearrange("p (b m t) -> p b t m", b=RP, t=PACK)
+            nc.vector.tensor_copy(by_slice[:, 0, :EARLY // P], as_given[:, 0, :EARLY // P])
+            nc.vector.tensor_copy(scale_rows[:, :S].bitcast(I32), ts_got[:].bitcast(I32))
+            move_scale_rows((nc.scalar, nc.gpsimd), planes, slice(0, S + EARLY))
+            w4_first = keep.tile([P, KP, 2 * HALF], U8, tag="w4", align_bytes=64)
+            nc.vector.tensor_copy(w4_first[:].bitcast(U16).rearrange("p a (t c i) -> p a c t i", t=PACK, i=8),
+                                  w4_raw[:].bitcast(U16).rearrange("p a (c i t) -> p a c t i", t=PACK, i=8))
+            nc.vector.tensor_copy(by_slice[:, 0, EARLY // P:], as_given[:, 0, EARLY // P:])
+            nc.vector.tensor_copy(by_slice[:, 1], as_given[:, 1])
+            w4_codes = {t: w4_first[:, :, 2 * P * t:2 * P * (t + 1)] for t in range(PACK)}
+            load_table(keep, KP - 1)
             for a in range(KP - 1):
                 fetch_table(a, v_codes[a][:], list1[:])
+        held = ctx.enter_context(tc.tile_pool(name="held", bufs=1))
         for h in range(2):
             fetch_table(KP - 1, v_codes[KP - 1][:, cols(h)], entries(list1, h))
 
-        held = ctx.enter_context(tc.tile_pool(name="held", bufs=1))
         page_rows = page0.rearrange("(b p t) c -> b t p c", p=P, t=PACK)
         pages = {}
 
@@ -122,13 +127,18 @@ def tile_list_dialogue_reply_ranker_kernel(tc, tab_words, tab_scales, offs, offs
             for q in (0, 2, 1, 3):
                 nc.sync.dma_start(weights[t][32 * q:32 * q + 32, part], wgs_rows[:, t, part])
 
-        load_weights(0, cols(0))
         load_page(0)
+        load_weights(0, cols(0))
         load_weights(0, cols(1))
         for t in range(1, PACK):
             load_page(t)
             load_weights(t, slice(0, S))
             if t == 1:
+                w4_late = held.tile([P, KP, 2 * HALF], U8, align_bytes=64)
+                nc.sync.dma_start(w4_late[:].bitcast(I32), w4_rows[:, :, 2 * HALF:].bitcast(I32))
+                late_planes = held.tile([P, KP, H - EARLY], U8, align_bytes=64)
+                nc.gpsimd.memset(late_planes[:].bitcast(I32), 0)
+                move_scale_rows((nc.sync,), late_planes, slice(S + EARLY, S + H))
                 nc.sync.dma_start(gin_t[:], gin.rearrange("(b p t) -> p b t", p=P, t=PACK))
                 nc.sync.dma_start(gout_t[:], gout.rearrange("(b p t) -> p b t", p=P, t=PACK))
 
@@ -148,14 +158,19 @@ def tile_list_dialogue_reply_ranker_kernel(tc, tab_words, tab_scales, offs, offs
 
         def project(i):
             b, t = divmod(i, PACK)
+            if b == 1:
+                w4_codes[i] = keep.tile([P, KP, 2 * P], U8, name="w4_slice", tag="staged%d" % t, align_bytes=64)[:]
+                nc.gpsimd.tensor_copy(w4_codes[i].rearrange("p a (m e) -> p a m e", e=2),
+                                      w4_late[:].rearrange("p a (m t e) -> p a t m e", t=PACK, e=2)[:, :, t])
             staged[i] = keep.tile([P, S], F32, name="staged%d" % i, align_bytes=64)
             for h in range(2):
                 acc = bank(6 + h)
                 for a in range(KP):
                     nc.tensor.matmul_mx(
                         out=acc[:],
-                        lhsT=w4_codes[:, b, a, 2 * P * t:2 * P * (t + 1)].bitcast(FP4X4),
-                        lhsT_scale=planes[:, a, S + P * i:S + P * (i + 1)],
+                        lhsT=w4_codes[i][:, a].bitcast(FP4X4),
+                        lhsT_scale=(planes[:, a, S + P * i:S + P * (i + 1)] if P * i < EARLY
+                                    else late_planes[:, a, P * i - EARLY:P * (i + 1) - EARLY]),
                         rhs=v_codes[a][:, cols(h)].bitcast(FP8X4),
                         rhs_scale=planes[:, a, cols(h)],
                         start=(a == 0), stop=(a == KP - 1))
@@ -192,11 +207,11 @@ def tile_list_dialogue_reply_ranker_kernel(tc, tab_words, tab_scales, offs, offs
 
         def gelu_half(i, h):
             b, t = divmod(i, PACK)
-            if b not in z_rows:
+            if b == 0 and b not in z_rows:
                 z_rows[b] = keep.tile([P, PACK, M], BF16, name="z_rows%d" % b, align_bytes=64)
             ge = ring.tile([P, HALF], F32, name="ge", bufs=3)
             nc.scalar.activation(ge[:], x_f32[b][:, t, cols(h)], ACT.Gelu_apprx_tanh, scale=gin_t[:, b, t:t + 1])
-            dst = z_bf[b, h][:, :, t] if i == last else z_rows[b][:, t, cols(h)]
+            dst = z_bf[b, h][:, :, t] if b == 1 else z_rows[b][:, t, cols(h)]
             nc.scalar.activation(dst, ge[:], ACT.Copy, scale=gout_t[:, b, t:t + 1])
 
         def weave(copy, dst, src, b, h, t0=0, t1=PACK):
@@ -222,8 +237,7 @@ def tile_list_dialogue_reply_ranker_kernel(tc, tab_words, tab_scales, offs, offs
                 wv_raw[:, b].rearrange("p j (c i) -> p c j i", i=4), ACT.Copy, scale=0.5)
 
         def quantize_wv():
-            wv_codes = keep.tile([P, RP * N], U32, tag="staged%d" % last, align_bytes=64)
-            wv_q[0] = wv_codes
+            wv_codes = wv_q[0]
             for c0, c1 in ((0, 512), (512, RP * N)):
                 nc.vector.quantize_mx(out=wv_codes[:, c0:c1].bitcast(FP8X4), scales=wv_sc[:, c0:c1],
                                       in_=wv_bf[:, PACK * c0:PACK * c1])
@@ -262,34 +276,37 @@ def tile_list_dialogue_reply_ranker_kernel(tc, tab_words, tab_scales, offs, offs
                 for h in range(2):
                     weave(nc.scalar.copy, x_bf, x_f32, 1, h, 0, 2)
 
-        def code_tiles(pool, b, h, tag):
-            both = pool.tile([P, 2, HALF], U32, name="codes%d%d" % (b, h), tag=tag, align_bytes=64)
-            x_codes[b, h] = both[:, 0, :]
-            z_codes[b, h] = both[:, 1, :]
-
         fetch(last - 1)
-        code_tiles(held, 0, 0, "wgs%d" % (PACK - 2))
-        quantize(x_codes, x_sc, x_bf, 0, 0)
-        quantize(z_codes, z_sc, z_bf, 0, 0)
         for h in range(2):
             gelu_half(last - 1, h)
-            weave(nc.scalar.copy, z_bf, z_rows, 1, h, 0, PACK - 1)
+        nc.scalar.copy(x_bf[1, 1][:, :, PACK - 2], x_f32[1][:, PACK - 2, cols(1)])
 
         scatter(last)
-        quantize_wv()
+        x_first = keep.tile([P, HALF], U32, tag="staged%d" % last, align_bytes=64)
+        x_codes[0, 0] = x_first[:]
+        quantize(x_codes, x_sc, x_bf, 0, 0)
         fetch(last)
-        code_tiles(held, 0, 1, "page%d" % (last % 4))
-        code_tiles(keep, 1, 0, "codes10")
-        code_tiles(keep, 1, 1, "codes11")
+        after_fetch = held.tile([P, RP * N + HALF], U32, tag="page%d" % (last % 4), align_bytes=64)
+        wv_q[0] = after_fetch[:, :RP * N]
+        x_codes[0, 1] = after_fetch[:, RP * N:]
+        second_codes = keep.tile([P, 2, 2, HALF], U32, align_bytes=64)
         for h in range(2):
-            gelu_half(last, h)
-        quantize(x_codes, x_sc, x_bf, 0, 1)
+            x_codes[1, h] = second_codes[:, h, 0, :]
+            z_codes[1, h] = second_codes[:, h, 1, :]
+        gelu_half(last, 0)
+        nc.scalar.copy(x_bf[1, 1][:, :, PACK - 1], x_f32[1][:, PACK - 1, cols(1)])
+        gelu_half(last, 1)
         weave(nc.vector.tensor_copy, x_bf, x_f32, 1, 0, 2, PACK)
-        quantize(z_codes, z_sc, z_bf, 0, 1)
+        quantize_wv()
         quantize(x_codes, x_sc, x_bf, 1, 0)
-        weave(nc.vector.tensor_copy, x_bf, x_f32, 1, 1, 2, PACK)
+        z_first = keep.tile([P, 2, HALF], U32, tag="x_bf10", align_bytes=64)
+        for h in range(2):
+            z_codes[0, h] = z_first[:, h, :]
+        quantize(x_codes, x_sc, x_bf, 0, 1)
+        quantize(z_codes, z_sc, z_bf, 0, 0)
         quantize(z_codes, z_sc, z_bf, 1, 0)
         quantize(x_codes, x_sc, x_bf, 1, 1)
+        quantize(z_codes, z_sc, z_bf, 0, 1)
         quantize(z_codes, z_sc, z_bf, 1, 1)
 
         gate = {}
@@ -298,11 +315,13 @@ def tile_list_dialogue_reply_ranker_kernel(tc, tab_words, tab_scales, offs, offs
             gate[n, 0] = bank(n)
             gate_pass(gate[n, 0], n, 0, 0)
         for n in range(NT):
-            value[n, 0] = bank(NT + n)
-            value_pass(value[n, 0], n, 0, 0)
+            gate_pass(gate[n, 0], n, 1, 0)
         for n in range(2):
             gate[n, 1] = bank(6 + n)
             gate_pass(gate[n, 1], n, 0, 1)
+        for n in range(NT):
+            value[n, 0] = bank(NT + n)
+            value_pass(value[n, 0], n, 0, 0)
 
         th = {}
 
@@ -320,7 +339,6 @@ def tile_list_dialogue_reply_ranker_kernel(tc, tab_words, tab_scales, offs, offs
             nc.sync.dma_start(out[P * n:P * (n + 1), cols(h)], res[:])
 
         for n in range(NT):
-            gate_pass(gate[n, 0], n, 1, 0)
             squash(n, 0)
         for n in range(NT):
             value_pass(value[n, 0], n, 1, 0)

@@ -159,7 +159,7 @@ def tile_list_dialogue_reply_ranker_kernel(tc, tab_words, tab_scales, offs, offs
         def project(i):
             b, t = divmod(i, PACK)
             if b == 1:
-                w4_codes[i] = keep.tile([P, KP, 2 * P], U8, name="w4_slice", tag="staged%d" % t, align_bytes=64)[:]
+                w4_codes[i] = keep.tile([P, KP, 2 * P], U8, name="w4_slice", tag="staged%d" % (t + 1), align_bytes=64)[:]
                 nc.gpsimd.tensor_copy(w4_codes[i].rearrange("p a (m e) -> p a m e", e=2),
                                       w4_late[:].rearrange("p a (m t e) -> p a t m e", t=PACK, e=2)[:, :, t])
             staged[i] = keep.tile([P, S], F32, name="staged%d" % i, align_bytes=64)
@@ -207,11 +207,11 @@ def tile_list_dialogue_reply_ranker_kernel(tc, tab_words, tab_scales, offs, offs
 
         def gelu_half(i, h):
             b, t = divmod(i, PACK)
-            if b == 0 and b not in z_rows:
+            if b not in z_rows:
                 z_rows[b] = keep.tile([P, PACK, M], BF16, name="z_rows%d" % b, align_bytes=64)
             ge = ring.tile([P, HALF], F32, name="ge", bufs=3)
             nc.scalar.activation(ge[:], x_f32[b][:, t, cols(h)], ACT.Gelu_apprx_tanh, scale=gin_t[:, b, t:t + 1])
-            dst = z_bf[b, h][:, :, t] if b == 1 else z_rows[b][:, t, cols(h)]
+            dst = z_bf[b, h][:, :, t] if i == last else z_rows[b][:, t, cols(h)]
             nc.scalar.activation(dst, ge[:], ACT.Copy, scale=gout_t[:, b, t:t + 1])
 
         def weave(copy, dst, src, b, h, t0=0, t1=PACK):
@@ -237,7 +237,8 @@ def tile_list_dialogue_reply_ranker_kernel(tc, tab_words, tab_scales, offs, offs
                 wv_raw[:, b].rearrange("p j (c i) -> p c j i", i=4), ACT.Copy, scale=0.5)
 
         def quantize_wv():
-            wv_codes = wv_q[0]
+            wv_codes = keep.tile([P, RP * N], U32, tag="staged%d" % last, align_bytes=64)
+            wv_q[0] = wv_codes
             for c0, c1 in ((0, 512), (512, RP * N)):
                 nc.vector.quantize_mx(out=wv_codes[:, c0:c1].bitcast(FP8X4), scales=wv_sc[:, c0:c1],
                                       in_=wv_bf[:, PACK * c0:PACK * c1])
@@ -276,37 +277,34 @@ def tile_list_dialogue_reply_ranker_kernel(tc, tab_words, tab_scales, offs, offs
                 for h in range(2):
                     weave(nc.scalar.copy, x_bf, x_f32, 1, h, 0, 2)
 
+        def code_tiles(pool, b, h, tag):
+            both = pool.tile([P, 2, HALF], U32, name="codes%d%d" % (b, h), tag=tag, align_bytes=64)
+            x_codes[b, h] = both[:, 0, :]
+            z_codes[b, h] = both[:, 1, :]
+
         fetch(last - 1)
+        code_tiles(held, 0, 0, "wgs%d" % (PACK - 2))
+        quantize(x_codes, x_sc, x_bf, 0, 0)
+        quantize(z_codes, z_sc, z_bf, 0, 0)
         for h in range(2):
             gelu_half(last - 1, h)
-        nc.scalar.copy(x_bf[1, 1][:, :, PACK - 2], x_f32[1][:, PACK - 2, cols(1)])
+            weave(nc.scalar.copy, z_bf, z_rows, 1, h, 0, PACK - 1)
 
         scatter(last)
-        x_first = keep.tile([P, HALF], U32, tag="staged%d" % last, align_bytes=64)
-        x_codes[0, 0] = x_first[:]
-        quantize(x_codes, x_sc, x_bf, 0, 0)
-        fetch(last)
-        after_fetch = held.tile([P, RP * N + HALF], U32, tag="page%d" % (last % 4), align_bytes=64)
-        wv_q[0] = after_fetch[:, :RP * N]
-        x_codes[0, 1] = after_fetch[:, RP * N:]
-        second_codes = keep.tile([P, 2, 2, HALF], U32, align_bytes=64)
-        for h in range(2):
-            x_codes[1, h] = second_codes[:, h, 0, :]
-            z_codes[1, h] = second_codes[:, h, 1, :]
-        gelu_half(last, 0)
-        nc.scalar.copy(x_bf[1, 1][:, :, PACK - 1], x_f32[1][:, PACK - 1, cols(1)])
-        gelu_half(last, 1)
-        weave(nc.vector.tensor_copy, x_bf, x_f32, 1, 0, 2, PACK)
         quantize_wv()
-        quantize(x_codes, x_sc, x_bf, 1, 0)
-        z_first = keep.tile([P, 2, HALF], U32, tag="x_bf10", align_bytes=64)
+        fetch(last)
+        code_tiles(held, 0, 1, "page%d" % (last % 4))
+        code_tiles(keep, 1, 0, "codes10")
+        code_tiles(keep, 1, 1, "codes11")
         for h in range(2):
-            z_codes[0, h] = z_first[:, h, :]
+            gelu_half(last, h)
         quantize(x_codes, x_sc, x_bf, 0, 1)
-        quantize(z_codes, z_sc, z_bf, 0, 0)
+        weave(nc.vector.tensor_copy, x_bf, x_f32, 1, 0, 2, PACK)
+        quantize(z_codes, z_sc, z_bf, 0, 1)
+        quantize(x_codes, x_sc, x_bf, 1, 0)
+        weave(nc.vector.tensor_copy, x_bf, x_f32, 1, 1, 2, PACK)
         quantize(z_codes, z_sc, z_bf, 1, 0)
         quantize(x_codes, x_sc, x_bf, 1, 1)
-        quantize(z_codes, z_sc, z_bf, 0, 1)
         quantize(z_codes, z_sc, z_bf, 1, 1)
 
         gate = {}
@@ -315,13 +313,11 @@ def tile_list_dialogue_reply_ranker_kernel(tc, tab_words, tab_scales, offs, offs
             gate[n, 0] = bank(n)
             gate_pass(gate[n, 0], n, 0, 0)
         for n in range(NT):
-            gate_pass(gate[n, 0], n, 1, 0)
+            value[n, 0] = bank(NT + n)
+            value_pass(value[n, 0], n, 0, 0)
         for n in range(2):
             gate[n, 1] = bank(6 + n)
             gate_pass(gate[n, 1], n, 0, 1)
-        for n in range(NT):
-            value[n, 0] = bank(NT + n)
-            value_pass(value[n, 0], n, 0, 0)
 
         th = {}
 
@@ -339,6 +335,7 @@ def tile_list_dialogue_reply_ranker_kernel(tc, tab_words, tab_scales, offs, offs
             nc.sync.dma_start(out[P * n:P * (n + 1), cols(h)], res[:])
 
         for n in range(NT):
+            gate_pass(gate[n, 0], n, 1, 0)
             squash(n, 0)
         for n in range(NT):
             value_pass(value[n, 0], n, 1, 0)

@@ -211,8 +211,9 @@ def tile_list_dialogue_reply_ranker_kernel(tc, tab_words, tab_scales, offs, offs
                 z_rows[b] = keep.tile([P, PACK, M], BF16, name="z_rows%d" % b, align_bytes=64)
             ge = ring.tile([P, HALF], F32, name="ge", bufs=3)
             nc.scalar.activation(ge[:], x_f32[b][:, t, cols(h)], ACT.Gelu_apprx_tanh, scale=gin_t[:, b, t:t + 1])
-            dst = z_bf[b, h][:, :, t] if i == last else z_rows[b][:, t, cols(h)]
-            nc.scalar.activation(dst, ge[:], ACT.Copy, scale=gout_t[:, b, t:t + 1])
+            nc.scalar.activation(z_rows[b][:, t, cols(h)], ge[:], ACT.Copy, scale=gout_t[:, b, t:t + 1])
+            if i == last:
+                nc.scalar.copy(z_bf[b, h][:, :, t], z_rows[b][:, t, cols(h)])
 
         def weave(copy, dst, src, b, h, t0=0, t1=PACK):
             copy(dst[b, h][:, :, t0:t1].rearrange("p (c i) t -> p c t i", i=4),
@@ -237,8 +238,7 @@ def tile_list_dialogue_reply_ranker_kernel(tc, tab_words, tab_scales, offs, offs
                 wv_raw[:, b].rearrange("p j (c i) -> p c j i", i=4), ACT.Copy, scale=0.5)
 
         def quantize_wv():
-            wv_codes = keep.tile([P, RP * N], U32, tag="staged%d" % last, align_bytes=64)
-            wv_q[0] = wv_codes
+            wv_codes = wv_q[0]
             for c0, c1 in ((0, 512), (512, RP * N)):
                 nc.vector.quantize_mx(out=wv_codes[:, c0:c1].bitcast(FP8X4), scales=wv_sc[:, c0:c1],
                                       in_=wv_bf[:, PACK * c0:PACK * c1])
@@ -291,9 +291,12 @@ def tile_list_dialogue_reply_ranker_kernel(tc, tab_words, tab_scales, offs, offs
             weave(nc.scalar.copy, z_bf, z_rows, 1, h, 0, PACK - 1)
 
         scatter(last)
-        quantize_wv()
         fetch(last)
-        code_tiles(held, 0, 1, "page%d" % (last % 4))
+        after_fetch = held.tile([P, 2 * HALF + RP * N], U32, tag="page%d" % (last % 4), align_bytes=64)
+        x_codes[0, 1] = after_fetch[:, :HALF]
+        z_codes[0, 1] = after_fetch[:, HALF:2 * HALF]
+        wv_q[0] = after_fetch[:, 2 * HALF:]
+        quantize_wv()
         code_tiles(keep, 1, 0, "codes10")
         code_tiles(keep, 1, 1, "codes11")
         for h in range(2):

@@ -127,9 +127,10 @@ def tile_list_dialogue_reply_ranker_kernel(tc, tab_words, tab_scales, offs, offs
             for q in (0, 2, 1, 3):
                 nc.sync.dma_start(weights[t][32 * q:32 * q + 32, part], wgs_rows[:, t, part])
 
+        first_parts = (slice(0, S // 4), slice(S // 4, HALF), cols(1))
+        load_weights(0, first_parts[0])
         load_page(0)
-        load_weights(0, cols(0))
-        load_weights(0, cols(1))
+        load_weights(0, slice(S // 4, S))
         for t in range(1, PACK):
             load_page(t)
             load_weights(t, slice(0, S))
@@ -155,6 +156,7 @@ def tile_list_dialogue_reply_ranker_kernel(tc, tab_words, tab_scales, offs, offs
                               w8_scales[:, 4 * q:4 * q + 4, :].rearrange("b r c -> r b c").bitcast(I32))
 
         staged = {}
+        quarters = (slice(0, HALF // 2), slice(HALF // 2, HALF))
 
         def project(i):
             b, t = divmod(i, PACK)
@@ -180,17 +182,18 @@ def tile_list_dialogue_reply_ranker_kernel(tc, tab_words, tab_scales, offs, offs
             t = i % PACK
             weight = weights[t][:]
             if i == 0:
-                for h in range(2):
-                    nc.vector.tensor_tensor(pages[i][:].indirect(entries(list2, h)), staged[i][:, cols(h)],
-                                            weight[:, cols(h)], ALU.mult)
+                for part in first_parts:
+                    nc.vector.tensor_tensor(pages[i][:].indirect(list2[:, part.start // 16:part.stop // 16]),
+                                            staged[i][:, part], weight[:, part], ALU.mult)
             else:
                 nc.vector.tensor_tensor(pages[i][:].indirect(list2[:]), staged[i][:], weight, ALU.mult)
 
         def fetch(i):
             b, t = divmod(i, PACK)
             if i == RP * PACK - 1:
-                for h in range(2):
-                    nc.vector.tensor_copy(x_f32[b][:, t, cols(h)], pages[i][:].indirect(entries(list3, h)))
+                for part in quarters + (cols(1),):
+                    nc.vector.tensor_copy(x_f32[b][:, t, part],
+                                          pages[i][:].indirect(list3[:, part.start // 16:part.stop // 16]))
             else:
                 nc.vector.tensor_copy(x_f32[b][:, t, :], pages[i][:].indirect(list3[:]))
             if i + 4 < RP * PACK:
@@ -209,11 +212,13 @@ def tile_list_dialogue_reply_ranker_kernel(tc, tab_words, tab_scales, offs, offs
             b, t = divmod(i, PACK)
             if b not in z_rows:
                 z_rows[b] = keep.tile([P, PACK, M], BF16, name="z_rows%d" % b, align_bytes=64)
-            ge = ring.tile([P, HALF], F32, name="ge", bufs=3)
-            nc.scalar.activation(ge[:], x_f32[b][:, t, cols(h)], ACT.Gelu_apprx_tanh, scale=gin_t[:, b, t:t + 1])
-            nc.scalar.activation(z_rows[b][:, t, cols(h)], ge[:], ACT.Copy, scale=gout_t[:, b, t:t + 1])
-            if i == last:
-                nc.scalar.copy(z_bf[b, h][:, :, t], z_rows[b][:, t, cols(h)])
+            if (i, h) == (last, 1):
+                ge = z_rows[b][:, t, :].bitcast(F32)
+            else:
+                ge = ring.tile([P, HALF], F32, name="ge", bufs=3)[:]
+            nc.scalar.activation(ge, x_f32[b][:, t, cols(h)], ACT.Gelu_apprx_tanh, scale=gin_t[:, b, t:t + 1])
+            dst = z_bf[b, h][:, :, t] if i == last else z_rows[b][:, t, cols(h)]
+            nc.scalar.activation(dst, ge, ACT.Copy, scale=gout_t[:, b, t:t + 1])
 
         def weave(copy, dst, src, b, h, t0=0, t1=PACK):
             copy(dst[b, h][:, :, t0:t1].rearrange("p (c i) t -> p c t i", i=4),
@@ -274,8 +279,7 @@ def tile_list_dialogue_reply_ranker_kernel(tc, tab_words, tab_scales, offs, offs
                 for h in range(2):
                     weave(nc.scalar.copy, z_bf, z_rows, 0, h)
             if i == 6:
-                for h in range(2):
-                    weave(nc.scalar.copy, x_bf, x_f32, 1, h, 0, 2)
+                weave(nc.scalar.copy, x_bf, x_f32, 1, 1, 0, 2)
 
         def code_tiles(pool, b, h, tag):
             both = pool.tile([P, 2, HALF], U32, name="codes%d%d" % (b, h), tag=tag, align_bytes=64)
@@ -289,6 +293,7 @@ def tile_list_dialogue_reply_ranker_kernel(tc, tab_words, tab_scales, offs, offs
         for h in range(2):
             gelu_half(last - 1, h)
             weave(nc.scalar.copy, z_bf, z_rows, 1, h, 0, PACK - 1)
+        weave(nc.scalar.copy, x_bf, x_f32, 1, 0, 0, PACK - 1)
 
         scatter(last)
         fetch(last)
@@ -299,13 +304,19 @@ def tile_list_dialogue_reply_ranker_kernel(tc, tab_words, tab_scales, offs, offs
         quantize_wv()
         code_tiles(keep, 1, 0, "codes10")
         code_tiles(keep, 1, 1, "codes11")
-        for h in range(2):
-            gelu_half(last, h)
+        ge_left = ring.tile([P, HALF], F32, name="ge", bufs=3)
+        for part in quarters:
+            nc.scalar.activation(ge_left[:, part], x_f32[1][:, PACK - 1, part], ACT.Gelu_apprx_tanh,
+                                 scale=gin_t[:, 1, PACK - 1:PACK])
+            nc.scalar.copy(x_bf[1, 0][:, part, PACK - 1], x_f32[1][:, PACK - 1, part])
+        for part in quarters:
+            nc.scalar.activation(z_bf[1, 0][:, part, PACK - 1], ge_left[:, part], ACT.Copy,
+                                 scale=gout_t[:, 1, PACK - 1:PACK])
+        gelu_half(last, 1)
         quantize(x_codes, x_sc, x_bf, 0, 1)
-        weave(nc.vector.tensor_copy, x_bf, x_f32, 1, 0, 2, PACK)
-        quantize(z_codes, z_sc, z_bf, 0, 1)
-        quantize(x_codes, x_sc, x_bf, 1, 0)
         weave(nc.vector.tensor_copy, x_bf, x_f32, 1, 1, 2, PACK)
+        quantize(x_codes, x_sc, x_bf, 1, 0)
+        quantize(z_codes, z_sc, z_bf, 0, 1)
         quantize(z_codes, z_sc, z_bf, 1, 0)
         quantize(x_codes, x_sc, x_bf, 1, 1)
         quantize(z_codes, z_sc, z_bf, 1, 1)
@@ -322,18 +333,16 @@ def tile_list_dialogue_reply_ranker_kernel(tc, tab_words, tab_scales, offs, offs
             gate[n, 1] = bank(6 + n)
             gate_pass(gate[n, 1], n, 0, 1)
 
+        th_all = keep.tile([P, 2, NT, HALF], F32, tag="z_rows1", align_bytes=64)
         th = {}
 
         def squash(n, h):
-            if h == 0:
-                th[n, h] = held.tile([P, HALF], F32, name="th", tag="wgs%d" % (0, 1, 3)[n], align_bytes=64)
-            else:
-                th[n, h] = held.tile([P, HALF], F32, name="th", tag="page%d" % n, align_bytes=64)
-            nc.scalar.activation(th[n, h][:], gate[n, h][:], ACT.Tanh, scale=0.5)
+            th[n, h] = th_all[:, h, n, :]
+            nc.scalar.activation(th[n, h], gate[n, h][:], ACT.Tanh, scale=0.5)
 
         def finish(n, h):
             res = keep.tile([P, HALF], F32, name="res", tag="staged%d" % (NT * h + n), align_bytes=64)
-            nc.vector.scalar_tensor_tensor(out=res[:], in0=th[n, h][:], scalar=1.0, in1=value[n, h][:],
+            nc.vector.scalar_tensor_tensor(out=res[:], in0=th[n, h], scalar=1.0, in1=value[n, h][:],
                                            op0=ALU.add, op1=ALU.mult)
             nc.sync.dma_start(out[P * n:P * (n + 1), cols(h)], res[:])
 

@@ -67,17 +67,17 @@ def tile_list_dialogue_reply_ranker_kernel(tc, tab_words, tab_scales, offs, offs
             nc.vector.memset(tile[0:32, :].bitcast(I32), 0)
             nc.vector.memset(tile[64:112, :].bitcast(I32), 0)
 
-        def move_scale_rows(queues, dst, part):
+        def move_scale_rows(queues, dst, src):
             for a in range(KP):
                 for q in range(QUADS):
                     first = row_first[a] + 4 * q
                     queue = queues[(QUADS * a + q) * len(queues) // (KP * QUADS)]
                     queue.dma_start(dst[32 * q:32 * q + 4, a, :].bitcast(I32),
-                                    scale_rows[first:first + 4, part].bitcast(I32))
+                                    src[first:first + 4, :].bitcast(I32))
 
         w4s_raw = keep.tile([P, H], U8, align_bytes=64)
         ts_got = keep.tile([P, S], U8, tag="w4", align_bytes=64)
-        scale_rows = keep.tile([P, S + H], U8, align_bytes=64)
+        scale_rows = keep.tile([P, S + EARLY], U8, align_bytes=64)
         planes = keep.tile([P, KP, S + EARLY], U8, align_bytes=64)
         v_codes = [keep.tile([P, S], U32, name="v_codes%d" % a, align_bytes=64) for a in range(KP)]
         w4_raw = keep.tile([P, KP, 2 * HALF], U8, tag="tab2", align_bytes=64)
@@ -93,29 +93,31 @@ def tile_list_dialogue_reply_ranker_kernel(tc, tab_words, tab_scales, offs, offs
             load_table(early, 1)
             nc.gpsimd.memset(planes[:].bitcast(I32), 0)
             nc.vector.tensor_copy(ts_got[:], ts_win[:].indirect(list1[:]))
-            by_slice = scale_rows[:, S:].rearrange("p (b t m) -> p b t m", b=RP, t=PACK)
             as_given = w4s_raw[:].rearrange("p (b m t) -> p b t m", b=RP, t=PACK)
-            nc.vector.tensor_copy(by_slice[:, 0, :EARLY // P], as_given[:, 0, :EARLY // P])
+            nc.vector.tensor_copy(scale_rows[:, S:].rearrange("p (t m) -> p t m", m=P), as_given[:, 0, :EARLY // P])
             nc.vector.tensor_copy(scale_rows[:, :S].bitcast(I32), ts_got[:].bitcast(I32))
-            move_scale_rows((nc.scalar, nc.gpsimd), planes, slice(0, S + EARLY))
+            move_scale_rows((nc.scalar, nc.gpsimd), planes, scale_rows)
             w4_first = keep.tile([P, KP, 2 * HALF], U8, tag="w4", align_bytes=64)
             nc.vector.tensor_copy(w4_first[:].bitcast(U16).rearrange("p a (t c i) -> p a c t i", t=PACK, i=8),
                                   w4_raw[:].bitcast(U16).rearrange("p a (c i t) -> p a c t i", t=PACK, i=8))
-            nc.vector.tensor_copy(by_slice[:, 0, EARLY // P:], as_given[:, 0, EARLY // P:])
-            nc.vector.tensor_copy(by_slice[:, 1], as_given[:, 1])
             w4_codes = {t: w4_first[:, :, 2 * P * t:2 * P * (t + 1)] for t in range(PACK)}
             load_table(keep, KP - 1)
-            for a in range(KP - 1):
-                fetch_table(a, v_codes[a][:], list1[:])
+            fetch_table(0, v_codes[0][:], list1[:])
+            late_rows = keep.tile([P, H - EARLY], U8, align_bytes=64)
+            by_slice = late_rows[:].rearrange("p (t m) -> p t m", m=P)
+            nc.vector.tensor_copy(by_slice[:, :PACK - EARLY // P], as_given[:, 0, EARLY // P:])
+            nc.vector.tensor_copy(by_slice[:, PACK - EARLY // P:], as_given[:, 1])
+            fetch_table(1, v_codes[1][:], list1[:])
         held = ctx.enter_context(tc.tile_pool(name="held", bufs=1))
         for h in range(2):
             fetch_table(KP - 1, v_codes[KP - 1][:, cols(h)], entries(list1, h))
 
         page_rows = page0.rearrange("(b p t) c -> b t p c", p=P, t=PACK)
         pages = {}
+        page_tag = ["page%d" % k for k in (0, 1, 2, 3, 0, 2, 3, 0)]
 
         def load_page(i):
-            pages[i] = held.tile([P, T2], F32, name="page%d" % i, tag="page%d" % (i % 4), align_bytes=64)
+            pages[i] = held.tile([P, T2], F32, name="page%d" % i, tag=page_tag[i], align_bytes=64)
             nc.sync.dma_start(pages[i][:], page_rows[i // PACK, i % PACK])
 
         wgs_rows = wgs.rearrange("(q t) j -> q t j", t=PACK)
@@ -139,23 +141,26 @@ def tile_list_dialogue_reply_ranker_kernel(tc, tab_words, tab_scales, offs, offs
                 nc.sync.dma_start(w4_late[:].bitcast(I32), w4_rows[:, :, 2 * HALF:].bitcast(I32))
                 late_planes = held.tile([P, KP, H - EARLY], U8, align_bytes=64)
                 nc.gpsimd.memset(late_planes[:].bitcast(I32), 0)
-                move_scale_rows((nc.sync,), late_planes, slice(S + EARLY, S + H))
+                move_scale_rows((nc.sync,), late_planes, late_rows)
+            if t == PACK - 1:
                 nc.sync.dma_start(gin_t[:], gin.rearrange("(b p t) -> p b t", p=P, t=PACK))
                 nc.sync.dma_start(gout_t[:], gout.rearrange("(b p t) -> p b t", p=P, t=PACK))
 
         x_f32 = [keep.tile([P, PACK, M], F32, name="x_f32_0", tag="tab0", align_bytes=64),
                  keep.tile([P, PACK, M], F32, name="x_f32_1", tag="tab2", align_bytes=64)]
-        wv_raw = held.tile([P, RP, PACK, N], F32)
-        nc.sync.dma_start(wv_raw[:], wv.rearrange("(b p j) n -> p b j n", p=P, j=PACK))
         w8_sc = held.tile([P, RP, N], U8, align_bytes=64)
         nc.gpsimd.memset(w8_sc[:].bitcast(I32), 0)
-        w8_codes = held.tile([P, RP, N], U32, align_bytes=64)
-        nc.sync.dma_start(w8_codes[:].bitcast(I32), w8_words.rearrange("b p c i -> p b (c i)").bitcast(I32))
-        for q in range(QUADS):
-            nc.sync.dma_start(w8_sc[32 * q:32 * q + 4, :, :].bitcast(I32),
-                              w8_scales[:, 4 * q:4 * q + 4, :].rearrange("b r c -> r b c").bitcast(I32))
 
-        staged = {}
+        def load_w8():
+            w8_codes = keep.tile([P, RP, N], U32, tag="staged5", align_bytes=64)
+            nc.sync.dma_start(w8_codes[:].bitcast(I32), w8_words.rearrange("b p c i -> p b (c i)").bitcast(I32))
+            for q in range(QUADS):
+                nc.sync.dma_start(w8_sc[32 * q:32 * q + 4, :, :].bitcast(I32),
+                                  w8_scales[:, 4 * q:4 * q + 4, :].rearrange("b r c -> r b c").bitcast(I32))
+            return w8_codes
+
+        staged = [keep.tile([P, S], F32, name="staged%d" % i, align_bytes=64) for i in range(RP * PACK)]
+        middle = slice(S // 4, 3 * S // 4)
         quarters = (slice(0, HALF // 2), slice(HALF // 2, HALF))
 
         def project(i):
@@ -164,9 +169,8 @@ def tile_list_dialogue_reply_ranker_kernel(tc, tab_words, tab_scales, offs, offs
                 w4_codes[i] = keep.tile([P, KP, 2 * P], U8, name="w4_slice", tag="staged%d" % (t + 1), align_bytes=64)[:]
                 nc.gpsimd.tensor_copy(w4_codes[i].rearrange("p a (m e) -> p a m e", e=2),
                                       w4_late[:].rearrange("p a (m t e) -> p a t m e", t=PACK, e=2)[:, :, t])
-            staged[i] = keep.tile([P, S], F32, name="staged%d" % i, align_bytes=64)
             for h in range(2):
-                acc = bank(6 + h)
+                acc = bank((4 if i > 0 and i % 2 == 0 else 6) + h)
                 for a in range(KP):
                     nc.tensor.matmul_mx(
                         out=acc[:],
@@ -196,8 +200,6 @@ def tile_list_dialogue_reply_ranker_kernel(tc, tab_words, tab_scales, offs, offs
                                           pages[i][:].indirect(list3[:, part.start // 16:part.stop // 16]))
             else:
                 nc.vector.tensor_copy(x_f32[b][:, t, :], pages[i][:].indirect(list3[:]))
-            if i + 4 < RP * PACK:
-                load_page(i + 4)
 
         x_bf = {}
         z_bf = {}
@@ -206,12 +208,17 @@ def tile_list_dialogue_reply_ranker_kernel(tc, tab_words, tab_scales, offs, offs
                 x_bf[b, h] = keep.tile([P, HALF, PACK], BF16, name="x_bf%d%d" % (b, h), align_bytes=64)
                 z_bf[b, h] = keep.tile([P, HALF, PACK], BF16, name="z_bf%d%d" % (b, h), align_bytes=64)
 
-        z_rows = {}
+        z_rows = [keep.tile([P, PACK, M], BF16, name="z_rows%d" % b, align_bytes=64) for b in range(RP)]
+
+        def gelu_parts(i, parts):
+            b, t = divmod(i, PACK)
+            for part, ge in parts:
+                nc.scalar.activation(ge, x_f32[b][:, t, part], ACT.Gelu_apprx_tanh, scale=gin_t[:, b, t:t + 1])
+            for part, ge in parts:
+                nc.scalar.activation(z_rows[b][:, t, part], ge, ACT.Copy, scale=gout_t[:, b, t:t + 1])
 
         def gelu_half(i, h):
             b, t = divmod(i, PACK)
-            if b not in z_rows:
-                z_rows[b] = keep.tile([P, PACK, M], BF16, name="z_rows%d" % b, align_bytes=64)
             if (i, h) == (last, 1):
                 ge = z_rows[b][:, t, :].bitcast(F32)
             else:
@@ -237,7 +244,7 @@ def tile_list_dialogue_reply_ranker_kernel(tc, tab_words, tab_scales, offs, offs
         wv_q = {}
         wv_sc = keep.tile([P, RP * N], U8, align_bytes=64)
 
-        def weave_wv(b):
+        def weave_wv(wv_raw, b):
             nc.scalar.activation(
                 wv_bf[:, b * N * PACK:(b + 1) * N * PACK].rearrange("p (c i j) -> p c j i", i=4, j=PACK),
                 wv_raw[:, b].rearrange("p j (c i) -> p c j i", i=4), ACT.Copy, scale=0.5)
@@ -264,22 +271,46 @@ def tile_list_dialogue_reply_ranker_kernel(tc, tab_words, tab_scales, offs, offs
         project(0)
         project(1)
         scatter(0)
-        for i in range(1, last):
-            project(i + 1)
-            scatter(i)
-            fetch(i - 1)
-            for h in range(2):
-                gelu_half(i - 1, h)
-            if i in (2, 3):
-                weave_wv(i - 2)
-            if i == 4:
-                for h in range(2):
-                    weave(nc.scalar.copy, x_bf, x_f32, 0, h)
-            if i == 5:
-                for h in range(2):
-                    weave(nc.scalar.copy, z_bf, z_rows, 0, h)
-            if i == 6:
-                weave(nc.scalar.copy, x_bf, x_f32, 1, 1, 0, 2)
+        project(2)
+        fetch(0)
+        load_page(4)
+        scatter(1)
+        for i in range(2):
+            if i == 1:
+                scatter(2)
+                fetch(1)
+            gelu_parts(i, [(cols(0), x_f32[0][:, i + 1, cols(0)]), (cols(1), staged[i + 3][:, middle])])
+            project(i + 3)
+        wv_raw = held.tile([P, RP, PACK, N], F32, tag=page_tag[1], align_bytes=64)
+        nc.sync.dma_start(wv_raw[:], wv.rearrange("(b p j) n -> p b j n", p=P, j=PACK))
+        scatter(3)
+        fetch(2)
+        load_page(5)
+        gelu_parts(2, [(quarters[0], x_f32[0][:, 3, quarters[0]]), (quarters[1], x_f32[1][:, 0, quarters[0]]),
+                       (cols(1), staged[5][:, middle])])
+        project(5)
+        for b in range(RP):
+            weave_wv(wv_raw, b)
+        scatter(4)
+        fetch(3)
+        load_page(6)
+        fetch(4)
+        load_page(7)
+        for i in (3, 4):
+            ge = ring.tile([P, HALF], F32, name="ge", bufs=3)
+            gelu_parts(i, [(cols(0), ge[:]), (cols(1), staged[i + 3][:, middle])])
+            project(i + 3)
+        for h in range(2):
+            weave(nc.scalar.copy, x_bf, x_f32, 0, h)
+        scatter(5)
+        w8_codes = load_w8()
+        fetch(5)
+        for h in range(2):
+            gelu_half(5, h)
+        for h in range(2):
+            weave(nc.scalar.copy, z_bf, z_rows, 0, h)
+        weave(nc.scalar.copy, x_bf, x_f32, 1, 1, 0, 2)
+        scatter(6)
 
         def code_tiles(pool, b, h, tag):
             both = pool.tile([P, 2, HALF], U32, name="codes%d%d" % (b, h), tag=tag, align_bytes=64)
@@ -297,7 +328,7 @@ def tile_list_dialogue_reply_ranker_kernel(tc, tab_words, tab_scales, offs, offs
 
         scatter(last)
         fetch(last)
-        after_fetch = held.tile([P, 2 * HALF + RP * N], U32, tag="page%d" % (last % 4), align_bytes=64)
+        after_fetch = held.tile([P, 2 * HALF + RP * N], U32, tag=page_tag[last], align_bytes=64)
         x_codes[0, 1] = after_fetch[:, :HALF]
         z_codes[0, 1] = after_fetch[:, HALF:2 * HALF]
         wv_q[0] = after_fetch[:, 2 * HALF:]
@@ -341,7 +372,7 @@ def tile_list_dialogue_reply_ranker_kernel(tc, tab_words, tab_scales, offs, offs
             nc.scalar.activation(th[n, h], gate[n, h][:], ACT.Tanh, scale=0.5)
 
         def finish(n, h):
-            res = keep.tile([P, HALF], F32, name="res", tag="staged%d" % (NT * h + n), align_bytes=64)
+            res = keep.tile([P, HALF], F32, name="res", tag="staged%d" % (0, 1, 2, 3, 4, 6)[NT * h + n], align_bytes=64)
             nc.vector.scalar_tensor_tensor(out=res[:], in0=th[n, h], scalar=1.0, in1=value[n, h][:],
                                            op0=ALU.add, op1=ALU.mult)
             nc.sync.dma_start(out[P * n:P * (n + 1), cols(h)], res[:])

@@ -249,11 +249,11 @@ def tile_list_dialogue_reply_ranker_kernel(tc, tab_words, tab_scales, offs, offs
                 wv_bf[:, b * N * PACK:(b + 1) * N * PACK].rearrange("p (c i j) -> p c j i", i=4, j=PACK),
                 wv_raw[:, b].rearrange("p j (c i) -> p c j i", i=4), ACT.Copy, scale=0.5)
 
-        def quantize_wv():
-            wv_codes = wv_q[0]
-            for c0, c1 in ((0, 512), (512, RP * N)):
-                nc.vector.quantize_mx(out=wv_codes[:, c0:c1].bitcast(FP8X4), scales=wv_sc[:, c0:c1],
-                                      in_=wv_bf[:, PACK * c0:PACK * c1])
+        def quantize_wv(k, codes):
+            wv_q[k] = codes
+            c0, c1 = 2 * P * k, 2 * P * (k + 1)
+            nc.vector.quantize_mx(out=codes.bitcast(FP8X4), scales=wv_sc[:, c0:c1],
+                                  in_=wv_bf[:, PACK * c0:PACK * c1])
 
         def gate_pass(acc, n, b, h):
             nc.tensor.matmul_mx(out=acc[:], lhsT=w8_codes[:, b, P * n:P * (n + 1)].bitcast(FP8X4),
@@ -263,7 +263,7 @@ def tile_list_dialogue_reply_ranker_kernel(tc, tab_words, tab_scales, offs, offs
 
         def value_pass(acc, n, b, h):
             c0 = b * N + P * n
-            nc.tensor.matmul_mx(out=acc[:], lhsT=wv_q[0][:, c0:c0 + P].bitcast(FP8X4), lhsT_scale=wv_sc[:, c0:c0 + P],
+            nc.tensor.matmul_mx(out=acc[:], lhsT=wv_q[c0 // (2 * P)][:, c0 % (2 * P):c0 % (2 * P) + P].bitcast(FP8X4), lhsT_scale=wv_sc[:, c0:c0 + P],
                                 rhs=z_codes[b, h].bitcast(FP8X4), rhs_scale=z_sc[:, b, cols(h)],
                                 start=(b == 0), stop=(b == RP - 1))
 
@@ -297,20 +297,26 @@ def tile_list_dialogue_reply_ranker_kernel(tc, tab_words, tab_scales, offs, offs
         fetch(4)
         load_page(7)
         for i in (3, 4):
-            ge = ring.tile([P, HALF], F32, name="ge", bufs=3)
-            gelu_parts(i, [(cols(0), ge[:]), (cols(1), staged[i + 3][:, middle])])
+            ge = keep.tile([P, 2 * P], F32, name="ge%d" % i, tag="wv_part%d" % (i - 3), align_bytes=64)
+            gelu_parts(i, [(quarters[0], ge[:]), (quarters[1], x_f32[1][:, i - 2, quarters[0]]),
+                           (cols(1), staged[i + 3][:, middle])])
             project(i + 3)
         for h in range(2):
             weave(nc.scalar.copy, x_bf, x_f32, 0, h)
         scatter(5)
         w8_codes = load_w8()
+        quantize_wv(0, keep.tile([P, 2 * P], U32, name="wv_codes0", tag="wv_part0", align_bytes=64)[:])
         fetch(5)
         for h in range(2):
-            gelu_half(5, h)
-        for h in range(2):
             weave(nc.scalar.copy, z_bf, z_rows, 0, h)
-        weave(nc.scalar.copy, x_bf, x_f32, 1, 1, 0, 2)
+        ge_first = keep.tile([P, P], F32, tag="codes00", align_bytes=64)
+        ge_last = held.tile([P, P], F32, tag=page_tag[1], align_bytes=64)
+        gelu_parts(5, [(slice(0, P), ge_first[:]), (slice(P, M - P), x_f32[1][:, 3, P:M - P]),
+                       (slice(M - P, M), ge_last[:])])
+        for h in range(2):
+            weave(nc.scalar.copy, x_bf, x_f32, 1, h, 0, 2)
         scatter(6)
+        quantize_wv(1, keep.tile([P, 2 * P], U32, name="wv_codes1", tag="wv_part1", align_bytes=64)[:])
 
         def code_tiles(pool, b, h, tag):
             both = pool.tile([P, 2, HALF], U32, name="codes%d%d" % (b, h), tag=tag, align_bytes=64)
@@ -318,36 +324,36 @@ def tile_list_dialogue_reply_ranker_kernel(tc, tab_words, tab_scales, offs, offs
             z_codes[b, h] = both[:, 1, :]
 
         fetch(last - 1)
-        code_tiles(held, 0, 0, "wgs%d" % (PACK - 2))
+        code_tiles(keep, 0, 0, "codes00")
         quantize(x_codes, x_sc, x_bf, 0, 0)
         quantize(z_codes, z_sc, z_bf, 0, 0)
         for h in range(2):
             gelu_half(last - 1, h)
             weave(nc.scalar.copy, z_bf, z_rows, 1, h, 0, PACK - 1)
-        weave(nc.scalar.copy, x_bf, x_f32, 1, 0, 0, PACK - 1)
 
         scatter(last)
         fetch(last)
-        after_fetch = held.tile([P, 2 * HALF + RP * N], U32, tag=page_tag[last], align_bytes=64)
+        after_fetch = held.tile([P, 2 * HALF + 2 * P], U32, tag=page_tag[1], align_bytes=64)
         x_codes[0, 1] = after_fetch[:, :HALF]
         z_codes[0, 1] = after_fetch[:, HALF:2 * HALF]
-        wv_q[0] = after_fetch[:, 2 * HALF:]
-        quantize_wv()
         code_tiles(keep, 1, 0, "codes10")
-        code_tiles(keep, 1, 1, "codes11")
-        ge_left = ring.tile([P, HALF], F32, name="ge", bufs=3)
-        for part in quarters:
-            nc.scalar.activation(ge_left[:, part], x_f32[1][:, PACK - 1, part], ACT.Gelu_apprx_tanh,
+        ge_second = keep.tile([P, HALF // 2], F32, tag="codes11", align_bytes=64)
+        ge_left = (z_rows[1][:, PACK - 1, :].bitcast(F32)[:, quarters[0]], ge_second[:])
+        for part, ge in zip(quarters, ge_left):
+            nc.scalar.activation(ge, x_f32[1][:, PACK - 1, part], ACT.Gelu_apprx_tanh,
                                  scale=gin_t[:, 1, PACK - 1:PACK])
-            nc.scalar.copy(x_bf[1, 0][:, part, PACK - 1], x_f32[1][:, PACK - 1, part])
-        for part in quarters:
-            nc.scalar.activation(z_bf[1, 0][:, part, PACK - 1], ge_left[:, part], ACT.Copy,
+            nc.gpsimd.tensor_scalar(x_bf[1, 0][:, part, 2:], x_f32[1][:, 2:, part].rearrange("p t c -> p c t"),
+                                    1.0, 0.0, ALU.mult, ALU.add)
+        for part, ge in zip(quarters, ge_left):
+            nc.scalar.activation(z_bf[1, 0][:, part, PACK - 1], ge, ACT.Copy,
                                  scale=gout_t[:, 1, PACK - 1:PACK])
         gelu_half(last, 1)
+        code_tiles(keep, 1, 1, "codes11")
         quantize(x_codes, x_sc, x_bf, 0, 1)
-        weave(nc.vector.tensor_copy, x_bf, x_f32, 1, 1, 2, PACK)
-        quantize(x_codes, x_sc, x_bf, 1, 0)
         quantize(z_codes, z_sc, z_bf, 0, 1)
+        quantize_wv(2, after_fetch[:, 2 * HALF:])
+        quantize(x_codes, x_sc, x_bf, 1, 0)
+        weave(nc.vector.tensor_copy, x_bf, x_f32, 1, 1, 2, PACK)
         quantize(z_codes, z_sc, z_bf, 1, 0)
         quantize(x_codes, x_sc, x_bf, 1, 1)
         quantize(z_codes, z_sc, z_bf, 1, 1)

@@ -31,6 +31,7 @@ def tile_list_dialogue_reply_ranker_kernel(tc, tab_words, tab_scales, offs, offs
     nc = tc.nc
     with ExitStack() as ctx:
         keep = ctx.enter_context(tc.tile_pool(name="keep", bufs=1))
+        first = ctx.enter_context(tc.tile_pool(name="first", bufs=1))
         ring = ctx.enter_context(tc.tile_pool(name="ring", bufs=2))
         psum = ctx.enter_context(tc.psum_pool(name="psum", bufs=1))
 
@@ -50,8 +51,8 @@ def tile_list_dialogue_reply_ranker_kernel(tc, tab_words, tab_scales, offs, offs
 
         tabs = []
 
-        def load_table(pool, a):
-            tab = pool.tile([P, T], I32, name="tab%d" % a, align_bytes=64)
+        def load_table(pool, a, **place):
+            tab = pool.tile([P, T], I32, name="tab%d" % a, align_bytes=64, **place)
             nc.sync.dma_start(tab[:], tab_words[a].rearrange("p t i -> p (t i)").bitcast(I32))
             tabs.append(tab)
 
@@ -87,7 +88,7 @@ def tile_list_dialogue_reply_ranker_kernel(tc, tab_words, tab_scales, offs, offs
             load_scale_rows(w4s_raw, w4_scales)
             w4_rows = w4_words.rearrange("a p c -> p a c")
             nc.sync.dma_start(w4_raw[:].bitcast(I32), w4_rows[:, :, :2 * HALF].bitcast(I32))
-            load_table(keep, 0)
+            load_table(first, 0, offset=0)
             nc.sync.dma_start(list2[:], offs2)
             nc.sync.dma_start(list3[:], offs3)
             load_table(early, 1)
@@ -129,7 +130,7 @@ def tile_list_dialogue_reply_ranker_kernel(tc, tab_words, tab_scales, offs, offs
             for q in (0, 2, 1, 3):
                 nc.sync.dma_start(weights[t][32 * q:32 * q + 32, part], wgs_rows[:, t, part])
 
-        first_parts = (slice(0, S // 4), slice(S // 4, HALF), cols(1))
+        first_parts = (slice(0, S // 4), slice(S // 4, S))
         load_weights(0, first_parts[0])
         load_page(0)
         load_weights(0, slice(S // 4, S))
@@ -146,7 +147,7 @@ def tile_list_dialogue_reply_ranker_kernel(tc, tab_words, tab_scales, offs, offs
                 nc.sync.dma_start(gin_t[:], gin.rearrange("(b p t) -> p b t", p=P, t=PACK))
                 nc.sync.dma_start(gout_t[:], gout.rearrange("(b p t) -> p b t", p=P, t=PACK))
 
-        x_f32 = [keep.tile([P, PACK, M], F32, name="x_f32_0", tag="tab0", align_bytes=64),
+        x_f32 = [first.tile([P, PACK, M], F32, name="x_f32_0", align_bytes=64, offset=0),
                  keep.tile([P, PACK, M], F32, name="x_f32_1", tag="tab2", align_bytes=64)]
         w8_sc = held.tile([P, RP, N], U8, align_bytes=64)
         nc.gpsimd.memset(w8_sc[:].bitcast(I32), 0)
@@ -220,7 +221,7 @@ def tile_list_dialogue_reply_ranker_kernel(tc, tab_words, tab_scales, offs, offs
         def gelu_half(i, h):
             b, t = divmod(i, PACK)
             if (i, h) == (last, 1):
-                ge = z_rows[b][:, t, :].bitcast(F32)
+                ge = first.tile([P, HALF], F32, name="ge_right", align_bytes=64, offset=late_bytes)[:]
             else:
                 ge = ring.tile([P, HALF], F32, name="ge", bufs=3)[:]
             nc.scalar.activation(ge, x_f32[b][:, t, cols(h)], ACT.Gelu_apprx_tanh, scale=gin_t[:, b, t:t + 1])
@@ -313,8 +314,7 @@ def tile_list_dialogue_reply_ranker_kernel(tc, tab_words, tab_scales, offs, offs
         ge_last = held.tile([P, P], F32, tag=page_tag[1], align_bytes=64)
         gelu_parts(5, [(slice(0, P), ge_first[:]), (slice(P, M - P), x_f32[1][:, 3, P:M - P]),
                        (slice(M - P, M), ge_last[:])])
-        for h in range(2):
-            weave(nc.scalar.copy, x_bf, x_f32, 1, h, 0, 2)
+        weave(nc.scalar.copy, x_bf, x_f32, 1, 1, 0, 2)
         scatter(6)
         quantize_wv(1, keep.tile([P, 2 * P], U32, name="wv_codes1", tag="wv_part1", align_bytes=64)[:])
 
@@ -324,35 +324,38 @@ def tile_list_dialogue_reply_ranker_kernel(tc, tab_words, tab_scales, offs, offs
             z_codes[b, h] = both[:, 1, :]
 
         fetch(last - 1)
-        code_tiles(keep, 0, 0, "codes00")
+        x_codes[0, 0] = keep.tile([P, HALF], U32, name="x_codes00", tag="codes00", align_bytes=64)[:]
         quantize(x_codes, x_sc, x_bf, 0, 0)
-        quantize(z_codes, z_sc, z_bf, 0, 0)
         for h in range(2):
             gelu_half(last - 1, h)
             weave(nc.scalar.copy, z_bf, z_rows, 1, h, 0, PACK - 1)
+        weave(nc.scalar.copy, x_bf, x_f32, 1, 0, 0, PACK - 1)
 
         scatter(last)
         fetch(last)
-        after_fetch = held.tile([P, 2 * HALF + 2 * P], U32, tag=page_tag[1], align_bytes=64)
-        x_codes[0, 1] = after_fetch[:, :HALF]
-        z_codes[0, 1] = after_fetch[:, HALF:2 * HALF]
+        x_codes[0, 1] = held.tile([P, HALF], U32, name="x_codes01", tag=page_tag[1], align_bytes=64)[:]
         code_tiles(keep, 1, 0, "codes10")
         ge_second = keep.tile([P, HALF // 2], F32, tag="codes11", align_bytes=64)
-        ge_left = (z_rows[1][:, PACK - 1, :].bitcast(F32)[:, quarters[0]], ge_second[:])
+        late_words = 2 * HALF + 2 * P
+        late_bytes = 4 * late_words
+        ge_front = first.tile([P, HALF // 2], F32, align_bytes=64, offset=late_bytes - HALF)
+        ge_left = (ge_front[:], ge_second[:])
         for part, ge in zip(quarters, ge_left):
             nc.scalar.activation(ge, x_f32[1][:, PACK - 1, part], ACT.Gelu_apprx_tanh,
                                  scale=gin_t[:, 1, PACK - 1:PACK])
-            nc.gpsimd.tensor_scalar(x_bf[1, 0][:, part, 2:], x_f32[1][:, 2:, part].rearrange("p t c -> p c t"),
-                                    1.0, 0.0, ALU.mult, ALU.add)
+            nc.scalar.copy(x_bf[1, 0][:, part, PACK - 1], x_f32[1][:, PACK - 1, part])
         for part, ge in zip(quarters, ge_left):
             nc.scalar.activation(z_bf[1, 0][:, part, PACK - 1], ge, ACT.Copy,
                                  scale=gout_t[:, 1, PACK - 1:PACK])
         gelu_half(last, 1)
         code_tiles(keep, 1, 1, "codes11")
         quantize(x_codes, x_sc, x_bf, 0, 1)
-        quantize(z_codes, z_sc, z_bf, 0, 1)
-        quantize_wv(2, after_fetch[:, 2 * HALF:])
         quantize(x_codes, x_sc, x_bf, 1, 0)
+        late_codes = first.tile([P, late_words], U32, align_bytes=64, offset=0)
+        for h in range(2):
+            z_codes[0, h] = late_codes[:, cols(h)]
+            quantize(z_codes, z_sc, z_bf, 0, h)
+        quantize_wv(2, late_codes[:, 2 * HALF:])
         weave(nc.vector.tensor_copy, x_bf, x_f32, 1, 1, 2, PACK)
         quantize(z_codes, z_sc, z_bf, 1, 0)
         quantize(x_codes, x_sc, x_bf, 1, 1)
@@ -370,7 +373,7 @@ def tile_list_dialogue_reply_ranker_kernel(tc, tab_words, tab_scales, offs, offs
             gate[n, 1] = bank(6 + n)
             gate_pass(gate[n, 1], n, 0, 1)
 
-        th_all = keep.tile([P, 2, NT, HALF], F32, tag="z_rows1", align_bytes=64)
+        th_all = first.tile([P, 2, NT, HALF], F32, align_bytes=64, offset=late_bytes)
         th = {}
 
         def squash(n, h):

@@ -149,6 +149,8 @@ def tile_list_dialogue_reply_ranker_kernel(tc, tab_words, tab_scales, offs, offs
 
         x_f32 = [first.tile([P, PACK, M], F32, name="x_f32_0", align_bytes=64, offset=0),
                  keep.tile([P, PACK, M], F32, name="x_f32_1", tag="tab2", align_bytes=64)]
+        wv_raw = x_f32[1][:, :PACK - 1, :].rearrange("p t m -> p (t m)").rearrange("p (b j n) -> p b j n", b=RP, j=PACK)
+        nc.sync.dma_start(wv_raw, wv.rearrange("(b p j) n -> p b j n", p=P, j=PACK))
         w8_sc = held.tile([P, RP, N], U8, align_bytes=64)
         nc.gpsimd.memset(w8_sc[:].bitcast(I32), 0)
 
@@ -282,16 +284,19 @@ def tile_list_dialogue_reply_ranker_kernel(tc, tab_words, tab_scales, offs, offs
                 fetch(1)
             gelu_parts(i, [(cols(0), x_f32[0][:, i + 1, cols(0)]), (cols(1), staged[i + 3][:, middle])])
             project(i + 3)
-        wv_raw = held.tile([P, RP, PACK, N], F32, tag=page_tag[1], align_bytes=64)
-        nc.sync.dma_start(wv_raw[:], wv.rearrange("(b p j) n -> p b j n", p=P, j=PACK))
+            for h in range(2):
+                if i == 0:
+                    weave_wv(wv_raw, h)
+                else:
+                    weave(nc.scalar.copy, x_bf, x_f32, 0, h, 0, 2)
         scatter(3)
         fetch(2)
         load_page(5)
         gelu_parts(2, [(quarters[0], x_f32[0][:, 3, quarters[0]]), (quarters[1], x_f32[1][:, 0, quarters[0]]),
                        (cols(1), staged[5][:, middle])])
         project(5)
-        for b in range(RP):
-            weave_wv(wv_raw, b)
+        for h in range(2):
+            weave(nc.scalar.copy, z_bf, z_rows, 0, h, 0, 2)
         scatter(4)
         fetch(3)
         load_page(6)
@@ -303,18 +308,19 @@ def tile_list_dialogue_reply_ranker_kernel(tc, tab_words, tab_scales, offs, offs
                            (cols(1), staged[i + 3][:, middle])])
             project(i + 3)
         for h in range(2):
-            weave(nc.scalar.copy, x_bf, x_f32, 0, h)
+            weave(nc.scalar.copy, x_bf, x_f32, 0, h, 2, PACK)
         scatter(5)
         w8_codes = load_w8()
         quantize_wv(0, keep.tile([P, 2 * P], U32, name="wv_codes0", tag="wv_part0", align_bytes=64)[:])
         fetch(5)
         for h in range(2):
-            weave(nc.scalar.copy, z_bf, z_rows, 0, h)
+            weave(nc.scalar.copy, z_bf, z_rows, 0, h, 2, PACK)
         ge_first = keep.tile([P, P], F32, tag="codes00", align_bytes=64)
         ge_last = held.tile([P, P], F32, tag=page_tag[1], align_bytes=64)
         gelu_parts(5, [(slice(0, P), ge_first[:]), (slice(P, M - P), x_f32[1][:, 3, P:M - P]),
                        (slice(M - P, M), ge_last[:])])
-        weave(nc.scalar.copy, x_bf, x_f32, 1, 1, 0, 2)
+        for h in range(2):
+            weave(nc.scalar.copy, x_bf, x_f32, 1, h, 0, 2)
         scatter(6)
         quantize_wv(1, keep.tile([P, 2 * P], U32, name="wv_codes1", tag="wv_part1", align_bytes=64)[:])
 
@@ -329,7 +335,6 @@ def tile_list_dialogue_reply_ranker_kernel(tc, tab_words, tab_scales, offs, offs
         for h in range(2):
             gelu_half(last - 1, h)
             weave(nc.scalar.copy, z_bf, z_rows, 1, h, 0, PACK - 1)
-        weave(nc.scalar.copy, x_bf, x_f32, 1, 0, 0, PACK - 1)
 
         scatter(last)
         fetch(last)
@@ -343,12 +348,12 @@ def tile_list_dialogue_reply_ranker_kernel(tc, tab_words, tab_scales, offs, offs
         for part, ge in zip(quarters, ge_left):
             nc.scalar.activation(ge, x_f32[1][:, PACK - 1, part], ACT.Gelu_apprx_tanh,
                                  scale=gin_t[:, 1, PACK - 1:PACK])
-            nc.scalar.copy(x_bf[1, 0][:, part, PACK - 1], x_f32[1][:, PACK - 1, part])
         for part, ge in zip(quarters, ge_left):
             nc.scalar.activation(z_bf[1, 0][:, part, PACK - 1], ge, ACT.Copy,
                                  scale=gout_t[:, 1, PACK - 1:PACK])
         gelu_half(last, 1)
         code_tiles(keep, 1, 1, "codes11")
+        weave(nc.vector.tensor_copy, x_bf, x_f32, 1, 0, 2, PACK)
         quantize(x_codes, x_sc, x_bf, 0, 1)
         quantize(x_codes, x_sc, x_bf, 1, 0)
         late_codes = first.tile([P, late_words], U32, align_bytes=64, offset=0)

@@ -109,6 +109,7 @@ def tile_list_dialogue_reply_ranker_kernel(tc, tab_words, tab_scales, offs, offs
             nc.vector.tensor_copy(by_slice[:, :PACK - EARLY // P], as_given[:, 0, EARLY // P:])
             nc.vector.tensor_copy(by_slice[:, PACK - EARLY // P:], as_given[:, 1])
             fetch_table(1, v_codes[1][:], list1[:])
+        second = ctx.enter_context(tc.tile_pool(name="second", bufs=1))
         held = ctx.enter_context(tc.tile_pool(name="held", bufs=1))
         for h in range(2):
             fetch_table(KP - 1, v_codes[KP - 1][:, cols(h)], entries(list1, h))
@@ -118,11 +119,15 @@ def tile_list_dialogue_reply_ranker_kernel(tc, tab_words, tab_scales, offs, offs
         page_tag = ["page%d" % k for k in (0, 1, 2, 3, 0, 2, 3, 0)]
 
         def load_page(i):
-            pages[i] = held.tile([P, T2], F32, name="page%d" % i, tag=page_tag[i], align_bytes=64)
+            if page_tag[i] == page_tag[0]:
+                pages[i] = first.tile([P, T2], F32, name="page%d" % i, tag=page_tag[i], align_bytes=64, offset=0)
+            else:
+                pages[i] = held.tile([P, T2], F32, name="page%d" % i, tag=page_tag[i], align_bytes=64)
             nc.sync.dma_start(pages[i][:], page_rows[i // PACK, i % PACK])
 
         wgs_rows = wgs.rearrange("(q t) j -> q t j", t=PACK)
-        weights = [held.tile([P, S], F32, name="wgs%d" % t, align_bytes=64) for t in range(PACK)]
+        weights = [first.tile([P, S], F32, name="wgs0", align_bytes=64, offset=4 * T2)]
+        weights.extend(held.tile([P, S], F32, name="wgs%d" % t, align_bytes=64) for t in range(1, PACK))
         gin_t = held.tile([P, RP, PACK], F32)
         gout_t = held.tile([P, RP, PACK], F32)
 
@@ -147,7 +152,7 @@ def tile_list_dialogue_reply_ranker_kernel(tc, tab_words, tab_scales, offs, offs
                 nc.sync.dma_start(gin_t[:], gin.rearrange("(b p t) -> p b t", p=P, t=PACK))
                 nc.sync.dma_start(gout_t[:], gout.rearrange("(b p t) -> p b t", p=P, t=PACK))
 
-        x_f32 = [first.tile([P, PACK, M], F32, name="x_f32_0", align_bytes=64, offset=0),
+        x_f32 = [second.tile([P, PACK, M], F32, name="x_f32_0", align_bytes=64, offset=0),
                  keep.tile([P, PACK, M], F32, name="x_f32_1", tag="tab2", align_bytes=64)]
         wv_raw = x_f32[1][:, :PACK - 1, :].rearrange("p t m -> p (t m)").rearrange("p (b j n) -> p b j n", b=RP, j=PACK)
         nc.sync.dma_start(wv_raw, wv.rearrange("(b p j) n -> p b j n", p=P, j=PACK))
@@ -223,16 +228,16 @@ def tile_list_dialogue_reply_ranker_kernel(tc, tab_words, tab_scales, offs, offs
         def gelu_half(i, h):
             b, t = divmod(i, PACK)
             if (i, h) == (last, 1):
-                ge = first.tile([P, HALF], F32, name="ge_right", align_bytes=64, offset=late_bytes)[:]
+                ge = second.tile([P, HALF], F32, name="ge_right", align_bytes=64, offset=late_bytes)[:]
             else:
                 ge = ring.tile([P, HALF], F32, name="ge", bufs=3)[:]
             nc.scalar.activation(ge, x_f32[b][:, t, cols(h)], ACT.Gelu_apprx_tanh, scale=gin_t[:, b, t:t + 1])
             dst = z_bf[b, h][:, :, t] if i == last else z_rows[b][:, t, cols(h)]
             nc.scalar.activation(dst, ge, ACT.Copy, scale=gout_t[:, b, t:t + 1])
 
-        def weave(copy, dst, src, b, h, t0=0, t1=PACK):
-            copy(dst[b, h][:, :, t0:t1].rearrange("p (c i) t -> p c t i", i=4),
-                 src[b][:, t0:t1, cols(h)].rearrange("p t (c i) -> p c t i", i=4))
+        def weave(copy, dst, src, b, h, t0=0, t1=PACK, part=slice(0, HALF)):
+            copy(dst[b, h][:, part, t0:t1].rearrange("p (c i) t -> p c t i", i=4),
+                 src[b][:, t0:t1, cols(h)][:, :, part].rearrange("p t (c i) -> p c t i", i=4))
 
         x_codes = {}
         z_codes = {}
@@ -343,20 +348,21 @@ def tile_list_dialogue_reply_ranker_kernel(tc, tab_words, tab_scales, offs, offs
         ge_second = keep.tile([P, HALF // 2], F32, tag="codes11", align_bytes=64)
         late_words = 2 * HALF + 2 * P
         late_bytes = 4 * late_words
-        ge_front = first.tile([P, HALF // 2], F32, align_bytes=64, offset=late_bytes - HALF)
+        ge_front = second.tile([P, HALF // 2], F32, align_bytes=64, offset=late_bytes - HALF)
         ge_left = (ge_front[:], ge_second[:])
         for part, ge in zip(quarters, ge_left):
             nc.scalar.activation(ge, x_f32[1][:, PACK - 1, part], ACT.Gelu_apprx_tanh,
                                  scale=gin_t[:, 1, PACK - 1:PACK])
+        weave(nc.scalar.copy, x_bf, x_f32, 1, 0, 2, PACK, quarters[0])
         for part, ge in zip(quarters, ge_left):
             nc.scalar.activation(z_bf[1, 0][:, part, PACK - 1], ge, ACT.Copy,
                                  scale=gout_t[:, 1, PACK - 1:PACK])
         gelu_half(last, 1)
         code_tiles(keep, 1, 1, "codes11")
-        weave(nc.vector.tensor_copy, x_bf, x_f32, 1, 0, 2, PACK)
+        weave(nc.vector.tensor_copy, x_bf, x_f32, 1, 0, 2, PACK, quarters[1])
         quantize(x_codes, x_sc, x_bf, 0, 1)
         quantize(x_codes, x_sc, x_bf, 1, 0)
-        late_codes = first.tile([P, late_words], U32, align_bytes=64, offset=0)
+        late_codes = second.tile([P, late_words], U32, align_bytes=64, offset=0)
         for h in range(2):
             z_codes[0, h] = late_codes[:, cols(h)]
             quantize(z_codes, z_sc, z_bf, 0, h)
@@ -378,7 +384,7 @@ def tile_list_dialogue_reply_ranker_kernel(tc, tab_words, tab_scales, offs, offs
             gate[n, 1] = bank(6 + n)
             gate_pass(gate[n, 1], n, 0, 1)
 
-        th_all = first.tile([P, 2, NT, HALF], F32, align_bytes=64, offset=late_bytes)
+        th_all = second.tile([P, 2, NT, HALF], F32, align_bytes=64, offset=late_bytes)
         th = {}
 
         def squash(n, h):

@@ -59,22 +59,18 @@ def tile_list_dialogue_reply_ranker_kernel(tc, tab_words, tab_scales, offs, offs
         def fetch_table(a, dst, offsets):
             nc.vector.tensor_copy(dst, tabs[a][:].bitcast(U32).indirect(offsets))
 
-        row_first = (32, 48, 112)
+        row_first = (48, 64, 80)
 
         def load_scale_rows(tile, scales):
             rows = scales.rearrange("a q c -> (a q) c").bitcast(I32)
-            nc.sync.dma_start(tile[32:64, :].bitcast(I32), rows[0:32, :])
-            nc.sync.dma_start(tile[112:128, :].bitcast(I32), rows[32:48, :])
-            nc.vector.memset(tile[0:32, :].bitcast(I32), 0)
-            nc.vector.memset(tile[64:112, :].bitcast(I32), 0)
+            nc.sync.dma_start(tile[48:96, :].bitcast(I32), rows)
+            nc.vector.memset(tile[0:48, :].bitcast(I32), 0)
+            nc.vector.memset(tile[96:128, :].bitcast(I32), 0)
 
-        def move_scale_rows(queues, dst, src):
-            for a in range(KP):
-                for q in range(QUADS):
-                    first = row_first[a] + 4 * q
-                    queue = queues[(QUADS * a + q) * len(queues) // (KP * QUADS)]
-                    queue.dma_start(dst[32 * q:32 * q + 4, a, :].bitcast(I32),
-                                    src[first:first + 4, :].bitcast(I32))
+        def move_scale_rows(queue, plane, src, a, quads):
+            for q in quads:
+                row = row_first[a] + 4 * q
+                queue.dma_start(plane[32 * q:32 * q + 4, :].bitcast(I32), src[row:row + 4, :].bitcast(I32))
 
         w4s_raw = keep.tile([P, H], U8, align_bytes=64)
         ts_got = keep.tile([P, S], U8, tag="w4", align_bytes=64)
@@ -84,20 +80,25 @@ def tile_list_dialogue_reply_ranker_kernel(tc, tab_words, tab_scales, offs, offs
         w4_raw = keep.tile([P, KP, 2 * HALF], U8, tag="tab2", align_bytes=64)
         with tc.tile_pool(name="early", bufs=1) as early:
             ts_win = early.tile([P, T], U8, align_bytes=64)
-            load_scale_rows(ts_win, tab_scales)
-            load_scale_rows(w4s_raw, w4_scales)
             w4_rows = w4_words.rearrange("a p c -> p a c")
             nc.sync.dma_start(w4_raw[:].bitcast(I32), w4_rows[:, :, :2 * HALF].bitcast(I32))
+            load_scale_rows(ts_win, tab_scales)
+            load_scale_rows(w4s_raw, w4_scales)
             load_table(first, 0, offset=0)
             nc.sync.dma_start(list2[:], offs2)
             nc.sync.dma_start(list3[:], offs3)
             load_table(early, 1)
             nc.gpsimd.memset(planes[:].bitcast(I32), 0)
+            late_planes = [keep.tile([P, H - EARLY], U8, name="late_plane0", align_bytes=64)]
+            nc.gpsimd.memset(late_planes[0][:].bitcast(I32), 0)
             nc.vector.tensor_copy(ts_got[:], ts_win[:].indirect(list1[:]))
             as_given = w4s_raw[:].rearrange("p (b m t) -> p b t m", b=RP, t=PACK)
             nc.vector.tensor_copy(scale_rows[:, S:].rearrange("p (t m) -> p t m", m=P), as_given[:, 0, :EARLY // P])
             nc.vector.tensor_copy(scale_rows[:, :S].bitcast(I32), ts_got[:].bitcast(I32))
-            move_scale_rows((nc.scalar, nc.gpsimd), planes, scale_rows)
+            move_scale_rows(nc.scalar, planes[:, 0, :], scale_rows, 0, (0, 2, 1, 3))
+            move_scale_rows(nc.scalar, planes[:, 1, :], scale_rows, 1, (0, 2))
+            move_scale_rows(nc.gpsimd, planes[:, 1, :], scale_rows, 1, (1, 3))
+            move_scale_rows(nc.gpsimd, planes[:, 2, :], scale_rows, 2, (0, 2, 1, 3))
             w4_first = keep.tile([P, KP, 2 * HALF], U8, tag="w4", align_bytes=64)
             nc.vector.tensor_copy(w4_first[:].bitcast(U16).rearrange("p a (t c i) -> p a c t i", t=PACK, i=8),
                                   w4_raw[:].bitcast(U16).rearrange("p a (c i t) -> p a c t i", t=PACK, i=8))
@@ -131,26 +132,36 @@ def tile_list_dialogue_reply_ranker_kernel(tc, tab_words, tab_scales, offs, offs
         gin_t = held.tile([P, RP, PACK], F32)
         gout_t = held.tile([P, RP, PACK], F32)
 
-        def load_weights(t, part):
-            for q in (0, 2, 1, 3):
+        def load_weights(t, part, quads=(0, 2, 1, 3)):
+            for q in quads:
                 nc.sync.dma_start(weights[t][32 * q:32 * q + 32, part], wgs_rows[:, t, part])
 
         first_parts = (slice(0, S // 4), slice(S // 4, S))
         load_weights(0, first_parts[0])
         load_page(0)
         load_weights(0, slice(S // 4, S))
-        for t in range(1, PACK):
-            load_page(t)
-            load_weights(t, slice(0, S))
-            if t == 1:
-                w4_late = held.tile([P, KP, 2 * HALF], U8, align_bytes=64)
-                nc.sync.dma_start(w4_late[:].bitcast(I32), w4_rows[:, :, 2 * HALF:].bitcast(I32))
-                late_planes = held.tile([P, KP, H - EARLY], U8, align_bytes=64)
-                nc.gpsimd.memset(late_planes[:].bitcast(I32), 0)
-                move_scale_rows((nc.sync,), late_planes, late_rows)
-            if t == PACK - 1:
-                nc.sync.dma_start(gin_t[:], gin.rearrange("(b p t) -> p b t", p=P, t=PACK))
-                nc.sync.dma_start(gout_t[:], gout.rearrange("(b p t) -> p b t", p=P, t=PACK))
+        for a in range(1, KP):
+            late_planes.append(held.tile([P, H - EARLY], U8, name="late_plane%d" % a, align_bytes=64))
+            nc.gpsimd.memset(late_planes[a][:].bitcast(I32), 0)
+
+        def move_late(a):
+            move_scale_rows(nc.sync, late_planes[a], late_rows, a, (0, 2, 1, 3))
+
+        whole = slice(0, S)
+        move_late(0)
+        load_page(1)
+        load_weights(1, whole, (0, 2))
+        move_late(1)
+        load_weights(1, whole, (1, 3))
+        load_page(2)
+        move_late(2)
+        load_weights(2, whole)
+        load_page(3)
+        load_weights(3, whole)
+        nc.sync.dma_start(gin_t[:], gin.rearrange("(b p t) -> p b t", p=P, t=PACK))
+        nc.sync.dma_start(gout_t[:], gout.rearrange("(b p t) -> p b t", p=P, t=PACK))
+        w4_late = held.tile([P, KP, 2 * HALF], U8, align_bytes=64)
+        nc.sync.dma_start(w4_late[:].bitcast(I32), w4_rows[:, :, 2 * HALF:].bitcast(I32))
 
         x_f32 = [second.tile([P, PACK, M], F32, name="x_f32_0", align_bytes=64, offset=0),
                  keep.tile([P, PACK, M], F32, name="x_f32_1", tag="tab2", align_bytes=64)]
@@ -184,7 +195,7 @@ def tile_list_dialogue_reply_ranker_kernel(tc, tab_words, tab_scales, offs, offs
                         out=acc[:],
                         lhsT=w4_codes[i][:, a].bitcast(FP4X4),
                         lhsT_scale=(planes[:, a, S + P * i:S + P * (i + 1)] if P * i < EARLY
-                                    else late_planes[:, a, P * i - EARLY:P * (i + 1) - EARLY]),
+                                    else late_planes[a][:, P * i - EARLY:P * (i + 1) - EARLY]),
                         rhs=v_codes[a][:, cols(h)].bitcast(FP8X4),
                         rhs_scale=planes[:, a, cols(h)],
                         start=(a == 0), stop=(a == KP - 1))

@@ -186,8 +186,8 @@ def tile_list_dialogue_reply_ranker_kernel(tc, tab_words, tab_scales, offs, offs
             b, t = divmod(i, PACK)
             if b == 1:
                 w4_codes[i] = keep.tile([P, KP, 2 * P], U8, name="w4_slice", tag="staged%d" % (t + 1), align_bytes=64)[:]
-                nc.gpsimd.tensor_copy(w4_codes[i].rearrange("p a (m e) -> p a m e", e=2),
-                                      w4_late[:].rearrange("p a (m t e) -> p a t m e", t=PACK, e=2)[:, :, t])
+                nc.scalar.copy(w4_codes[i].bitcast(U16),
+                               w4_late[:].bitcast(U16).rearrange("p a (m t) -> p a t m", t=PACK)[:, :, t])
             for h in range(2):
                 acc = bank((4 if i > 0 and i % 2 == 0 else 6) + h)
                 for a in range(KP):

@@ -20,410 +20,346 @@ P = 128
 PACK = 4
 KP = K // (P * PACK)
 RP = H // (P * PACK)
+SLICES = RP * PACK
 HALF = 512
+QUARTER = 256
 NT = N // P
-QUADS = 4
+QUADS = (0, 2, 1, 3)
 EARLY = 2 * P
+LATE = H - EARLY
+ROWS0 = 48
+KB = 1024
+
+AT_TAB = 0
+AT_PAGE0 = 48 * KB
+AT_WGS = 56 * KB
+AT_V = 72 * KB
+AT_PLANES = 84 * KB
+AT_LATE = 88 * KB
+AT_W4 = 91 * KB
+AT_XBF = 97 * KB
+AT_ZBF = 113 * KB
+AT_ZROWS = 129 * KB
+AT_X = 145 * KB
+AT_STAGED = 177 * KB
+AT_WV = 189 * KB
+AT_WVBF = 201 * KB
+AT_W8 = 207 * KB
+AT_SC = 210 * KB
+AT_HEAD = 216 * KB
+AT_GAINS = 231 * KB
 
 
 def tile_list_dialogue_reply_ranker_kernel(tc, tab_words, tab_scales, offs, offs2, offs3, w4_words, w4_scales,
-                                                    w8_words, w8_scales, wv, page0, wgs, gin, gout, out):
+                                                        w8_words, w8_scales, wv, page0, wgs, gin, gout, out):
     nc = tc.nc
     with ExitStack() as ctx:
-        keep = ctx.enter_context(tc.tile_pool(name="keep", bufs=1))
-        first = ctx.enter_context(tc.tile_pool(name="first", bufs=1))
-        ring = ctx.enter_context(tc.tile_pool(name="ring", bufs=2))
+        lists = ctx.enter_context(tc.tile_pool(name="lists", bufs=1))
+        mem = ctx.enter_context(tc.tile_pool(name="mem", bufs=1))
         psum = ctx.enter_context(tc.psum_pool(name="psum", bufs=1))
 
-        def bank(b):
-            return psum.tile([P, HALF], F32, name="bank%d" % b)
+        def at(name, shape, dtype, offset):
+            return mem.tile(shape, dtype, name=name, align_bytes=64, offset=offset)
+
+        def bank(n):
+            return psum.tile([P, HALF], F32, name="bank%d" % n)
 
         def cols(h):
             return slice(h * HALF, (h + 1) * HALF)
 
-        def entries(lst, h):
-            return lst[:, h * HALF // 16:(h + 1) * HALF // 16]
+        def entries(lst, part):
+            return lst[:, part.start // 16:part.stop // 16]
 
-        list1 = keep.tile([P, S // 16], U16)
-        list2 = keep.tile([P, S // 16], U16)
-        list3 = keep.tile([P, M // 16], U16)
-        nc.sync.dma_start(list1[:], offs)
+        list1 = lists.tile([P, S // 16], U16)
+        list2 = lists.tile([P, S // 16], U16)
+        list3 = lists.tile([P, M // 16], U16)
 
-        tabs = []
+        tabs = [at("tab%d" % a, [P, T], I32, AT_TAB + 16 * KB * a) for a in range(KP)]
+        ts_win = at("ts_win", [P, T], U8, AT_HEAD)
+        w4s_raw = at("w4s_raw", [P, H], U8, AT_HEAD + 4 * KB)
+        ts_got = at("ts_got", [P, S], U8, AT_HEAD + 5 * KB)
+        early_rows = at("early_rows", [P, S + EARLY], U8, AT_HEAD + 6 * KB)
+        late_rows = at("late_rows", [P, LATE], U8, AT_HEAD + 8 * KB)
+        w4_raw = [at("w4_raw%d" % b, [P, KP, 2 * HALF], U8, AT_HEAD + (9 + 3 * b) * KB) for b in range(RP)]
+        w4_dealt = [at("w4_dealt%d" % b, [P, KP, 2 * HALF], U8, AT_W4 + 3 * KB * b) for b in range(RP)]
+        planes = at("planes", [P, KP, S + EARLY], U8, AT_PLANES)
+        late_planes = at("late_planes", [P, KP, LATE], U8, AT_LATE)
+        v_codes = [at("v_codes%d" % a, [P, S], U32, AT_V + 4 * KB * a) for a in range(KP)]
+        weights = [at("wgs%d" % t, [P, S], F32, AT_WGS + 4 * KB * t) for t in range(PACK)]
+        w8_sc = at("w8_sc", [P, RP, N], U8, AT_SC)
+        wv_sc = at("wv_sc", [P, RP * N], U8, AT_SC + KB)
+        x_sc = at("x_sc", [P, RP, M], U8, AT_SC + 2 * KB)
+        z_sc = at("z_sc", [P, RP, M], U8, AT_SC + 4 * KB)
 
-        def load_table(pool, a, **place):
-            tab = pool.tile([P, T], I32, name="tab%d" % a, align_bytes=64, **place)
-            nc.sync.dma_start(tab[:], tab_words[a].rearrange("p t i -> p (t i)").bitcast(I32))
-            tabs.append(tab)
-
-        def fetch_table(a, dst, offsets):
-            nc.vector.tensor_copy(dst, tabs[a][:].bitcast(U32).indirect(offsets))
-
-        row_first = (48, 64, 80)
+        def load_table(a):
+            nc.sync.dma_start(tabs[a][:], tab_words[a].rearrange("p t i -> p (t i)").bitcast(I32))
 
         def load_scale_rows(tile, scales):
-            rows = scales.rearrange("a q c -> (a q) c").bitcast(I32)
-            nc.sync.dma_start(tile[48:96, :].bitcast(I32), rows)
-            nc.vector.memset(tile[0:48, :].bitcast(I32), 0)
-            nc.vector.memset(tile[96:128, :].bitcast(I32), 0)
+            nc.scalar.dma_start(tile[ROWS0:2 * ROWS0, :].bitcast(I32), scales.rearrange("a q c -> q a c").bitcast(I32))
+            nc.vector.memset(tile[0:ROWS0, :].bitcast(I32), 0)
+            nc.vector.memset(tile[2 * ROWS0:P, :].bitcast(I32), 0)
 
-        def move_scale_rows(queue, plane, src, a, quads):
-            for q in quads:
-                row = row_first[a] + 4 * q
-                queue.dma_start(plane[32 * q:32 * q + 4, :].bitcast(I32), src[row:row + 4, :].bitcast(I32))
+        def move_scale_rows(queue, dst, src):
+            for q in QUADS:
+                row = ROWS0 + 4 * KP * q
+                queue.dma_start(dst[32 * q:32 * q + 4].rearrange("p a c -> p (a c)").bitcast(I32),
+                                src[row:row + 4 * KP, :].bitcast(I32))
 
-        w4s_raw = keep.tile([P, H], U8, align_bytes=64)
-        ts_got = keep.tile([P, S], U8, tag="w4", align_bytes=64)
-        scale_rows = keep.tile([P, S + EARLY], U8, align_bytes=64)
-        planes = keep.tile([P, KP, S + EARLY], U8, align_bytes=64)
-        v_codes = [keep.tile([P, S], U32, name="v_codes%d" % a, align_bytes=64) for a in range(KP)]
-        w4_raw = keep.tile([P, KP, 2 * HALF], U8, tag="tab2", align_bytes=64)
-        with tc.tile_pool(name="early", bufs=1) as early:
-            ts_win = early.tile([P, T], U8, align_bytes=64)
-            w4_rows = w4_words.rearrange("a p c -> p a c")
-            nc.sync.dma_start(w4_raw[:].bitcast(I32), w4_rows[:, :, :2 * HALF].bitcast(I32))
-            load_scale_rows(ts_win, tab_scales)
-            load_scale_rows(w4s_raw, w4_scales)
-            load_table(first, 0, offset=0)
-            nc.sync.dma_start(list2[:], offs2)
-            nc.sync.dma_start(list3[:], offs3)
-            load_table(early, 1)
-            nc.gpsimd.memset(planes[:].bitcast(I32), 0)
-            late_planes = [keep.tile([P, H - EARLY], U8, name="late_plane0", align_bytes=64)]
-            nc.gpsimd.memset(late_planes[0][:].bitcast(I32), 0)
-            nc.vector.tensor_copy(ts_got[:], ts_win[:].indirect(list1[:]))
-            as_given = w4s_raw[:].rearrange("p (b m t) -> p b t m", b=RP, t=PACK)
-            nc.vector.tensor_copy(scale_rows[:, S:].rearrange("p (t m) -> p t m", m=P), as_given[:, 0, :EARLY // P])
-            nc.vector.tensor_copy(scale_rows[:, :S].bitcast(I32), ts_got[:].bitcast(I32))
-            move_scale_rows(nc.scalar, planes[:, 0, :], scale_rows, 0, (0, 2, 1, 3))
-            move_scale_rows(nc.scalar, planes[:, 1, :], scale_rows, 1, (0, 2))
-            move_scale_rows(nc.gpsimd, planes[:, 1, :], scale_rows, 1, (1, 3))
-            move_scale_rows(nc.gpsimd, planes[:, 2, :], scale_rows, 2, (0, 2, 1, 3))
-            w4_first = keep.tile([P, KP, 2 * HALF], U8, tag="w4", align_bytes=64)
-            nc.vector.tensor_copy(w4_first[:].bitcast(U16).rearrange("p a (t c i) -> p a c t i", t=PACK, i=8),
-                                  w4_raw[:].bitcast(U16).rearrange("p a (c i t) -> p a c t i", t=PACK, i=8))
-            w4_codes = {t: w4_first[:, :, 2 * P * t:2 * P * (t + 1)] for t in range(PACK)}
-            load_table(keep, KP - 1)
-            fetch_table(0, v_codes[0][:], list1[:])
-            late_rows = keep.tile([P, H - EARLY], U8, align_bytes=64)
-            by_slice = late_rows[:].rearrange("p (t m) -> p t m", m=P)
-            nc.vector.tensor_copy(by_slice[:, :PACK - EARLY // P], as_given[:, 0, EARLY // P:])
-            nc.vector.tensor_copy(by_slice[:, PACK - EARLY // P:], as_given[:, 1])
-            fetch_table(1, v_codes[1][:], list1[:])
-        second = ctx.enter_context(tc.tile_pool(name="second", bufs=1))
-        held = ctx.enter_context(tc.tile_pool(name="held", bufs=1))
-        for h in range(2):
-            fetch_table(KP - 1, v_codes[KP - 1][:, cols(h)], entries(list1, h))
+        w4_rows = w4_words.rearrange("a p c -> p a c")
+
+        def load_w4(queue, b):
+            queue.dma_start(w4_raw[b][:].bitcast(I32), w4_rows[:, :, 2 * HALF * b:2 * HALF * (b + 1)].bitcast(I32))
+
+        def deal_w4(b):
+            nc.scalar.copy(w4_dealt[b][:].bitcast(U16).rearrange("p a (t c i) -> p a c t i", t=PACK, i=8),
+                           w4_raw[b][:].bitcast(U16).rearrange("p a (c i t) -> p a c t i", t=PACK, i=8))
+
+        wgs_rows = wgs.rearrange("(q t) j -> q t j", t=PACK)
+
+        def load_weights(queue, t, part):
+            for q in QUADS:
+                queue.dma_start(weights[t][32 * q:32 * q + 32, part], wgs_rows[:, t, part])
 
         page_rows = page0.rearrange("(b p t) c -> b t p c", p=P, t=PACK)
         pages = {}
-        page_tag = ["page%d" % k for k in (0, 1, 2, 3, 0, 2, 3, 0)]
 
         def load_page(i):
-            if page_tag[i] == page_tag[0]:
-                pages[i] = first.tile([P, T2], F32, name="page%d" % i, tag=page_tag[i], align_bytes=64, offset=0)
-            else:
-                pages[i] = held.tile([P, T2], F32, name="page%d" % i, tag=page_tag[i], align_bytes=64)
+            offset = AT_PAGE0 if i % (SLICES - 1) == 0 else AT_TAB + 8 * KB * (i - 1)
+            pages[i] = at("page%d" % i, [P, T2], F32, offset)
             nc.sync.dma_start(pages[i][:], page_rows[i // PACK, i % PACK])
 
-        wgs_rows = wgs.rearrange("(q t) j -> q t j", t=PACK)
-        weights = [first.tile([P, S], F32, name="wgs0", align_bytes=64, offset=4 * T2)]
-        weights.extend(held.tile([P, S], F32, name="wgs%d" % t, align_bytes=64) for t in range(1, PACK))
-        gin_t = held.tile([P, RP, PACK], F32)
-        gout_t = held.tile([P, RP, PACK], F32)
-
-        def load_weights(t, part, quads=(0, 2, 1, 3)):
-            for q in quads:
-                nc.sync.dma_start(weights[t][32 * q:32 * q + 32, part], wgs_rows[:, t, part])
-
-        first_parts = (slice(0, S // 4), slice(S // 4, S))
-        load_weights(0, first_parts[0])
+        first, rest = slice(0, QUARTER), slice(QUARTER, S)
+        nc.sync.dma_start(list1[:], offs)
+        load_table(0)
+        load_scale_rows(ts_win, tab_scales)
+        load_scale_rows(w4s_raw, w4_scales)
+        load_w4(nc.scalar, 0)
+        load_weights(nc.gpsimd, 0, first)
+        load_table(1)
+        nc.sync.dma_start(list2[:], offs2)
+        load_table(2)
         load_page(0)
-        load_weights(0, slice(S // 4, S))
-        for a in range(1, KP):
-            late_planes.append(held.tile([P, H - EARLY], U8, name="late_plane%d" % a, align_bytes=64))
-            nc.gpsimd.memset(late_planes[a][:].bitcast(I32), 0)
+        load_weights(nc.sync, 0, rest)
+        nc.vector.memset(planes[:].bitcast(I32), 0)
+        nc.vector.memset(late_planes[:].bitcast(I32), 0)
+        nc.vector.memset(w8_sc[:].bitcast(I32), 0)
 
-        def move_late(a):
-            move_scale_rows(nc.sync, late_planes[a], late_rows, a, (0, 2, 1, 3))
+        nc.vector.tensor_copy(ts_got[:], ts_win[:].indirect(list1[:]))
+        as_given = w4s_raw[:].rearrange("p (b m t) -> p b t m", b=RP, t=PACK)
+        nc.vector.tensor_copy(early_rows[:, S:].rearrange("p (t m) -> p t m", m=P), as_given[:, 0, :EARLY // P])
+        nc.vector.tensor_copy(early_rows[:, :S].bitcast(I32), ts_got[:].bitcast(I32))
+        move_scale_rows(nc.gpsimd, planes, early_rows)
+        by_slice = late_rows[:].rearrange("p (t m) -> p t m", m=P)
+        nc.vector.tensor_copy(by_slice[:, :PACK - EARLY // P], as_given[:, 0, EARLY // P:])
+        nc.vector.tensor_copy(by_slice[:, PACK - EARLY // P:], as_given[:, 1])
+        deal_w4(0)
+
+        first_parts = (first, slice(QUARTER, HALF), cols(1))
+        for a in range(KP - 1):
+            nc.vector.tensor_copy(v_codes[a][:], tabs[a][:].bitcast(U32).indirect(list1[:]))
+        for part in first_parts:
+            nc.vector.tensor_copy(v_codes[KP - 1][:, part], tabs[KP - 1][:].bitcast(U32).indirect(entries(list1, part)))
+
+        gin_t = at("gin_t", [P, RP, PACK], F32, AT_GAINS)
+        gout_t = at("gout_t", [P, RP, PACK], F32, AT_GAINS + 64)
 
         whole = slice(0, S)
-        move_late(0)
-        load_page(1)
-        load_weights(1, whole, (0, 2))
-        move_late(1)
-        load_weights(1, whole, (1, 3))
-        load_page(2)
-        move_late(2)
-        load_weights(2, whole)
-        load_page(3)
-        load_weights(3, whole)
-        nc.sync.dma_start(gin_t[:], gin.rearrange("(b p t) -> p b t", p=P, t=PACK))
-        nc.sync.dma_start(gout_t[:], gout.rearrange("(b p t) -> p b t", p=P, t=PACK))
-        w4_late = held.tile([P, KP, 2 * HALF], U8, align_bytes=64)
-        nc.sync.dma_start(w4_late[:].bitcast(I32), w4_rows[:, :, 2 * HALF:].bitcast(I32))
+        wv_raw = at("wv_raw", [P, RP, PACK, N], F32, AT_WV)
+        w8_codes = at("w8_codes", [P, RP, N], U32, AT_W8)
+        move_scale_rows(nc.sync, late_planes, late_rows)
+        nc.sync.dma_start(list3[:], offs3)
+        for i in range(1, SLICES - 1):
+            load_page(i)
+            if i < PACK:
+                load_weights(nc.sync, i, whole)
+            if i == 1:
+                nc.sync.dma_start(gin_t[:], gin.rearrange("(b p t) -> p b t", p=P, t=PACK))
+            if i == 2:
+                load_w4(nc.sync, 1)
+            if i == PACK - 1:
+                nc.sync.dma_start(gout_t[:], gout.rearrange("(b p t) -> p b t", p=P, t=PACK))
+            if i == PACK:
+                nc.sync.dma_start(wv_raw[:], wv.rearrange("(b p j) n -> p b j n", p=P, j=PACK))
 
-        x_f32 = [second.tile([P, PACK, M], F32, name="x_f32_0", align_bytes=64, offset=0),
-                 keep.tile([P, PACK, M], F32, name="x_f32_1", tag="tab2", align_bytes=64)]
-        wv_raw = x_f32[1][:, :PACK - 1, :].rearrange("p t m -> p (t m)").rearrange("p (b j n) -> p b j n", b=RP, j=PACK)
-        nc.sync.dma_start(wv_raw, wv.rearrange("(b p j) n -> p b j n", p=P, j=PACK))
-        w8_sc = held.tile([P, RP, N], U8, align_bytes=64)
-        nc.gpsimd.memset(w8_sc[:].bitcast(I32), 0)
-
-        def load_w8():
-            w8_codes = keep.tile([P, RP, N], U32, tag="staged5", align_bytes=64)
-            nc.sync.dma_start(w8_codes[:].bitcast(I32), w8_words.rearrange("b p c i -> p b (c i)").bitcast(I32))
-            for q in range(QUADS):
-                nc.sync.dma_start(w8_sc[32 * q:32 * q + 4, :, :].bitcast(I32),
-                                  w8_scales[:, 4 * q:4 * q + 4, :].rearrange("b r c -> r b c").bitcast(I32))
-            return w8_codes
-
-        staged = [keep.tile([P, S], F32, name="staged%d" % i, align_bytes=64) for i in range(RP * PACK)]
-        middle = slice(S // 4, 3 * S // 4)
-        quarters = (slice(0, HALF // 2), slice(HALF // 2, HALF))
-
-        def project(i):
-            b, t = divmod(i, PACK)
-            if b == 1:
-                w4_codes[i] = keep.tile([P, KP, 2 * P], U8, name="w4_slice", tag="staged%d" % (t + 1), align_bytes=64)[:]
-                nc.scalar.copy(w4_codes[i].bitcast(U16),
-                               w4_late[:].bitcast(U16).rearrange("p a (m t) -> p a t m", t=PACK)[:, :, t])
-            for h in range(2):
-                acc = bank((4 if i > 0 and i % 2 == 0 else 6) + h)
-                for a in range(KP):
-                    nc.tensor.matmul_mx(
-                        out=acc[:],
-                        lhsT=w4_codes[i][:, a].bitcast(FP4X4),
-                        lhsT_scale=(planes[:, a, S + P * i:S + P * (i + 1)] if P * i < EARLY
-                                    else late_planes[a][:, P * i - EARLY:P * (i + 1) - EARLY]),
-                        rhs=v_codes[a][:, cols(h)].bitcast(FP8X4),
-                        rhs_scale=planes[:, a, cols(h)],
-                        start=(a == 0), stop=(a == KP - 1))
-                nc.scalar.copy(staged[i][:, cols(h)], acc[:])
-
-        def scatter(i):
-            t = i % PACK
-            weight = weights[t][:]
-            if i == 0:
-                for part in first_parts:
-                    nc.vector.tensor_tensor(pages[i][:].indirect(list2[:, part.start // 16:part.stop // 16]),
-                                            staged[i][:, part], weight[:, part], ALU.mult)
-            else:
-                nc.vector.tensor_tensor(pages[i][:].indirect(list2[:]), staged[i][:], weight, ALU.mult)
-
-        def fetch(i):
-            b, t = divmod(i, PACK)
-            if i == RP * PACK - 1:
-                for part in quarters + (cols(1),):
-                    nc.vector.tensor_copy(x_f32[b][:, t, part],
-                                          pages[i][:].indirect(list3[:, part.start // 16:part.stop // 16]))
-            else:
-                nc.vector.tensor_copy(x_f32[b][:, t, :], pages[i][:].indirect(list3[:]))
-
+        x_f32 = [at("x_f32_%d" % b, [P, PACK, M], F32, AT_X + 16 * KB * b) for b in range(RP)]
+        z_rows = [at("z_rows%d" % b, [P, PACK, M], BF16, AT_ZROWS + 8 * KB * b) for b in range(RP)]
         x_bf = {}
         z_bf = {}
         for b in range(RP):
             for h in range(2):
-                x_bf[b, h] = keep.tile([P, HALF, PACK], BF16, name="x_bf%d%d" % (b, h), align_bytes=64)
-                z_bf[b, h] = keep.tile([P, HALF, PACK], BF16, name="z_bf%d%d" % (b, h), align_bytes=64)
+                x_bf[b, h] = at("x_bf%d%d" % (b, h), [P, HALF, PACK], BF16, AT_XBF + 4 * KB * (2 * b + h))
+                z_bf[b, h] = at("z_bf%d%d" % (b, h), [P, HALF, PACK], BF16, AT_ZBF + 4 * KB * (2 * b + h))
+        staged = {}
 
-        z_rows = [keep.tile([P, PACK, M], BF16, name="z_rows%d" % b, align_bytes=64) for b in range(RP)]
+        def staged_at(i):
+            return AT_STAGED + 4 * KB * (i % 3)
 
-        def gelu_parts(i, parts):
+        def x_row(i):
+            return x_f32[i // PACK][:, i % PACK]
+
+        def project(i):
             b, t = divmod(i, PACK)
-            for part, ge in parts:
-                nc.scalar.activation(ge, x_f32[b][:, t, part], ACT.Gelu_apprx_tanh, scale=gin_t[:, b, t:t + 1])
-            for part, ge in parts:
-                nc.scalar.activation(z_rows[b][:, t, part], ge, ACT.Copy, scale=gout_t[:, b, t:t + 1])
-
-        def gelu_half(i, h):
-            b, t = divmod(i, PACK)
-            if (i, h) == (last, 1):
-                ge = second.tile([P, HALF], F32, name="ge_right", align_bytes=64, offset=late_bytes)[:]
+            staged[i] = at("staged%d" % i, [P, S], F32, staged_at(i))
+            if i == 0:
+                groups = zip(first_parts, (7, 6, 5))
             else:
-                ge = ring.tile([P, HALF], F32, name="ge", bufs=3)[:]
-            nc.scalar.activation(ge, x_f32[b][:, t, cols(h)], ACT.Gelu_apprx_tanh, scale=gin_t[:, b, t:t + 1])
-            dst = z_bf[b, h][:, :, t] if i == last else z_rows[b][:, t, cols(h)]
+                groups = zip((cols(0), cols(1)), (6, 7) if i % 2 else (4, 5))
+            for part, n in groups:
+                acc = bank(n)
+                width = part.stop - part.start
+                for a in range(KP):
+                    nc.tensor.matmul_mx(
+                        out=acc[:, :width],
+                        lhsT=w4_dealt[b][:, a, 2 * P * t:2 * P * (t + 1)].bitcast(FP4X4),
+                        lhsT_scale=(planes[:, a, S + P * i:S + P * (i + 1)] if P * i < EARLY
+                                    else late_planes[:, a, P * i - EARLY:P * (i + 1) - EARLY]),
+                        rhs=v_codes[a][:, part].bitcast(FP8X4),
+                        rhs_scale=planes[:, a, part],
+                        start=(a == 0), stop=(a == KP - 1))
+                nc.scalar.copy(staged[i][:, part], acc[:, :width])
+
+        def scatter(i):
+            for part in (first, rest) if i == 0 else (whole,):
+                nc.vector.tensor_tensor(pages[i][:].indirect(entries(list2, part)), staged[i][:, part],
+                                        weights[i % PACK][:, part], ALU.mult)
+
+        def fetch(i, part):
+            nc.vector.tensor_copy(x_row(i)[:, part], pages[i][:].indirect(entries(list3, part)))
+
+        def gelu(i, part, ge):
+            b, t = divmod(i, PACK)
+            nc.scalar.activation(ge, x_row(i)[:, part], ACT.Gelu_apprx_tanh, scale=gin_t[:, b, t:t + 1])
+
+        def gain(i, dst, ge):
+            b, t = divmod(i, PACK)
             nc.scalar.activation(dst, ge, ACT.Copy, scale=gout_t[:, b, t:t + 1])
 
-        def weave(copy, dst, src, b, h, t0=0, t1=PACK, part=slice(0, HALF)):
+        def make_z(i):
+            b, t = divmod(i, PACK)
+            if i < SLICES - 3:
+                parked = at("parked%d" % i, [P, HALF], F32, staged_at(i + 3))
+                parts = [(cols(0), x_row(i + 1)[:, cols(0)]), (cols(1), parked[:])]
+                if i == 2:
+                    ahead = at("ahead_of_wv", [P, QUARTER], F32, AT_WVBF)
+                    parts = [parts[0], (slice(HALF, HALF + QUARTER), parked[:, :QUARTER]), (slice(HALF + QUARTER, M), ahead[:])]
+            else:
+                parts = [(slice(QUARTER * k, QUARTER * (k + 1)),
+                          x_row(i + 1 + k % 2)[:, HALF * (k // 2):HALF * (k // 2) + QUARTER]) for k in range(4)]
+            for part, ge in parts:
+                gelu(i, part, ge)
+            for k, (part, ge) in enumerate(parts):
+                gain(i, z_bf[b, k][:, :, 0] if i == PACK else z_rows[b][:, t, part], ge)
+
+        def weave(copy, dst, src, b, h, t0, t1, part=slice(0, HALF)):
             copy(dst[b, h][:, part, t0:t1].rearrange("p (c i) t -> p c t i", i=4),
                  src[b][:, t0:t1, cols(h)][:, :, part].rearrange("p t (c i) -> p c t i", i=4))
 
-        x_codes = {}
-        z_codes = {}
-        x_sc = keep.tile([P, RP, M], U8, align_bytes=64)
-        z_sc = keep.tile([P, RP, M], U8, align_bytes=64)
-
-        def quantize(codes, scales, src, b, h):
-            nc.vector.quantize_mx(out=codes[b, h].bitcast(FP8X4), scales=scales[:, b, cols(h)],
-                                  in_=src[b, h][:].rearrange("p m t -> p (m t)"))
-
-        wv_bf = keep.tile([P, RP * N * PACK], BF16, tag="spare", align_bytes=64)
-        wv_q = {}
-        wv_sc = keep.tile([P, RP * N], U8, align_bytes=64)
-
-        def weave_wv(wv_raw, b):
+        def weave_wv(wv_bf, b):
             nc.scalar.activation(
                 wv_bf[:, b * N * PACK:(b + 1) * N * PACK].rearrange("p (c i j) -> p c j i", i=4, j=PACK),
                 wv_raw[:, b].rearrange("p j (c i) -> p c j i", i=4), ACT.Copy, scale=0.5)
 
-        def quantize_wv(k, codes):
-            wv_q[k] = codes
-            c0, c1 = 2 * P * k, 2 * P * (k + 1)
-            nc.vector.quantize_mx(out=codes.bitcast(FP8X4), scales=wv_sc[:, c0:c1],
-                                  in_=wv_bf[:, PACK * c0:PACK * c1])
-
-        def gate_pass(acc, n, b, h):
-            nc.tensor.matmul_mx(out=acc[:], lhsT=w8_codes[:, b, P * n:P * (n + 1)].bitcast(FP8X4),
-                                lhsT_scale=w8_sc[:, b, P * n:P * (n + 1)],
-                                rhs=x_codes[b, h].bitcast(FP8X4), rhs_scale=x_sc[:, b, cols(h)],
-                                start=(b == 0), stop=(b == RP - 1))
-
-        def value_pass(acc, n, b, h):
-            c0 = b * N + P * n
-            nc.tensor.matmul_mx(out=acc[:], lhsT=wv_q[c0 // (2 * P)][:, c0 % (2 * P):c0 % (2 * P) + P].bitcast(FP8X4), lhsT_scale=wv_sc[:, c0:c0 + P],
-                                rhs=z_codes[b, h].bitcast(FP8X4), rhs_scale=z_sc[:, b, cols(h)],
-                                start=(b == 0), stop=(b == RP - 1))
-
-        last = RP * PACK - 1
         project(0)
         project(1)
         scatter(0)
         project(2)
-        fetch(0)
-        load_page(4)
+        fetch(0, whole)
+        load_page(SLICES - 1)
+        nc.sync.dma_start(w8_codes[:].bitcast(I32), w8_words.rearrange("b p c i -> p b (c i)").bitcast(I32))
+        for q in QUADS:
+            nc.sync.dma_start(w8_sc[32 * q:32 * q + 4, :, :].bitcast(I32),
+                              w8_scales[:, 4 * q:4 * q + 4, :].rearrange("b r c -> r b c").bitcast(I32))
         scatter(1)
-        for i in range(2):
-            if i == 1:
-                scatter(2)
-                fetch(1)
-            gelu_parts(i, [(cols(0), x_f32[0][:, i + 1, cols(0)]), (cols(1), staged[i + 3][:, middle])])
-            project(i + 3)
-            for h in range(2):
-                if i == 0:
-                    weave_wv(wv_raw, h)
-                else:
-                    weave(nc.scalar.copy, x_bf, x_f32, 0, h, 0, 2)
-        scatter(3)
-        fetch(2)
-        load_page(5)
-        gelu_parts(2, [(quarters[0], x_f32[0][:, 3, quarters[0]]), (quarters[1], x_f32[1][:, 0, quarters[0]]),
-                       (cols(1), staged[5][:, middle])])
-        project(5)
-        for h in range(2):
-            weave(nc.scalar.copy, z_bf, z_rows, 0, h, 0, 2)
-        scatter(4)
-        fetch(3)
-        load_page(6)
-        fetch(4)
-        load_page(7)
-        for i in (3, 4):
-            ge = keep.tile([P, 2 * P], F32, name="ge%d" % i, tag="wv_part%d" % (i - 3), align_bytes=64)
-            gelu_parts(i, [(quarters[0], ge[:]), (quarters[1], x_f32[1][:, i - 2, quarters[0]]),
-                           (cols(1), staged[i + 3][:, middle])])
-            project(i + 3)
-        for h in range(2):
-            weave(nc.scalar.copy, x_bf, x_f32, 0, h, 2, PACK)
-        scatter(5)
-        w8_codes = load_w8()
-        quantize_wv(0, keep.tile([P, 2 * P], U32, name="wv_codes0", tag="wv_part0", align_bytes=64)[:])
-        fetch(5)
-        for h in range(2):
-            weave(nc.scalar.copy, z_bf, z_rows, 0, h, 2, PACK)
-        ge_first = keep.tile([P, P], F32, tag="codes00", align_bytes=64)
-        ge_last = held.tile([P, P], F32, tag=page_tag[1], align_bytes=64)
-        gelu_parts(5, [(slice(0, P), ge_first[:]), (slice(P, M - P), x_f32[1][:, 3, P:M - P]),
-                       (slice(M - P, M), ge_last[:])])
-        for h in range(2):
-            weave(nc.scalar.copy, x_bf, x_f32, 1, h, 0, 2)
-        scatter(6)
-        quantize_wv(1, keep.tile([P, 2 * P], U32, name="wv_codes1", tag="wv_part1", align_bytes=64)[:])
+        for i in range(SLICES - 2):
+            scatter(i + 2)
+            make_z(i)
+            if i == 0:
+                deal_w4(1)
+            if i + 3 < SLICES:
+                project(i + 3)
+            if i + 1 < SLICES - 2:
+                fetch(i + 1, whole)
+            if i == 2:
+                wv_bf = at("wv_bf", [P, RP * N * PACK], BF16, AT_WVBF)
+                for b in range(RP):
+                    weave_wv(wv_bf, b)
+            if i in (1, 3):
+                for h in range(2):
+                    weave(nc.scalar.copy, x_bf, x_f32, 0, h, i - 1, i + 1)
+                    weave(nc.scalar.copy, z_bf, z_rows, 0, h, i - 1, i + 1)
+            if i == PACK:
+                for h in range(2):
+                    nc.scalar.copy(x_bf[1, h][:, :, 0], x_row(i)[:, cols(h)])
 
-        def code_tiles(pool, b, h, tag):
-            both = pool.tile([P, 2, HALF], U32, name="codes%d%d" % (b, h), tag=tag, align_bytes=64)
-            x_codes[b, h] = both[:, 0, :]
-            z_codes[b, h] = both[:, 1, :]
+        pair = (SLICES - 2, SLICES - 1)
+        for h in range(2):
+            for i in pair:
+                fetch(i, cols(h))
+        at_page = lambda i: AT_TAB + 8 * KB * (i - 1)
+        x_codes = {(0, 0): at("x_codes00", [P, HALF], U32, at_page(6) + 4 * KB),
+                   (0, 1): at("x_codes01", [P, HALF], U32, at_page(6) + 6 * KB),
+                   (1, 0): at("x_codes10", [P, HALF], U32, AT_V),
+                   (1, 1): at("x_codes11", [P, HALF], U32, AT_V + 2 * KB)}
+        z_codes = {(0, 0): at("z_codes00", [P, HALF], U32, at_page(6)),
+                   (0, 1): at("z_codes01", [P, HALF], U32, at_page(6) + 2 * KB),
+                   (1, 0): at("z_codes10", [P, HALF], U32, AT_V + 4 * KB),
+                   (1, 1): at("z_codes11", [P, HALF], U32, AT_V + 6 * KB)}
+        wv_codes = at("wv_codes", [P, RP * N], U32, AT_PAGE0)
 
-        fetch(last - 1)
-        x_codes[0, 0] = keep.tile([P, HALF], U32, name="x_codes00", tag="codes00", align_bytes=64)[:]
+        def quantize(codes, scales, src, b, h):
+            nc.vector.quantize_mx(out=codes[b, h][:].bitcast(FP8X4), scales=scales[:, b, cols(h)],
+                                  in_=src[b, h][:].rearrange("p m t -> p (m t)"))
+
+        for h in range(2):
+            ge = {i: at("ge%d%d" % (i, h), [P, HALF], F32, at_page(5) + 2 * KB * (2 * h + i % 2)) for i in pair}
+            for i in pair:
+                gelu(i, cols(h), ge[i][:])
+            for i in pair:
+                gain(i, z_rows[1][:, i % PACK, cols(h)], ge[i][:])
+            if h == 0:
+                weave(nc.scalar.copy, x_bf, x_f32, 1, 0, 1, PACK)
+            weave(nc.scalar.copy, z_bf, z_rows, 1, h, 1, PACK)
+
         quantize(x_codes, x_sc, x_bf, 0, 0)
-        for h in range(2):
-            gelu_half(last - 1, h)
-            weave(nc.scalar.copy, z_bf, z_rows, 1, h, 0, PACK - 1)
-
-        scatter(last)
-        fetch(last)
-        x_codes[0, 1] = held.tile([P, HALF], U32, name="x_codes01", tag=page_tag[1], align_bytes=64)[:]
-        code_tiles(keep, 1, 0, "codes10")
-        ge_second = keep.tile([P, HALF // 2], F32, tag="codes11", align_bytes=64)
-        late_words = 2 * HALF + 2 * P
-        late_bytes = 4 * late_words
-        ge_front = second.tile([P, HALF // 2], F32, align_bytes=64, offset=late_bytes - HALF)
-        ge_left = (ge_front[:], ge_second[:])
-        for part, ge in zip(quarters, ge_left):
-            nc.scalar.activation(ge, x_f32[1][:, PACK - 1, part], ACT.Gelu_apprx_tanh,
-                                 scale=gin_t[:, 1, PACK - 1:PACK])
-        weave(nc.scalar.copy, x_bf, x_f32, 1, 0, 2, PACK, quarters[0])
-        for part, ge in zip(quarters, ge_left):
-            nc.scalar.activation(z_bf[1, 0][:, part, PACK - 1], ge, ACT.Copy,
-                                 scale=gout_t[:, 1, PACK - 1:PACK])
-        gelu_half(last, 1)
-        code_tiles(keep, 1, 1, "codes11")
-        weave(nc.vector.tensor_copy, x_bf, x_f32, 1, 0, 2, PACK, quarters[1])
+        weave(nc.vector.tensor_copy, x_bf, x_f32, 1, 1, 1, PACK)
         quantize(x_codes, x_sc, x_bf, 0, 1)
         quantize(x_codes, x_sc, x_bf, 1, 0)
-        late_codes = second.tile([P, late_words], U32, align_bytes=64, offset=0)
-        for h in range(2):
-            z_codes[0, h] = late_codes[:, cols(h)]
-            quantize(z_codes, z_sc, z_bf, 0, h)
-        quantize_wv(2, late_codes[:, 2 * HALF:])
-        weave(nc.vector.tensor_copy, x_bf, x_f32, 1, 1, 2, PACK)
-        quantize(z_codes, z_sc, z_bf, 1, 0)
         quantize(x_codes, x_sc, x_bf, 1, 1)
-        quantize(z_codes, z_sc, z_bf, 1, 1)
+        for b in range(RP):
+            nc.vector.quantize_mx(out=wv_codes[:, b * N:(b + 1) * N].bitcast(FP8X4), scales=wv_sc[:, b * N:(b + 1) * N],
+                                  in_=wv_bf[:, b * N * PACK:(b + 1) * N * PACK])
+        for b in range(RP):
+            for h in range(2):
+                quantize(z_codes, z_sc, z_bf, b, h)
 
+        def gate_pass(acc, n, b, h):
+            nc.tensor.matmul_mx(out=acc[:], lhsT=w8_codes[:, b, P * n:P * (n + 1)].bitcast(FP8X4),
+                                lhsT_scale=w8_sc[:, b, P * n:P * (n + 1)],
+                                rhs=x_codes[b, h][:].bitcast(FP8X4), rhs_scale=x_sc[:, b, cols(h)],
+                                start=(b == 0), stop=(b == RP - 1))
+
+        def value_pass(acc, n, b, h):
+            c0 = b * N + P * n
+            nc.tensor.matmul_mx(out=acc[:], lhsT=wv_codes[:, c0:c0 + P].bitcast(FP8X4), lhsT_scale=wv_sc[:, c0:c0 + P],
+                                rhs=z_codes[b, h][:].bitcast(FP8X4), rhs_scale=z_sc[:, b, cols(h)],
+                                start=(b == 0), stop=(b == RP - 1))
+
+        order = [(n, h) for h in range(2) for n in range(NT)]
         gate = {}
-        value = {}
-        for n in range(NT):
-            gate[n, 0] = bank(n)
-            gate_pass(gate[n, 0], n, 0, 0)
-        for n in range(NT):
-            value[n, 0] = bank(NT + n)
-            value_pass(value[n, 0], n, 0, 0)
-        for n in range(2):
-            gate[n, 1] = bank(6 + n)
-            gate_pass(gate[n, 1], n, 0, 1)
-
-        th_all = second.tile([P, 2, NT, HALF], F32, align_bytes=64, offset=late_bytes)
+        for k, (n, h) in enumerate(order):
+            gate[n, h] = bank(k)
+        for b in range(RP):
+            for n, h in order:
+                gate_pass(gate[n, h], n, b, h)
         th = {}
-
-        def squash(n, h):
-            th[n, h] = th_all[:, h, n, :]
-            nc.scalar.activation(th[n, h], gate[n, h][:], ACT.Tanh, scale=0.5)
-
-        def finish(n, h):
-            res = keep.tile([P, HALF], F32, name="res", tag="staged%d" % (0, 1, 2, 3, 4, 6)[NT * h + n], align_bytes=64)
-            nc.vector.scalar_tensor_tensor(out=res[:], in0=th[n, h], scalar=1.0, in1=value[n, h][:],
+        for k, (n, h) in enumerate(order):
+            th[n, h] = at("th%d" % k, [P, HALF], F32, at_page(1) + 2 * KB * k)
+            nc.scalar.activation(th[n, h][:], gate[n, h][:], ACT.Tanh, scale=0.5)
+        for k, (n, h) in enumerate(order):
+            value = bank((6 + k) % 8)
+            for b in range(RP):
+                value_pass(value, n, b, h)
+            res = at("res%d" % k, [P, HALF], F32, at_page(3) + 2 * KB * k)
+            nc.vector.scalar_tensor_tensor(out=res[:], in0=th[n, h][:], scalar=1.0, in1=value[:],
                                            op0=ALU.add, op1=ALU.mult)
             nc.sync.dma_start(out[P * n:P * (n + 1), cols(h)], res[:])
-
-        for n in range(NT):
-            gate_pass(gate[n, 0], n, 1, 0)
-            squash(n, 0)
-        for n in range(NT):
-            value_pass(value[n, 0], n, 1, 0)
-        for n in range(2):
-            gate_pass(gate[n, 1], n, 1, 1)
-        gate[2, 1] = bank(0)
-        for b in range(RP):
-            gate_pass(gate[2, 1], 2, b, 1)
-        for n in range(NT):
-            finish(n, 0)
-        for n in range(NT):
-            value[n, 1] = bank(1 + n)
-            for b in range(RP):
-                value_pass(value[n, 1], n, b, 1)
-        for n in range(NT):
-            squash(n, 1)
-            finish(n, 1)

@@ -25,26 +25,25 @@ HALF = 512
 QUARTER = 256
 NT = N // P
 QUADS = (0, 2, 1, 3)
-EARLY = 2 * P
+EARLY = 3 * P
 LATE = H - EARLY
 ROWS0 = 48
 KB = 1024
 
 AT_TAB = 0
-AT_PAGE0 = 48 * KB
-AT_WGS = 56 * KB
+AT_WV = 45 * KB
+AT_PAGE0 = 57 * KB
+AT_WGS0 = 65 * KB
 AT_V = 72 * KB
 AT_PLANES = 84 * KB
-AT_LATE = 88 * KB
 AT_W4 = 91 * KB
 AT_XBF = 97 * KB
 AT_ZBF = 113 * KB
 AT_ZROWS = 129 * KB
 AT_X = 145 * KB
 AT_STAGED = 177 * KB
-AT_WV = 189 * KB
+AT_TAIL = 189 * KB
 AT_WVBF = 201 * KB
-AT_W8 = 207 * KB
 AT_SC = 210 * KB
 AT_HEAD = 216 * KB
 AT_GAINS = 231 * KB
@@ -80,13 +79,11 @@ def tile_list_dialogue_reply_ranker_kernel(tc, tab_words, tab_scales, offs, offs
         ts_got = at("ts_got", [P, S], U8, AT_HEAD + 5 * KB)
         early_rows = at("early_rows", [P, S + EARLY], U8, AT_HEAD + 6 * KB)
         late_rows = at("late_rows", [P, LATE], U8, AT_HEAD + 8 * KB)
-        w4_raw = [at("w4_raw%d" % b, [P, KP, 2 * HALF], U8, AT_HEAD + (9 + 3 * b) * KB) for b in range(RP)]
+        w4_raw = {0: at("w4_raw0", [P, KP, 2 * HALF], U8, AT_HEAD + 9 * KB)}
         w4_dealt = [at("w4_dealt%d" % b, [P, KP, 2 * HALF], U8, AT_W4 + 3 * KB * b) for b in range(RP)]
         planes = at("planes", [P, KP, S + EARLY], U8, AT_PLANES)
-        late_planes = at("late_planes", [P, KP, LATE], U8, AT_LATE)
         v_codes = [at("v_codes%d" % a, [P, S], U32, AT_V + 4 * KB * a) for a in range(KP)]
-        weights = [at("wgs%d" % t, [P, S], F32, AT_WGS + 4 * KB * t) for t in range(PACK)]
-        w8_sc = at("w8_sc", [P, RP, N], U8, AT_SC)
+        weights = {0: at("wgs0", [P, S], F32, AT_WGS0)}
         wv_sc = at("wv_sc", [P, RP * N], U8, AT_SC + KB)
         x_sc = at("x_sc", [P, RP, M], U8, AT_SC + 2 * KB)
         z_sc = at("z_sc", [P, RP, M], U8, AT_SC + 4 * KB)
@@ -123,9 +120,11 @@ def tile_list_dialogue_reply_ranker_kernel(tc, tab_words, tab_scales, offs, offs
         page_rows = page0.rearrange("(b p t) c -> b t p c", p=P, t=PACK)
         pages = {}
 
+        def at_page(i):
+            return AT_PAGE0 if i % PACK == 0 else AT_TAB + 16 * KB * (i % PACK - 1)
+
         def load_page(i):
-            offset = AT_PAGE0 if i % (SLICES - 1) == 0 else AT_TAB + 8 * KB * (i - 1)
-            pages[i] = at("page%d" % i, [P, T2], F32, offset)
+            pages[i] = at("page%d" % i, [P, T2], F32, at_page(i))
             nc.sync.dma_start(pages[i][:], page_rows[i // PACK, i % PACK])
 
         first, rest = slice(0, QUARTER), slice(QUARTER, S)
@@ -141,8 +140,6 @@ def tile_list_dialogue_reply_ranker_kernel(tc, tab_words, tab_scales, offs, offs
         load_page(0)
         load_weights(nc.sync, 0, rest)
         nc.vector.memset(planes[:].bitcast(I32), 0)
-        nc.vector.memset(late_planes[:].bitcast(I32), 0)
-        nc.vector.memset(w8_sc[:].bitcast(I32), 0)
 
         nc.vector.tensor_copy(ts_got[:], ts_win[:].indirect(list1[:]))
         as_given = w4s_raw[:].rearrange("p (b m t) -> p b t m", b=RP, t=PACK)
@@ -160,26 +157,31 @@ def tile_list_dialogue_reply_ranker_kernel(tc, tab_words, tab_scales, offs, offs
         for part in first_parts:
             nc.vector.tensor_copy(v_codes[KP - 1][:, part], tabs[KP - 1][:].bitcast(U32).indirect(entries(list1, part)))
 
-        gin_t = at("gin_t", [P, RP, PACK], F32, AT_GAINS)
-        gout_t = at("gout_t", [P, RP, PACK], F32, AT_GAINS + 64)
+        gin_t = at("gin_t", [P, RP, PACK], F32, AT_TAB + 12 * KB)
+        late_planes = at("late_planes", [P, KP, LATE], U8, AT_TAB + 13 * KB)
+        w4_raw[1] = at("w4_raw1", [P, KP, 2 * HALF], U8, AT_TAB + 28 * KB)
+        gout_t = at("gout_t", [P, RP, PACK], F32, AT_TAB + 44 * KB)
+        w8_sc = at("w8_sc", [P, RP, N], U8, AT_TAB + 44 * KB + 64)
+        nc.vector.memset(late_planes[:].bitcast(I32), 0)
+        nc.vector.memset(w8_sc[:].bitcast(I32), 0)
 
         whole = slice(0, S)
         wv_raw = at("wv_raw", [P, RP, PACK, N], F32, AT_WV)
-        w8_codes = at("w8_codes", [P, RP, N], U32, AT_W8)
-        move_scale_rows(nc.sync, late_planes, late_rows)
         nc.sync.dma_start(list3[:], offs3)
-        for i in range(1, SLICES - 1):
+        for i in range(1, PACK):
             load_page(i)
-            if i < PACK:
-                load_weights(nc.sync, i, whole)
+            weights[i] = at("wgs%d" % i, [P, S], F32, at_page(i) + 8 * KB)
+            load_weights(nc.sync, i, whole)
             if i == 1:
                 nc.sync.dma_start(gin_t[:], gin.rearrange("(b p t) -> p b t", p=P, t=PACK))
+                move_scale_rows(nc.sync, late_planes, late_rows)
             if i == 2:
                 load_w4(nc.sync, 1)
-            if i == PACK - 1:
-                nc.sync.dma_start(gout_t[:], gout.rearrange("(b p t) -> p b t", p=P, t=PACK))
-            if i == PACK:
-                nc.sync.dma_start(wv_raw[:], wv.rearrange("(b p j) n -> p b j n", p=P, j=PACK))
+        nc.sync.dma_start(gout_t[:], gout.rearrange("(b p t) -> p b t", p=P, t=PACK))
+        nc.sync.dma_start(wv_raw[:], wv.rearrange("(b p j) n -> p b j n", p=P, j=PACK))
+        for q in QUADS:
+            nc.sync.dma_start(w8_sc[32 * q:32 * q + 4, :, :].bitcast(I32),
+                              w8_scales[:, 4 * q:4 * q + 4, :].rearrange("b r c -> r b c").bitcast(I32))
 
         x_f32 = [at("x_f32_%d" % b, [P, PACK, M], F32, AT_X + 16 * KB * b) for b in range(RP)]
         z_rows = [at("z_rows%d" % b, [P, PACK, M], BF16, AT_ZROWS + 8 * KB * b) for b in range(RP)]
@@ -203,7 +205,7 @@ def tile_list_dialogue_reply_ranker_kernel(tc, tab_words, tab_scales, offs, offs
             if i == 0:
                 groups = zip(first_parts, (7, 6, 5))
             else:
-                groups = zip((cols(0), cols(1)), (6, 7) if i % 2 else (4, 5))
+                groups = zip((cols(0), cols(1)), (7 - (2 * i + 1) % 3, 7 - (2 * i + 2) % 3))
             for part, n in groups:
                 acc = bank(n)
                 width = part.stop - part.start
@@ -264,38 +266,43 @@ def tile_list_dialogue_reply_ranker_kernel(tc, tab_words, tab_scales, offs, offs
         scatter(0)
         project(2)
         fetch(0, whole)
-        load_page(SLICES - 1)
-        nc.sync.dma_start(w8_codes[:].bitcast(I32), w8_words.rearrange("b p c i -> p b (c i)").bitcast(I32))
-        for q in QUADS:
-            nc.sync.dma_start(w8_sc[32 * q:32 * q + 4, :, :].bitcast(I32),
-                              w8_scales[:, 4 * q:4 * q + 4, :].rearrange("b r c -> r b c").bitcast(I32))
+        load_page(PACK)
+        for h in range(2):
+            nc.scalar.copy(x_bf[0, h][:, :, 0], x_row(0)[:, cols(h)])
         scatter(1)
         for i in range(SLICES - 2):
             scatter(i + 2)
             make_z(i)
             if i == 0:
                 deal_w4(1)
+                w8_codes = at("w8_codes", [P, RP, N], U32, AT_TAB + 28 * KB)
+                nc.sync.dma_start(w8_codes[:].bitcast(I32), w8_words.rearrange("b p c i -> p b (c i)").bitcast(I32))
             if i + 3 < SLICES:
                 project(i + 3)
             if i + 1 < SLICES - 2:
                 fetch(i + 1, whole)
+            if i + 1 < PACK:
+                load_page(i + 1 + PACK)
             if i == 2:
                 wv_bf = at("wv_bf", [P, RP * N * PACK], BF16, AT_WVBF)
                 for b in range(RP):
                     weave_wv(wv_bf, b)
-            if i in (1, 3):
+            if i == 1:
                 for h in range(2):
-                    weave(nc.scalar.copy, x_bf, x_f32, 0, h, i - 1, i + 1)
-                    weave(nc.scalar.copy, z_bf, z_rows, 0, h, i - 1, i + 1)
+                    weave(nc.scalar.copy, z_bf, z_rows, 0, h, 0, 2)
+            if i == PACK - 1:
+                for h in range(2):
+                    weave(nc.scalar.copy, x_bf, x_f32, 0, h, 1, PACK)
+                weave(nc.scalar.copy, z_bf, z_rows, 0, 0, 2, PACK)
             if i == PACK:
                 for h in range(2):
                     nc.scalar.copy(x_bf[1, h][:, :, 0], x_row(i)[:, cols(h)])
+                weave(nc.scalar.copy, z_bf, z_rows, 0, 1, 2, PACK)
 
         pair = (SLICES - 2, SLICES - 1)
         for h in range(2):
             for i in pair:
                 fetch(i, cols(h))
-        at_page = lambda i: AT_TAB + 8 * KB * (i - 1)
         x_codes = {(0, 0): at("x_codes00", [P, HALF], U32, at_page(6) + 4 * KB),
                    (0, 1): at("x_codes01", [P, HALF], U32, at_page(6) + 6 * KB),
                    (1, 0): at("x_codes10", [P, HALF], U32, AT_V),
@@ -304,7 +311,7 @@ def tile_list_dialogue_reply_ranker_kernel(tc, tab_words, tab_scales, offs, offs
                    (0, 1): at("z_codes01", [P, HALF], U32, at_page(6) + 2 * KB),
                    (1, 0): at("z_codes10", [P, HALF], U32, AT_V + 4 * KB),
                    (1, 1): at("z_codes11", [P, HALF], U32, AT_V + 6 * KB)}
-        wv_codes = at("wv_codes", [P, RP * N], U32, AT_PAGE0)
+        wv_codes = at("wv_codes", [P, RP * N], U32, at_page(7))
 
         def quantize(codes, scales, src, b, h):
             nc.vector.quantize_mx(out=codes[b, h][:].bitcast(FP8X4), scales=scales[:, b, cols(h)],
@@ -353,13 +360,13 @@ def tile_list_dialogue_reply_ranker_kernel(tc, tab_words, tab_scales, offs, offs
                 gate_pass(gate[n, h], n, b, h)
         th = {}
         for k, (n, h) in enumerate(order):
-            th[n, h] = at("th%d" % k, [P, HALF], F32, at_page(1) + 2 * KB * k)
+            th[n, h] = at("th%d" % k, [P, HALF], F32, AT_TAIL + 2 * KB * k)
             nc.scalar.activation(th[n, h][:], gate[n, h][:], ACT.Tanh, scale=0.5)
         for k, (n, h) in enumerate(order):
             value = bank((6 + k) % 8)
             for b in range(RP):
                 value_pass(value, n, b, h)
-            res = at("res%d" % k, [P, HALF], F32, at_page(3) + 2 * KB * k)
+            res = at("res%d" % k, [P, HALF], F32, AT_WV + 2 * KB * k)
             nc.vector.scalar_tensor_tensor(out=res[:], in0=th[n, h][:], scalar=1.0, in1=value[:],
                                            op0=ALU.add, op1=ALU.mult)
             nc.sync.dma_start(out[P * n:P * (n + 1), cols(h)], res[:])

@@ -30,20 +30,25 @@ LATE = H - EARLY
 ROWS0 = 48
 KB = 1024
 
-AT_TAB = 0
-AT_WV = 45 * KB
-AT_PAGE0 = 57 * KB
-AT_WGS0 = 65 * KB
-AT_V = 72 * KB
-AT_PLANES = 84 * KB
-AT_W4 = 91 * KB
-AT_XBF = 97 * KB
-AT_ZBF = 113 * KB
-AT_ZROWS = 129 * KB
-AT_X = 145 * KB
-AT_STAGED = 177 * KB
-AT_TAIL = 189 * KB
-AT_WVBF = 201 * KB
+SHIFT = KB // 4
+AT_TABS = (4 * KB, 20 * KB + SHIFT, 36 * KB + SHIFT)
+AT_PAGES = (8 * KB, AT_TABS[2] + 64, AT_TABS[2] - 8 * KB + 64, 64, 8 * KB + 64)
+AT_WGS0 = 16 * KB + 64
+AT_W4_LATE = AT_TABS[2] + 9 * KB
+AT_LATE = AT_TABS[2] + 12 * KB
+AT_W8_SC = AT_TABS[2] + 14 * KB
+AT_LATER = AT_TABS[2] + 16 * KB - 64
+AT_WV = AT_TABS[2] + 28 * KB
+AT_V = 77 * KB
+AT_PLANES = 89 * KB
+AT_W4 = 94 * KB
+AT_XBF = 100 * KB
+AT_ZBF = 116 * KB
+AT_ZROWS = 132 * KB
+AT_X = 148 * KB
+AT_STAGED = 180 * KB
+AT_TAIL = 192 * KB
+AT_WVBF = 204 * KB
 AT_SC = 210 * KB
 AT_HEAD = 216 * KB
 AT_GAINS = 231 * KB
@@ -73,17 +78,16 @@ def tile_list_dialogue_reply_ranker_kernel(tc, tab_words, tab_scales, offs, offs
         list2 = lists.tile([P, S // 16], U16)
         list3 = lists.tile([P, M // 16], U16)
 
-        tabs = [at("tab%d" % a, [P, T], I32, AT_TAB + 16 * KB * a) for a in range(KP)]
-        ts_win = at("ts_win", [P, T], U8, AT_HEAD)
+        tabs = [at("tab%d" % a, [P, T], I32, AT_TABS[a]) for a in range(KP)]
+        ts_win = at("ts_win", [P, T], U8, AT_V)
         w4s_raw = at("w4s_raw", [P, H], U8, AT_HEAD + 4 * KB)
         ts_got = at("ts_got", [P, S], U8, AT_HEAD + 5 * KB)
         early_rows = at("early_rows", [P, S + EARLY], U8, AT_HEAD + 6 * KB)
-        late_rows = at("late_rows", [P, LATE], U8, AT_HEAD + 8 * KB)
+        late_rows = at("late_rows", [P, LATE], U8, AT_WV)
         w4_raw = {0: at("w4_raw0", [P, KP, 2 * HALF], U8, AT_HEAD + 9 * KB)}
         w4_dealt = [at("w4_dealt%d" % b, [P, KP, 2 * HALF], U8, AT_W4 + 3 * KB * b) for b in range(RP)]
         planes = at("planes", [P, KP, S + EARLY], U8, AT_PLANES)
-        v_codes = [at("v_codes%d" % a, [P, S], U32, AT_V + 4 * KB * a) for a in range(KP)]
-        weights = {0: at("wgs0", [P, S], F32, AT_WGS0)}
+        weights = {}
         wv_sc = at("wv_sc", [P, RP * N], U8, AT_SC + KB)
         x_sc = at("x_sc", [P, RP, M], U8, AT_SC + 2 * KB)
         z_sc = at("z_sc", [P, RP, M], U8, AT_SC + 4 * KB)
@@ -92,12 +96,12 @@ def tile_list_dialogue_reply_ranker_kernel(tc, tab_words, tab_scales, offs, offs
             nc.sync.dma_start(tabs[a][:], tab_words[a].rearrange("p t i -> p (t i)").bitcast(I32))
 
         def load_scale_rows(tile, scales):
-            nc.scalar.dma_start(tile[ROWS0:2 * ROWS0, :].bitcast(I32), scales.rearrange("a q c -> q a c").bitcast(I32))
+            nc.sync.dma_start(tile[ROWS0:2 * ROWS0, :].bitcast(I32), scales.rearrange("a q c -> q a c").bitcast(I32))
             nc.vector.memset(tile[0:ROWS0, :].bitcast(I32), 0)
             nc.vector.memset(tile[2 * ROWS0:P, :].bitcast(I32), 0)
 
-        def move_scale_rows(queue, dst, src):
-            for q in QUADS:
+        def move_scale_rows(queue, dst, src, quads=QUADS):
+            for q in quads:
                 row = ROWS0 + 4 * KP * q
                 queue.dma_start(dst[32 * q:32 * q + 4].rearrange("p a c -> p (a c)").bitcast(I32),
                                 src[row:row + 4 * KP, :].bitcast(I32))
@@ -121,7 +125,7 @@ def tile_list_dialogue_reply_ranker_kernel(tc, tab_words, tab_scales, offs, offs
         pages = {}
 
         def at_page(i):
-            return AT_PAGE0 if i % PACK == 0 else AT_TAB + 16 * KB * (i % PACK - 1)
+            return AT_PAGES[i if i <= PACK else i - PACK]
 
         def load_page(i):
             pages[i] = at("page%d" % i, [P, T2], F32, at_page(i))
@@ -132,56 +136,55 @@ def tile_list_dialogue_reply_ranker_kernel(tc, tab_words, tab_scales, offs, offs
         load_table(0)
         load_scale_rows(ts_win, tab_scales)
         load_scale_rows(w4s_raw, w4_scales)
-        load_w4(nc.scalar, 0)
-        load_weights(nc.gpsimd, 0, first)
+        load_w4(nc.sync, 0)
         load_table(1)
         nc.sync.dma_start(list2[:], offs2)
+        nc.sync.dma_start(list3[:], offs3)
         load_table(2)
-        load_page(0)
-        load_weights(nc.sync, 0, rest)
         nc.vector.memset(planes[:].bitcast(I32), 0)
 
         nc.vector.tensor_copy(ts_got[:], ts_win[:].indirect(list1[:]))
         as_given = w4s_raw[:].rearrange("p (b m t) -> p b t m", b=RP, t=PACK)
         nc.vector.tensor_copy(early_rows[:, S:].rearrange("p (t m) -> p t m", m=P), as_given[:, 0, :EARLY // P])
         nc.vector.tensor_copy(early_rows[:, :S].bitcast(I32), ts_got[:].bitcast(I32))
-        move_scale_rows(nc.gpsimd, planes, early_rows)
+        move_scale_rows(nc.scalar, planes, early_rows, QUADS[:2])
+        move_scale_rows(nc.gpsimd, planes, early_rows, QUADS[2:])
         by_slice = late_rows[:].rearrange("p (t m) -> p t m", m=P)
         nc.vector.tensor_copy(by_slice[:, :PACK - EARLY // P], as_given[:, 0, EARLY // P:])
         nc.vector.tensor_copy(by_slice[:, PACK - EARLY // P:], as_given[:, 1])
         deal_w4(0)
 
+        v_codes = [at("v_codes%d" % a, [P, S], U32, AT_V + 4 * KB * a) for a in range(KP)]
         first_parts = (first, slice(QUARTER, HALF), cols(1))
         for a in range(KP - 1):
             nc.vector.tensor_copy(v_codes[a][:], tabs[a][:].bitcast(U32).indirect(list1[:]))
         for part in first_parts:
             nc.vector.tensor_copy(v_codes[KP - 1][:, part], tabs[KP - 1][:].bitcast(U32).indirect(entries(list1, part)))
 
-        gin_t = at("gin_t", [P, RP, PACK], F32, AT_TAB + 12 * KB)
-        late_planes = at("late_planes", [P, KP, LATE], U8, AT_TAB + 13 * KB)
-        w4_raw[1] = at("w4_raw1", [P, KP, 2 * HALF], U8, AT_TAB + 28 * KB)
-        gout_t = at("gout_t", [P, RP, PACK], F32, AT_TAB + 44 * KB)
-        w8_sc = at("w8_sc", [P, RP, N], U8, AT_TAB + 44 * KB + 64)
-        nc.vector.memset(late_planes[:].bitcast(I32), 0)
-        nc.vector.memset(w8_sc[:].bitcast(I32), 0)
-
         whole = slice(0, S)
-        wv_raw = at("wv_raw", [P, RP, PACK, N], F32, AT_WV)
-        nc.sync.dma_start(list3[:], offs3)
+        weights[0] = at("wgs0", [P, S], F32, AT_WGS0)[:]
+        load_weights(nc.sync, 0, first)
+        load_page(0)
+        load_weights(nc.sync, 0, rest)
+        later = at("later", [P, (PACK - 1) * S + RP * PACK], F32, AT_LATER)
+        gin_t = later[:, (PACK - 1) * S:].rearrange("p (b t) -> p b t", t=PACK)
+        w4_raw[1] = at("w4_raw1", [P, KP, 2 * HALF], U8, AT_W4_LATE)
+        late_planes = at("late_planes", [P, KP, LATE], U8, AT_LATE)
+        w8_sc = at("w8_sc", [P, RP, N], U8, AT_W8_SC)
+        nc.gpsimd.memset(late_planes[:].bitcast(I32), 0)
+        nc.gpsimd.memset(w8_sc[:].bitcast(I32), 0)
         for i in range(1, PACK):
+            weights[i] = later[:, S * (i - 1):S * i]
+        for i in range(1, PACK - 1):
             load_page(i)
-            weights[i] = at("wgs%d" % i, [P, S], F32, at_page(i) + 8 * KB)
             load_weights(nc.sync, i, whole)
             if i == 1:
-                nc.sync.dma_start(gin_t[:], gin.rearrange("(b p t) -> p b t", p=P, t=PACK))
+                nc.sync.dma_start(gin_t, gin.rearrange("(b p t) -> p b t", p=P, t=PACK))
                 move_scale_rows(nc.sync, late_planes, late_rows)
-            if i == 2:
-                load_w4(nc.sync, 1)
-        nc.sync.dma_start(gout_t[:], gout.rearrange("(b p t) -> p b t", p=P, t=PACK))
-        nc.sync.dma_start(wv_raw[:], wv.rearrange("(b p j) n -> p b j n", p=P, j=PACK))
-        for q in QUADS:
-            nc.sync.dma_start(w8_sc[32 * q:32 * q + 4, :, :].bitcast(I32),
-                              w8_scales[:, 4 * q:4 * q + 4, :].rearrange("b r c -> r b c").bitcast(I32))
+        load_w4(nc.sync, 1)
+        latest = at("latest", [P, RP * PACK * (N + 1)], F32, AT_WV)
+        gout_t = latest[:, :RP * PACK].rearrange("p (b t) -> p b t", t=PACK)
+        wv_raw = latest[:, RP * PACK:].rearrange("p (b j n) -> p b j n", b=RP, j=PACK)
 
         x_f32 = [at("x_f32_%d" % b, [P, PACK, M], F32, AT_X + 16 * KB * b) for b in range(RP)]
         z_rows = [at("z_rows%d" % b, [P, PACK, M], BF16, AT_ZROWS + 8 * KB * b) for b in range(RP)]
@@ -228,9 +231,12 @@ def tile_list_dialogue_reply_ranker_kernel(tc, tab_words, tab_scales, offs, offs
         def fetch(i, part):
             nc.vector.tensor_copy(x_row(i)[:, part], pages[i][:].indirect(entries(list3, part)))
 
+        def shaped(row, like):
+            return row if like.ndim == 2 else row.rearrange("p (r c) -> p r c", r=like.shape[1])
+
         def gelu(i, part, ge):
             b, t = divmod(i, PACK)
-            nc.scalar.activation(ge, x_row(i)[:, part], ACT.Gelu_apprx_tanh, scale=gin_t[:, b, t:t + 1])
+            nc.scalar.activation(ge, shaped(x_row(i)[:, part], ge), ACT.Gelu_apprx_tanh, scale=gin_t[:, b, t:t + 1])
 
         def gain(i, dst, ge):
             b, t = divmod(i, PACK)
@@ -245,12 +251,12 @@ def tile_list_dialogue_reply_ranker_kernel(tc, tab_words, tab_scales, offs, offs
                     ahead = at("ahead_of_wv", [P, QUARTER], F32, AT_WVBF)
                     parts = [parts[0], (slice(HALF, HALF + QUARTER), parked[:, :QUARTER]), (slice(HALF + QUARTER, M), ahead[:])]
             else:
-                parts = [(slice(QUARTER * k, QUARTER * (k + 1)),
-                          x_row(i + 1 + k % 2)[:, HALF * (k // 2):HALF * (k // 2) + QUARTER]) for k in range(4)]
+                parts = [(slice(QUARTER * k, QUARTER * (k + 1)), x_row(i + 1 + k)[:, :QUARTER]) for k in range(2)]
+                parts.append((cols(1), x_f32[b][:, t + 1:, HALF:HALF + QUARTER]))
             for part, ge in parts:
                 gelu(i, part, ge)
             for k, (part, ge) in enumerate(parts):
-                gain(i, z_bf[b, k][:, :, 0] if i == PACK else z_rows[b][:, t, part], ge)
+                gain(i, z_bf[b, k][:, :, 0] if i == PACK else shaped(z_rows[b][:, t, part], ge), ge)
 
         def weave(copy, dst, src, b, h, t0, t1, part=slice(0, HALF)):
             copy(dst[b, h][:, part, t0:t1].rearrange("p (c i) t -> p c t i", i=4),
@@ -266,7 +272,14 @@ def tile_list_dialogue_reply_ranker_kernel(tc, tab_words, tab_scales, offs, offs
         scatter(0)
         project(2)
         fetch(0, whole)
+        load_page(PACK - 1)
+        load_weights(nc.sync, PACK - 1, whole)
+        nc.sync.dma_start(gout_t, gout.rearrange("(b p t) -> p b t", p=P, t=PACK))
         load_page(PACK)
+        nc.sync.dma_start(wv_raw, wv.rearrange("(b p j) n -> p b j n", p=P, j=PACK))
+        for q in QUADS:
+            nc.sync.dma_start(w8_sc[32 * q:32 * q + 4, :, :].bitcast(I32),
+                              w8_scales[:, 4 * q:4 * q + 4, :].rearrange("b r c -> r b c").bitcast(I32))
         for h in range(2):
             nc.scalar.copy(x_bf[0, h][:, :, 0], x_row(0)[:, cols(h)])
         scatter(1)
@@ -275,7 +288,7 @@ def tile_list_dialogue_reply_ranker_kernel(tc, tab_words, tab_scales, offs, offs
             make_z(i)
             if i == 0:
                 deal_w4(1)
-                w8_codes = at("w8_codes", [P, RP, N], U32, AT_TAB + 28 * KB)
+                w8_codes = at("w8_codes", [P, RP, N], U32, AT_W4_LATE)
                 nc.sync.dma_start(w8_codes[:].bitcast(I32), w8_words.rearrange("b p c i -> p b (c i)").bitcast(I32))
             if i + 3 < SLICES:
                 project(i + 3)
@@ -317,20 +330,32 @@ def tile_list_dialogue_reply_ranker_kernel(tc, tab_words, tab_scales, offs, offs
             nc.vector.quantize_mx(out=codes[b, h][:].bitcast(FP8X4), scales=scales[:, b, cols(h)],
                                   in_=src[b, h][:].rearrange("p m t -> p (m t)"))
 
-        for h in range(2):
-            ge = {i: at("ge%d%d" % (i, h), [P, HALF], F32, at_page(5) + 2 * KB * (2 * h + i % 2)) for i in pair}
-            for i in pair:
-                gelu(i, cols(h), ge[i][:])
-            for i in pair:
-                gain(i, z_rows[1][:, i % PACK, cols(h)], ge[i][:])
-            if h == 0:
-                weave(nc.scalar.copy, x_bf, x_f32, 1, 0, 1, PACK)
-            weave(nc.scalar.copy, z_bf, z_rows, 1, h, 1, PACK)
+        ge = {(i, h): at("ge%d%d" % (i, h), [P, HALF], F32, at_page(5) + 2 * KB * (2 * h + i % 2))
+              for h in range(2) for i in pair}
+
+        def last_gelu(i, h):
+            gelu(i, cols(h), ge[i, h][:])
+
+        def last_gain(i, h):
+            gain(i, z_rows[1][:, i % PACK, cols(h)], ge[i, h][:])
+
+        last_gelu(6, 0)
+        last_gelu(7, 0)
+        last_gain(6, 0)
+        weave(nc.scalar.copy, x_bf, x_f32, 1, 0, 1, PACK, first)
+        last_gain(7, 0)
+        last_gelu(6, 1)
+        weave(nc.scalar.copy, z_bf, z_rows, 1, 0, 1, PACK)
+        last_gelu(7, 1)
+        last_gain(6, 1)
+        last_gain(7, 1)
+        weave(nc.scalar.copy, z_bf, z_rows, 1, 1, 1, PACK)
 
         quantize(x_codes, x_sc, x_bf, 0, 0)
+        weave(nc.vector.tensor_copy, x_bf, x_f32, 1, 0, 1, PACK, slice(QUARTER, HALF))
         weave(nc.vector.tensor_copy, x_bf, x_f32, 1, 1, 1, PACK)
-        quantize(x_codes, x_sc, x_bf, 0, 1)
         quantize(x_codes, x_sc, x_bf, 1, 0)
+        quantize(x_codes, x_sc, x_bf, 0, 1)
         quantize(x_codes, x_sc, x_bf, 1, 1)
         for b in range(RP):
             nc.vector.quantize_mx(out=wv_codes[:, b * N:(b + 1) * N].bitcast(FP8X4), scales=wv_sc[:, b * N:(b + 1) * N],
@@ -366,7 +391,7 @@ def tile_list_dialogue_reply_ranker_kernel(tc, tab_words, tab_scales, offs, offs
             value = bank((6 + k) % 8)
             for b in range(RP):
                 value_pass(value, n, b, h)
-            res = at("res%d" % k, [P, HALF], F32, AT_WV + 2 * KB * k)
+            res = at("res%d" % k, [P, HALF], F32, AT_LATER + 2 * KB * k)
             nc.vector.scalar_tensor_tensor(out=res[:], in0=th[n, h][:], scalar=1.0, in1=value[:],
                                            op0=ALU.add, op1=ALU.mult)
             nc.sync.dma_start(out[P * n:P * (n + 1), cols(h)], res[:])

@@ -21,6 +21,7 @@ PACK = 4
 KP = K // (P * PACK)
 RP = H // (P * PACK)
 SLICES = RP * PACK
+ORDER = (0, 4, 1, 2, 3, 5, 6, 7)
 HALF = 512
 QUARTER = 256
 NT = N // P
@@ -111,9 +112,9 @@ def tile_list_dialogue_reply_ranker_kernel(tc, tab_words, tab_scales, offs, offs
         def load_w4(queue, b):
             queue.dma_start(w4_raw[b][:].bitcast(I32), w4_rows[:, :, 2 * HALF * b:2 * HALF * (b + 1)].bitcast(I32))
 
-        def deal_w4(b):
-            nc.scalar.copy(w4_dealt[b][:].bitcast(U16).rearrange("p a (t c i) -> p a c t i", t=PACK, i=8),
-                           w4_raw[b][:].bitcast(U16).rearrange("p a (c i t) -> p a c t i", t=PACK, i=8))
+        def deal_w4(b, slots):
+            nc.scalar.copy(w4_dealt[b][:].bitcast(U16).rearrange("p a (t c i) -> p a c t i", t=PACK, i=8)[:, :, :, slots],
+                           w4_raw[b][:].bitcast(U16).rearrange("p a (c i t) -> p a c t i", t=PACK, i=8)[:, :, :, slots])
 
         wgs_rows = wgs.rearrange("(q t) j -> q t j", t=PACK)
 
@@ -127,9 +128,9 @@ def tile_list_dialogue_reply_ranker_kernel(tc, tab_words, tab_scales, offs, offs
         def at_page(i):
             return AT_PAGES[i if i <= PACK else i - PACK]
 
-        def load_page(i):
-            pages[i] = at("page%d" % i, [P, T2], F32, at_page(i))
-            nc.sync.dma_start(pages[i][:], page_rows[i // PACK, i % PACK])
+        def load_page(k):
+            pages[k] = at("page%d" % k, [P, T2], F32, at_page(k))
+            nc.sync.dma_start(pages[k][:], page_rows[ORDER[k] // PACK, ORDER[k] % PACK])
 
         first, rest = slice(0, QUARTER), slice(QUARTER, S)
         nc.sync.dma_start(list1[:], offs)
@@ -145,14 +146,16 @@ def tile_list_dialogue_reply_ranker_kernel(tc, tab_words, tab_scales, offs, offs
 
         nc.vector.tensor_copy(ts_got[:], ts_win[:].indirect(list1[:]))
         as_given = w4s_raw[:].rearrange("p (b m t) -> p b t m", b=RP, t=PACK)
-        nc.vector.tensor_copy(early_rows[:, S:].rearrange("p (t m) -> p t m", m=P), as_given[:, 0, :EARLY // P])
+        early_by_slice = early_rows[:, S:].rearrange("p (k m) -> p k m", m=P)
+        nc.vector.tensor_copy(early_by_slice[:, :RP], as_given[:, :, 0])
+        nc.vector.tensor_copy(early_by_slice[:, RP], as_given[:, 0, 1])
         nc.vector.tensor_copy(early_rows[:, :S].bitcast(I32), ts_got[:].bitcast(I32))
         move_scale_rows(nc.scalar, planes, early_rows, QUADS[:2])
         move_scale_rows(nc.gpsimd, planes, early_rows, QUADS[2:])
         by_slice = late_rows[:].rearrange("p (t m) -> p t m", m=P)
-        nc.vector.tensor_copy(by_slice[:, :PACK - EARLY // P], as_given[:, 0, EARLY // P:])
-        nc.vector.tensor_copy(by_slice[:, PACK - EARLY // P:], as_given[:, 1])
-        deal_w4(0)
+        nc.vector.tensor_copy(by_slice[:, :2], as_given[:, 0, 2:])
+        nc.vector.tensor_copy(by_slice[:, 2:], as_given[:, 1, 1:])
+        deal_w4(0, slice(0, PACK))
 
         v_codes = [at("v_codes%d" % a, [P, S], U32, AT_V + 4 * KB * a) for a in range(KP)]
         first_parts = (first, slice(QUARTER, HALF), cols(1))
@@ -167,7 +170,8 @@ def tile_list_dialogue_reply_ranker_kernel(tc, tab_words, tab_scales, offs, offs
         load_page(0)
         load_weights(nc.sync, 0, rest)
         later = at("later", [P, (PACK - 1) * S + RP * PACK], F32, AT_LATER)
-        gin_t = later[:, (PACK - 1) * S:].rearrange("p (b t) -> p b t", t=PACK)
+        gin_first = later[:, (PACK - 1) * S:(PACK - 1) * S + RP]
+        gin_cols = gin.rearrange("(b p t) -> p b t", p=P, t=PACK)
         w4_raw[1] = at("w4_raw1", [P, KP, 2 * HALF], U8, AT_W4_LATE)
         late_planes = at("late_planes", [P, KP, LATE], U8, AT_LATE)
         w8_sc = at("w8_sc", [P, RP, N], U8, AT_W8_SC)
@@ -175,16 +179,19 @@ def tile_list_dialogue_reply_ranker_kernel(tc, tab_words, tab_scales, offs, offs
         nc.gpsimd.memset(w8_sc[:].bitcast(I32), 0)
         for i in range(1, PACK):
             weights[i] = later[:, S * (i - 1):S * i]
-        for i in range(1, PACK - 1):
-            load_page(i)
-            load_weights(nc.sync, i, whole)
-            if i == 1:
-                nc.sync.dma_start(gin_t, gin.rearrange("(b p t) -> p b t", p=P, t=PACK))
-                move_scale_rows(nc.sync, late_planes, late_rows)
         load_w4(nc.sync, 1)
-        latest = at("latest", [P, RP * PACK * (N + 1)], F32, AT_WV)
+        load_page(1)
+        load_weights(nc.sync, 1, whole)
+        load_page(2)
+        with nc.allow_non_contiguous_dma(reason="one gain a partition and pass"):
+            nc.sync.dma_start(gin_first, gin_cols[:, :, 0])
+        move_scale_rows(nc.sync, late_planes, late_rows)
+        load_weights(nc.sync, 2, whole)
+        deal_w4(1, slice(0, 1))
+        latest = at("latest", [P, RP * PACK * (N + 2)], F32, AT_WV)
         gout_t = latest[:, :RP * PACK].rearrange("p (b t) -> p b t", t=PACK)
-        wv_raw = latest[:, RP * PACK:].rearrange("p (b j n) -> p b j n", b=RP, j=PACK)
+        gin_rest = latest[:, RP * PACK:RP * (2 * PACK - 1)].rearrange("p (b t) -> p b t", b=RP)
+        wv_raw = latest[:, 2 * RP * PACK:].rearrange("p (b j n) -> p b j n", b=RP, j=PACK)
 
         x_f32 = [at("x_f32_%d" % b, [P, PACK, M], F32, AT_X + 16 * KB * b) for b in range(RP)]
         z_rows = [at("z_rows%d" % b, [P, PACK, M], BF16, AT_ZROWS + 8 * KB * b) for b in range(RP)]
@@ -192,7 +199,6 @@ def tile_list_dialogue_reply_ranker_kernel(tc, tab_words, tab_scales, offs, offs
         z_bf = {}
         for b in range(RP):
             for h in range(2):
-                x_bf[b, h] = at("x_bf%d%d" % (b, h), [P, HALF, PACK], BF16, AT_XBF + 4 * KB * (2 * b + h))
                 z_bf[b, h] = at("z_bf%d%d" % (b, h), [P, HALF, PACK], BF16, AT_ZBF + 4 * KB * (2 * b + h))
         staged = {}
 
@@ -200,10 +206,10 @@ def tile_list_dialogue_reply_ranker_kernel(tc, tab_words, tab_scales, offs, offs
             return AT_STAGED + 4 * KB * (i % 3)
 
         def x_row(i):
-            return x_f32[i // PACK][:, i % PACK]
+            return x_f32[ORDER[i] // PACK][:, ORDER[i] % PACK]
 
         def project(i):
-            b, t = divmod(i, PACK)
+            b, t = divmod(ORDER[i], PACK)
             staged[i] = at("staged%d" % i, [P, S], F32, staged_at(i))
             if i == 0:
                 groups = zip(first_parts, (7, 6, 5))
@@ -226,7 +232,7 @@ def tile_list_dialogue_reply_ranker_kernel(tc, tab_words, tab_scales, offs, offs
         def scatter(i):
             for part in (first, rest) if i == 0 else (whole,):
                 nc.vector.tensor_tensor(pages[i][:].indirect(entries(list2, part)), staged[i][:, part],
-                                        weights[i % PACK][:, part], ALU.mult)
+                                        weights[ORDER[i] % PACK][:, part], ALU.mult)
 
         def fetch(i, part):
             nc.vector.tensor_copy(x_row(i)[:, part], pages[i][:].indirect(entries(list3, part)))
@@ -235,20 +241,20 @@ def tile_list_dialogue_reply_ranker_kernel(tc, tab_words, tab_scales, offs, offs
             return row if like.ndim == 2 else row.rearrange("p (r c) -> p r c", r=like.shape[1])
 
         def gelu(i, part, ge):
-            b, t = divmod(i, PACK)
-            nc.scalar.activation(ge, shaped(x_row(i)[:, part], ge), ACT.Gelu_apprx_tanh, scale=gin_t[:, b, t:t + 1])
+            b, t = divmod(ORDER[i], PACK)
+            nc.scalar.activation(ge, shaped(x_row(i)[:, part], ge), ACT.Gelu_apprx_tanh, scale=gin_rest[:, b, t - 1:t] if t else gin_first[:, b:b + 1])
 
         def gain(i, dst, ge):
-            b, t = divmod(i, PACK)
+            b, t = divmod(ORDER[i], PACK)
             nc.scalar.activation(dst, ge, ACT.Copy, scale=gout_t[:, b, t:t + 1])
 
         def make_z(i):
-            b, t = divmod(i, PACK)
+            b, t = divmod(ORDER[i], PACK)
             if i < SLICES - 3:
                 parked = at("parked%d" % i, [P, HALF], F32, staged_at(i + 3))
                 parts = [(cols(0), x_row(i + 1)[:, cols(0)]), (cols(1), parked[:])]
-                if i == 2:
-                    ahead = at("ahead_of_wv", [P, QUARTER], F32, AT_WVBF)
+                if i in (0, 3):
+                    ahead = at("ahead%d" % i, [P, QUARTER], F32, AT_WVBF if i else AT_XBF + 4 * KB - HALF)
                     parts = [parts[0], (slice(HALF, HALF + QUARTER), parked[:, :QUARTER]), (slice(HALF + QUARTER, M), ahead[:])]
             else:
                 parts = [(slice(QUARTER * k, QUARTER * (k + 1)), x_row(i + 1 + k)[:, :QUARTER]) for k in range(2)]
@@ -256,7 +262,7 @@ def tile_list_dialogue_reply_ranker_kernel(tc, tab_words, tab_scales, offs, offs
             for part, ge in parts:
                 gelu(i, part, ge)
             for k, (part, ge) in enumerate(parts):
-                gain(i, z_bf[b, k][:, :, 0] if i == PACK else shaped(z_rows[b][:, t, part], ge), ge)
+                gain(i, z_bf[b, k][:, :, 0] if i == 1 else shaped(z_rows[b][:, t, part], ge), ge)
 
         def weave(copy, dst, src, b, h, t0, t1, part=slice(0, HALF)):
             copy(dst[b, h][:, part, t0:t1].rearrange("p (c i) t -> p c t i", i=4),
@@ -272,22 +278,20 @@ def tile_list_dialogue_reply_ranker_kernel(tc, tab_words, tab_scales, offs, offs
         scatter(0)
         project(2)
         fetch(0, whole)
-        load_page(PACK - 1)
-        load_weights(nc.sync, PACK - 1, whole)
+        load_page(3)
         nc.sync.dma_start(gout_t, gout.rearrange("(b p t) -> p b t", p=P, t=PACK))
-        load_page(PACK)
-        nc.sync.dma_start(wv_raw, wv.rearrange("(b p j) n -> p b j n", p=P, j=PACK))
+        load_weights(nc.sync, 3, whole)
+        load_page(4)
         for q in QUADS:
             nc.sync.dma_start(w8_sc[32 * q:32 * q + 4, :, :].bitcast(I32),
                               w8_scales[:, 4 * q:4 * q + 4, :].rearrange("b r c -> r b c").bitcast(I32))
-        for h in range(2):
-            nc.scalar.copy(x_bf[0, h][:, :, 0], x_row(0)[:, cols(h)])
+        nc.sync.dma_start(wv_raw, wv.rearrange("(b p j) n -> p b j n", p=P, j=PACK))
         scatter(1)
         for i in range(SLICES - 2):
             scatter(i + 2)
             make_z(i)
             if i == 0:
-                deal_w4(1)
+                deal_w4(1, slice(1, PACK))
                 w8_codes = at("w8_codes", [P, RP, N], U32, AT_W4_LATE)
                 nc.sync.dma_start(w8_codes[:].bitcast(I32), w8_words.rearrange("b p c i -> p b (c i)").bitcast(I32))
             if i + 3 < SLICES:
@@ -296,20 +300,24 @@ def tile_list_dialogue_reply_ranker_kernel(tc, tab_words, tab_scales, offs, offs
                 fetch(i + 1, whole)
             if i + 1 < PACK:
                 load_page(i + 1 + PACK)
+            if i == 0:
+                nc.sync.dma_start(gin_rest, gin_cols[:, :, 1:])
+            if i < RP:
+                for h in range(2):
+                    x_bf[i, h] = at("x_bf%d%d" % (i, h), [P, HALF, PACK], BF16, AT_XBF + 4 * KB * (2 * i + h))
+                    nc.scalar.copy(x_bf[i, h][:, :, 0], x_row(i)[:, cols(h)])
             if i == 2:
+                for h in range(2):
+                    weave(nc.scalar.copy, z_bf, z_rows, 0, h, 0, 2)
+            if i == 3:
                 wv_bf = at("wv_bf", [P, RP * N * PACK], BF16, AT_WVBF)
                 for b in range(RP):
                     weave_wv(wv_bf, b)
-            if i == 1:
-                for h in range(2):
-                    weave(nc.scalar.copy, z_bf, z_rows, 0, h, 0, 2)
-            if i == PACK - 1:
+            if i == 4:
                 for h in range(2):
                     weave(nc.scalar.copy, x_bf, x_f32, 0, h, 1, PACK)
                 weave(nc.scalar.copy, z_bf, z_rows, 0, 0, 2, PACK)
-            if i == PACK:
-                for h in range(2):
-                    nc.scalar.copy(x_bf[1, h][:, :, 0], x_row(i)[:, cols(h)])
+            if i == 5:
                 weave(nc.scalar.copy, z_bf, z_rows, 0, 1, 2, PACK)
 
         pair = (SLICES - 2, SLICES - 1)

@@ -79,10 +79,10 @@ def tile_list_dialogue_reply_ranker_kernel(tc, tab_words, tab_scales, offs, offs
         list2 = lists.tile([P, S // 16], U16)
         list3 = lists.tile([P, M // 16], U16)
 
-        tabs = [at("tab%d" % a, [P, T], I32, AT_TABS[a]) for a in range(KP)]
+        tabs = {}
         ts_win = at("ts_win", [P, T], U8, AT_V)
         w4s_raw = at("w4s_raw", [P, H], U8, AT_HEAD + 4 * KB)
-        ts_got = at("ts_got", [P, S], U8, AT_HEAD + 5 * KB)
+        ts_got = at("ts_got", [P, S], U8, AT_TABS[KP - 1])
         early_rows = at("early_rows", [P, S + EARLY], U8, AT_HEAD + 6 * KB)
         late_rows = at("late_rows", [P, LATE], U8, AT_WV)
         w4_raw = {0: at("w4_raw0", [P, KP, 2 * HALF], U8, AT_HEAD + 9 * KB)}
@@ -94,6 +94,7 @@ def tile_list_dialogue_reply_ranker_kernel(tc, tab_words, tab_scales, offs, offs
         z_sc = at("z_sc", [P, RP, M], U8, AT_SC + 4 * KB)
 
         def load_table(a):
+            tabs[a] = at("tab%d" % a, [P, T], I32, AT_TABS[a])
             nc.sync.dma_start(tabs[a][:], tab_words[a].rearrange("p t i -> p (t i)").bitcast(I32))
 
         def load_scale_rows(tile, scales):
@@ -141,7 +142,6 @@ def tile_list_dialogue_reply_ranker_kernel(tc, tab_words, tab_scales, offs, offs
         load_table(1)
         nc.sync.dma_start(list2[:], offs2)
         nc.sync.dma_start(list3[:], offs3)
-        load_table(2)
         nc.vector.memset(planes[:].bitcast(I32), 0)
 
         nc.vector.tensor_copy(ts_got[:], ts_win[:].indirect(list1[:]))
@@ -151,7 +151,8 @@ def tile_list_dialogue_reply_ranker_kernel(tc, tab_words, tab_scales, offs, offs
         nc.vector.tensor_copy(early_by_slice[:, RP], as_given[:, 0, 1])
         nc.vector.tensor_copy(early_rows[:, :S].bitcast(I32), ts_got[:].bitcast(I32))
         move_scale_rows(nc.scalar, planes, early_rows, QUADS[:2])
-        move_scale_rows(nc.gpsimd, planes, early_rows, QUADS[2:])
+        move_scale_rows(nc.sync, planes, early_rows, QUADS[2:])
+        load_table(KP - 1)
         by_slice = late_rows[:].rearrange("p (t m) -> p t m", m=P)
         nc.vector.tensor_copy(by_slice[:, :2], as_given[:, 0, 2:])
         nc.vector.tensor_copy(by_slice[:, 2:], as_given[:, 1, 1:])
@@ -175,8 +176,8 @@ def tile_list_dialogue_reply_ranker_kernel(tc, tab_words, tab_scales, offs, offs
         w4_raw[1] = at("w4_raw1", [P, KP, 2 * HALF], U8, AT_W4_LATE)
         late_planes = at("late_planes", [P, KP, LATE], U8, AT_LATE)
         w8_sc = at("w8_sc", [P, RP, N], U8, AT_W8_SC)
-        nc.gpsimd.memset(late_planes[:].bitcast(I32), 0)
-        nc.gpsimd.memset(w8_sc[:].bitcast(I32), 0)
+        nc.vector.memset(late_planes[:].bitcast(I32), 0)
+        nc.vector.memset(w8_sc[:].bitcast(I32), 0)
         for i in range(1, PACK):
             weights[i] = later[:, S * (i - 1):S * i]
         load_w4(nc.sync, 1)

@@ -26,7 +26,7 @@ HALF = 512
 QUARTER = 256
 NT = N // P
 QUADS = (0, 2, 1, 3)
-EARLY = 3 * P
+EARLY = P
 LATE = H - EARLY
 ROWS0 = 48
 KB = 1024
@@ -35,24 +35,23 @@ SHIFT = KB // 4
 AT_TABS = (4 * KB, 20 * KB + SHIFT, 36 * KB + SHIFT)
 AT_PAGES = (8 * KB, AT_TABS[2] + 64, AT_TABS[2] - 8 * KB + 64, 64, 8 * KB + 64)
 AT_WGS0 = 16 * KB + 64
-AT_W4_LATE = AT_TABS[2] + 9 * KB
-AT_LATE = AT_TABS[2] + 12 * KB
-AT_W8_SC = AT_TABS[2] + 14 * KB
+AT_W4_LATE = AT_TABS[0]
 AT_LATER = AT_TABS[2] + 16 * KB - 64
-AT_WV = AT_TABS[2] + 28 * KB
-AT_V = 77 * KB
-AT_PLANES = 89 * KB
-AT_W4 = 94 * KB
-AT_XBF = 100 * KB
-AT_ZBF = 116 * KB
-AT_ZROWS = 132 * KB
-AT_X = 148 * KB
-AT_STAGED = 180 * KB
-AT_TAIL = 192 * KB
-AT_WVBF = 204 * KB
-AT_SC = 210 * KB
-AT_HEAD = 216 * KB
-AT_GAINS = 231 * KB
+AT_W8 = AT_TABS[2] + 28 * KB
+AT_WV = AT_TABS[2] + 32 * KB
+AT_V = 81 * KB
+AT_PLANES = 93 * KB
+AT_W4 = 98 * KB
+AT_XBF = 104 * KB
+AT_ZBF = 120 * KB
+AT_ZROWS = 136 * KB
+AT_X = 152 * KB
+AT_STAGED = 184 * KB
+AT_TAIL = 196 * KB
+AT_WVBF = 208 * KB
+AT_SC = 214 * KB
+AT_HEAD = 220 * KB
+AT_GAINS = 235 * KB
 
 
 def tile_list_dialogue_reply_ranker_kernel(tc, tab_words, tab_scales, offs, offs2, offs3, w4_words, w4_scales,
@@ -84,9 +83,10 @@ def tile_list_dialogue_reply_ranker_kernel(tc, tab_words, tab_scales, offs, offs
         w4s_raw = at("w4s_raw", [P, H], U8, AT_HEAD + 4 * KB)
         ts_got = at("ts_got", [P, S], U8, AT_TABS[KP - 1])
         early_rows = at("early_rows", [P, S + EARLY], U8, AT_HEAD + 6 * KB)
-        late_rows = at("late_rows", [P, LATE], U8, AT_WV)
+        late_rows = at("late_rows", [P, LATE], U8, AT_HEAD + 8 * KB)
+        late_planes = at("late_planes", [P, KP, LATE], U8, AT_HEAD + 12 * KB)
         w4_raw = {0: at("w4_raw0", [P, KP, 2 * HALF], U8, AT_HEAD + 9 * KB)}
-        w4_dealt = [at("w4_dealt%d" % b, [P, KP, 2 * HALF], U8, AT_W4 + 3 * KB * b) for b in range(RP)]
+        w4_slice = {}
         planes = at("planes", [P, KP, S + EARLY], U8, AT_PLANES)
         weights = {}
         wv_sc = at("wv_sc", [P, RP * N], U8, AT_SC + KB)
@@ -113,9 +113,12 @@ def tile_list_dialogue_reply_ranker_kernel(tc, tab_words, tab_scales, offs, offs
         def load_w4(queue, b):
             queue.dma_start(w4_raw[b][:].bitcast(I32), w4_rows[:, :, 2 * HALF * b:2 * HALF * (b + 1)].bitcast(I32))
 
-        def deal_w4(b, slots):
-            nc.scalar.copy(w4_dealt[b][:].bitcast(U16).rearrange("p a (t c i) -> p a c t i", t=PACK, i=8)[:, :, :, slots],
-                           w4_raw[b][:].bitcast(U16).rearrange("p a (c i t) -> p a c t i", t=PACK, i=8)[:, :, :, slots])
+        def deal_w4(b, t0, t1, offset):
+            dealt = at("w4_dealt%d%d" % (b, t0), [P, KP, 2 * P * (t1 - t0)], U8, offset)
+            nc.scalar.copy(dealt[:].bitcast(U16).rearrange("p a (t c i) -> p a c t i", t=t1 - t0, i=8),
+                           w4_raw[b][:].bitcast(U16).rearrange("p a (c i t) -> p a c t i", t=PACK, i=8)[:, :, :, t0:t1])
+            for t in range(t0, t1):
+                w4_slice[PACK * b + t] = dealt[:, :, 2 * P * (t - t0):2 * P * (t - t0 + 1)]
 
         wgs_rows = wgs.rearrange("(q t) j -> q t j", t=PACK)
 
@@ -134,8 +137,8 @@ def tile_list_dialogue_reply_ranker_kernel(tc, tab_words, tab_scales, offs, offs
             nc.sync.dma_start(pages[k][:], page_rows[ORDER[k] // PACK, ORDER[k] % PACK])
 
         first, rest = slice(0, QUARTER), slice(QUARTER, S)
-        nc.sync.dma_start(list1[:], offs)
         load_table(0)
+        nc.sync.dma_start(list1[:], offs)
         load_scale_rows(ts_win, tab_scales)
         load_scale_rows(w4s_raw, w4_scales)
         load_w4(nc.sync, 0)
@@ -143,20 +146,19 @@ def tile_list_dialogue_reply_ranker_kernel(tc, tab_words, tab_scales, offs, offs
         nc.sync.dma_start(list2[:], offs2)
         nc.sync.dma_start(list3[:], offs3)
         nc.vector.memset(planes[:].bitcast(I32), 0)
+        nc.vector.memset(late_planes[:].bitcast(I32), 0)
 
         nc.vector.tensor_copy(ts_got[:], ts_win[:].indirect(list1[:]))
         as_given = w4s_raw[:].rearrange("p (b m t) -> p b t m", b=RP, t=PACK)
-        early_by_slice = early_rows[:, S:].rearrange("p (k m) -> p k m", m=P)
-        nc.vector.tensor_copy(early_by_slice[:, :RP], as_given[:, :, 0])
-        nc.vector.tensor_copy(early_by_slice[:, RP], as_given[:, 0, 1])
+        nc.vector.tensor_copy(early_rows[:, S:], as_given[:, 0, 0])
         nc.vector.tensor_copy(early_rows[:, :S].bitcast(I32), ts_got[:].bitcast(I32))
         move_scale_rows(nc.scalar, planes, early_rows, QUADS[:2])
         move_scale_rows(nc.sync, planes, early_rows, QUADS[2:])
         load_table(KP - 1)
         by_slice = late_rows[:].rearrange("p (t m) -> p t m", m=P)
-        nc.vector.tensor_copy(by_slice[:, :2], as_given[:, 0, 2:])
-        nc.vector.tensor_copy(by_slice[:, 2:], as_given[:, 1, 1:])
-        deal_w4(0, slice(0, PACK))
+        nc.vector.tensor_copy(by_slice[:, 0], as_given[:, 1, 0])
+        nc.vector.tensor_copy(by_slice[:, 1:].rearrange("p (b t) m -> p b t m", b=RP), as_given[:, :, 1:])
+        deal_w4(0, 0, PACK, AT_W4)
 
         v_codes = [at("v_codes%d" % a, [P, S], U32, AT_V + 4 * KB * a) for a in range(KP)]
         first_parts = (first, slice(QUARTER, HALF), cols(1))
@@ -170,29 +172,21 @@ def tile_list_dialogue_reply_ranker_kernel(tc, tab_words, tab_scales, offs, offs
         load_weights(nc.sync, 0, first)
         load_page(0)
         load_weights(nc.sync, 0, rest)
+        w4_raw[1] = at("w4_raw1", [P, KP, 2 * HALF], U8, AT_W4_LATE)
+        load_w4(nc.sync, 1)
+        move_scale_rows(nc.sync, late_planes, late_rows)
         later = at("later", [P, (PACK - 1) * S + RP * PACK], F32, AT_LATER)
         gin_first = later[:, (PACK - 1) * S:(PACK - 1) * S + RP]
         gin_cols = gin.rearrange("(b p t) -> p b t", p=P, t=PACK)
-        w4_raw[1] = at("w4_raw1", [P, KP, 2 * HALF], U8, AT_W4_LATE)
-        late_planes = at("late_planes", [P, KP, LATE], U8, AT_LATE)
-        w8_sc = at("w8_sc", [P, RP, N], U8, AT_W8_SC)
-        nc.vector.memset(late_planes[:].bitcast(I32), 0)
-        nc.vector.memset(w8_sc[:].bitcast(I32), 0)
         for i in range(1, PACK):
             weights[i] = later[:, S * (i - 1):S * i]
-        load_w4(nc.sync, 1)
         load_page(1)
         load_weights(nc.sync, 1, whole)
         load_page(2)
         with nc.allow_non_contiguous_dma(reason="one gain a partition and pass"):
             nc.sync.dma_start(gin_first, gin_cols[:, :, 0])
-        move_scale_rows(nc.sync, late_planes, late_rows)
         load_weights(nc.sync, 2, whole)
-        deal_w4(1, slice(0, 1))
-        latest = at("latest", [P, RP * PACK * (N + 2)], F32, AT_WV)
-        gout_t = latest[:, :RP * PACK].rearrange("p (b t) -> p b t", t=PACK)
-        gin_rest = latest[:, RP * PACK:RP * (2 * PACK - 1)].rearrange("p (b t) -> p b t", b=RP)
-        wv_raw = latest[:, 2 * RP * PACK:].rearrange("p (b j n) -> p b j n", b=RP, j=PACK)
+        deal_w4(1, 0, 1, AT_W4 + 3 * KB)
 
         x_f32 = [at("x_f32_%d" % b, [P, PACK, M], F32, AT_X + 16 * KB * b) for b in range(RP)]
         z_rows = [at("z_rows%d" % b, [P, PACK, M], BF16, AT_ZROWS + 8 * KB * b) for b in range(RP)]
@@ -210,8 +204,7 @@ def tile_list_dialogue_reply_ranker_kernel(tc, tab_words, tab_scales, offs, offs
             return x_f32[ORDER[i] // PACK][:, ORDER[i] % PACK]
 
         def project(i):
-            b, t = divmod(ORDER[i], PACK)
-            staged[i] = at("staged%d" % i, [P, S], F32, staged_at(i))
+            staged[i] = at("staged%d" % i, [P, S], F32, staged_at(i) if i else AT_WV - 2 * KB)
             if i == 0:
                 groups = zip(first_parts, (7, 6, 5))
             else:
@@ -222,7 +215,7 @@ def tile_list_dialogue_reply_ranker_kernel(tc, tab_words, tab_scales, offs, offs
                 for a in range(KP):
                     nc.tensor.matmul_mx(
                         out=acc[:, :width],
-                        lhsT=w4_dealt[b][:, a, 2 * P * t:2 * P * (t + 1)].bitcast(FP4X4),
+                        lhsT=w4_slice[ORDER[i]][:, a].bitcast(FP4X4),
                         lhsT_scale=(planes[:, a, S + P * i:S + P * (i + 1)] if P * i < EARLY
                                     else late_planes[:, a, P * i - EARLY:P * (i + 1) - EARLY]),
                         rhs=v_codes[a][:, part].bitcast(FP8X4),
@@ -276,25 +269,30 @@ def tile_list_dialogue_reply_ranker_kernel(tc, tab_words, tab_scales, offs, offs
 
         project(0)
         project(1)
+        deal_w4(1, 1, PACK, AT_W4 + 3 * KB + 2 * P * KP - 64)
         scatter(0)
         project(2)
         fetch(0, whole)
+        latest = at("latest", [P, RP * PACK * (N + 2)], F32, AT_WV)
+        gout_t = latest[:, :RP * PACK].rearrange("p (b t) -> p b t", t=PACK)
+        gin_rest = latest[:, RP * PACK:RP * (2 * PACK - 1)].rearrange("p (b t) -> p b t", b=RP)
+        wv_raw = latest[:, 2 * RP * PACK:].rearrange("p (b j n) -> p b j n", b=RP, j=PACK)
         load_page(3)
         nc.sync.dma_start(gout_t, gout.rearrange("(b p t) -> p b t", p=P, t=PACK))
         load_weights(nc.sync, 3, whole)
         load_page(4)
+        w8_codes = at("w8_codes", [P, RP, N], U32, AT_W8)
+        w8_sc = at("w8_sc", [P, RP, N], U8, AT_W8 + 3 * KB)
+        nc.gpsimd.memset(w8_sc[:].bitcast(I32), 0)
         for q in QUADS:
             nc.sync.dma_start(w8_sc[32 * q:32 * q + 4, :, :].bitcast(I32),
                               w8_scales[:, 4 * q:4 * q + 4, :].rearrange("b r c -> r b c").bitcast(I32))
+        nc.sync.dma_start(w8_codes[:].bitcast(I32), w8_words.rearrange("b p c i -> p b (c i)").bitcast(I32))
         nc.sync.dma_start(wv_raw, wv.rearrange("(b p j) n -> p b j n", p=P, j=PACK))
         scatter(1)
         for i in range(SLICES - 2):
             scatter(i + 2)
             make_z(i)
-            if i == 0:
-                deal_w4(1, slice(1, PACK))
-                w8_codes = at("w8_codes", [P, RP, N], U32, AT_W4_LATE)
-                nc.sync.dma_start(w8_codes[:].bitcast(I32), w8_words.rearrange("b p c i -> p b (c i)").bitcast(I32))
             if i + 3 < SLICES:
                 project(i + 3)
             if i + 1 < SLICES - 2:
@@ -401,6 +399,7 @@ def tile_list_dialogue_reply_ranker_kernel(tc, tab_words, tab_scales, offs, offs
             for b in range(RP):
                 value_pass(value, n, b, h)
             res = at("res%d" % k, [P, HALF], F32, AT_LATER + 2 * KB * k)
-            nc.vector.scalar_tensor_tensor(out=res[:], in0=th[n, h][:], scalar=1.0, in1=value[:],
-                                           op0=ALU.add, op1=ALU.mult)
-            nc.sync.dma_start(out[P * n:P * (n + 1), cols(h)], res[:])
+            for part in (first, slice(QUARTER, HALF)) if k == len(order) - 1 else (cols(0),):
+                nc.vector.scalar_tensor_tensor(out=res[:, part], in0=th[n, h][:, part], scalar=1.0, in1=value[:, part],
+                                               op0=ALU.add, op1=ALU.mult)
+                nc.sync.dma_start(out[P * n:P * (n + 1), cols(h)][:, part], res[:, part])

@@ -79,8 +79,8 @@ def tile_list_dialogue_reply_ranker_kernel(tc, tab_words, tab_scales, offs, offs
         list3 = lists.tile([P, M // 16], U16)
 
         tabs = {}
-        ts_win = at("ts_win", [P, T], U8, AT_V)
-        w4s_raw = at("w4s_raw", [P, H], U8, AT_HEAD + 4 * KB)
+        ts_win = at("ts_win", [P, T], U8, AT_HEAD)
+        w4s_raw = at("w4s_raw", [P, H], U8, AT_V)
         ts_got = at("ts_got", [P, S], U8, AT_TABS[KP - 1])
         early_rows = at("early_rows", [P, S + EARLY], U8, AT_HEAD + 6 * KB)
         late_rows = at("late_rows", [P, LATE], U8, AT_HEAD + 8 * KB)
@@ -114,11 +114,11 @@ def tile_list_dialogue_reply_ranker_kernel(tc, tab_words, tab_scales, offs, offs
             queue.dma_start(w4_raw[b][:].bitcast(I32), w4_rows[:, :, 2 * HALF * b:2 * HALF * (b + 1)].bitcast(I32))
 
         def deal_w4(b, t0, t1, offset):
-            dealt = at("w4_dealt%d%d" % (b, t0), [P, KP, 2 * P * (t1 - t0)], U8, offset)
-            nc.scalar.copy(dealt[:].bitcast(U16).rearrange("p a (t c i) -> p a c t i", t=t1 - t0, i=8),
+            dealt = at("w4_dealt%d%d" % (b, t0), [P, t1 - t0, KP, 2 * P], U8, offset)
+            nc.scalar.copy(dealt[:].bitcast(U16).rearrange("p t a (c i) -> p a c t i", i=8),
                            w4_raw[b][:].bitcast(U16).rearrange("p a (c i t) -> p a c t i", t=PACK, i=8)[:, :, :, t0:t1])
             for t in range(t0, t1):
-                w4_slice[PACK * b + t] = dealt[:, :, 2 * P * (t - t0):2 * P * (t - t0 + 1)]
+                w4_slice[PACK * b + t] = dealt[:, t - t0]
 
         wgs_rows = wgs.rearrange("(q t) j -> q t j", t=PACK)
 
@@ -137,9 +137,9 @@ def tile_list_dialogue_reply_ranker_kernel(tc, tab_words, tab_scales, offs, offs
             nc.sync.dma_start(pages[k][:], page_rows[ORDER[k] // PACK, ORDER[k] % PACK])
 
         first, rest = slice(0, QUARTER), slice(QUARTER, S)
-        load_table(0)
         nc.sync.dma_start(list1[:], offs)
         load_scale_rows(ts_win, tab_scales)
+        load_table(0)
         load_scale_rows(w4s_raw, w4_scales)
         load_w4(nc.sync, 0)
         load_table(1)
@@ -251,7 +251,7 @@ def tile_list_dialogue_reply_ranker_kernel(tc, tab_words, tab_scales, offs, offs
                     ahead = at("ahead%d" % i, [P, QUARTER], F32, AT_WVBF if i else AT_XBF + 4 * KB - HALF)
                     parts = [parts[0], (slice(HALF, HALF + QUARTER), parked[:, :QUARTER]), (slice(HALF + QUARTER, M), ahead[:])]
             else:
-                parts = [(slice(QUARTER * k, QUARTER * (k + 1)), x_row(i + 1 + k)[:, :QUARTER]) for k in range(2)]
+                parts = [(slice(QUARTER * k, QUARTER * (k + 1)), x_row(i + 1 + k)[:, P:P + QUARTER]) for k in range(2)]
                 parts.append((cols(1), x_f32[b][:, t + 1:, HALF:HALF + QUARTER]))
             for part, ge in parts:
                 gelu(i, part, ge)
@@ -282,8 +282,7 @@ def tile_list_dialogue_reply_ranker_kernel(tc, tab_words, tab_scales, offs, offs
         load_weights(nc.sync, 3, whole)
         load_page(4)
         w8_codes = at("w8_codes", [P, RP, N], U32, AT_W8)
-        w8_sc = at("w8_sc", [P, RP, N], U8, AT_W8 + 3 * KB)
-        nc.gpsimd.memset(w8_sc[:].bitcast(I32), 0)
+        w8_sc = w4_slice[0].rearrange("p a c -> p (a c)").rearrange("p (b c) -> p b c", b=RP)
         for q in QUADS:
             nc.sync.dma_start(w8_sc[32 * q:32 * q + 4, :, :].bitcast(I32),
                               w8_scales[:, 4 * q:4 * q + 4, :].rearrange("b r c -> r b c").bitcast(I32))
@@ -320,9 +319,12 @@ def tile_list_dialogue_reply_ranker_kernel(tc, tab_words, tab_scales, offs, offs
                 weave(nc.scalar.copy, z_bf, z_rows, 0, 1, 2, PACK)
 
         pair = (SLICES - 2, SLICES - 1)
-        for h in range(2):
-            for i in pair:
-                fetch(i, cols(h))
+        quarters = (first, slice(QUARTER, HALF))
+        for part in quarters:
+            fetch(6, part)
+        fetch(7, cols(0))
+        for i in pair:
+            fetch(i, cols(1))
         x_codes = {(0, 0): at("x_codes00", [P, HALF], U32, at_page(6) + 4 * KB),
                    (0, 1): at("x_codes01", [P, HALF], U32, at_page(6) + 6 * KB),
                    (1, 0): at("x_codes10", [P, HALF], U32, AT_V),
@@ -346,10 +348,12 @@ def tile_list_dialogue_reply_ranker_kernel(tc, tab_words, tab_scales, offs, offs
         def last_gain(i, h):
             gain(i, z_rows[1][:, i % PACK, cols(h)], ge[i, h][:])
 
-        last_gelu(6, 0)
+        for part in quarters:
+            gelu(6, part, ge[6, 0][:, part])
+        for part in quarters:
+            gain(6, z_rows[1][:, 2, part], ge[6, 0][:, part])
         last_gelu(7, 0)
-        last_gain(6, 0)
-        weave(nc.scalar.copy, x_bf, x_f32, 1, 0, 1, PACK, first)
+        weave(nc.scalar.copy, x_bf, x_f32, 1, 0, 1, PACK)
         last_gain(7, 0)
         last_gelu(6, 1)
         weave(nc.scalar.copy, z_bf, z_rows, 1, 0, 1, PACK)
@@ -359,7 +363,6 @@ def tile_list_dialogue_reply_ranker_kernel(tc, tab_words, tab_scales, offs, offs
         weave(nc.scalar.copy, z_bf, z_rows, 1, 1, 1, PACK)
 
         quantize(x_codes, x_sc, x_bf, 0, 0)
-        weave(nc.vector.tensor_copy, x_bf, x_f32, 1, 0, 1, PACK, slice(QUARTER, HALF))
         weave(nc.vector.tensor_copy, x_bf, x_f32, 1, 1, 1, PACK)
         quantize(x_codes, x_sc, x_bf, 1, 0)
         quantize(x_codes, x_sc, x_bf, 0, 1)

@@ -26,7 +26,7 @@ HALF = 512
 QUARTER = 256
 NT = N // P
 QUADS = (0, 2, 1, 3)
-EARLY = P
+EARLY = 2 * P
 LATE = H - EARLY
 ROWS0 = 48
 KB = 1024
@@ -79,11 +79,10 @@ def tile_list_dialogue_reply_ranker_kernel(tc, tab_words, tab_scales, offs, offs
         list3 = lists.tile([P, M // 16], U16)
 
         tabs = {}
-        ts_win = at("ts_win", [P, T], U8, AT_HEAD)
-        w4s_raw = at("w4s_raw", [P, H], U8, AT_V)
+        ts_win = at("ts_win", [P, T], U8, AT_V)
+        w4s_raw = at("w4s_raw", [P, H], U8, AT_HEAD + 4 * KB)
         ts_got = at("ts_got", [P, S], U8, AT_TABS[KP - 1])
         early_rows = at("early_rows", [P, S + EARLY], U8, AT_HEAD + 6 * KB)
-        late_rows = at("late_rows", [P, LATE], U8, AT_HEAD + 8 * KB)
         late_planes = at("late_planes", [P, KP, LATE], U8, AT_HEAD + 12 * KB)
         w4_raw = {0: at("w4_raw0", [P, KP, 2 * HALF], U8, AT_HEAD + 9 * KB)}
         w4_slice = {}
@@ -137,9 +136,9 @@ def tile_list_dialogue_reply_ranker_kernel(tc, tab_words, tab_scales, offs, offs
             nc.sync.dma_start(pages[k][:], page_rows[ORDER[k] // PACK, ORDER[k] % PACK])
 
         first, rest = slice(0, QUARTER), slice(QUARTER, S)
+        load_table(0)
         nc.sync.dma_start(list1[:], offs)
         load_scale_rows(ts_win, tab_scales)
-        load_table(0)
         load_scale_rows(w4s_raw, w4_scales)
         load_w4(nc.sync, 0)
         load_table(1)
@@ -150,20 +149,20 @@ def tile_list_dialogue_reply_ranker_kernel(tc, tab_words, tab_scales, offs, offs
 
         nc.vector.tensor_copy(ts_got[:], ts_win[:].indirect(list1[:]))
         as_given = w4s_raw[:].rearrange("p (b m t) -> p b t m", b=RP, t=PACK)
-        nc.vector.tensor_copy(early_rows[:, S:], as_given[:, 0, 0])
+        nc.vector.tensor_copy(early_rows[:, S:].rearrange("p (b m) -> p b m", b=RP), as_given[:, :, 0])
         nc.vector.tensor_copy(early_rows[:, :S].bitcast(I32), ts_got[:].bitcast(I32))
         move_scale_rows(nc.scalar, planes, early_rows, QUADS[:2])
         move_scale_rows(nc.sync, planes, early_rows, QUADS[2:])
         load_table(KP - 1)
-        by_slice = late_rows[:].rearrange("p (t m) -> p t m", m=P)
-        nc.vector.tensor_copy(by_slice[:, 0], as_given[:, 1, 0])
-        nc.vector.tensor_copy(by_slice[:, 1:].rearrange("p (b t) m -> p b t m", b=RP), as_given[:, :, 1:])
         deal_w4(0, 0, PACK, AT_W4)
 
         v_codes = [at("v_codes%d" % a, [P, S], U32, AT_V + 4 * KB * a) for a in range(KP)]
         first_parts = (first, slice(QUARTER, HALF), cols(1))
         for a in range(KP - 1):
             nc.vector.tensor_copy(v_codes[a][:], tabs[a][:].bitcast(U32).indirect(list1[:]))
+            if a == 0:
+                late_rows = at("late_rows", [P, LATE], U8, AT_W4_LATE + 3 * KB)
+                nc.vector.tensor_copy(late_rows[:].rearrange("p (b t m) -> p b t m", b=RP, m=P), as_given[:, :, 1:])
         for part in first_parts:
             nc.vector.tensor_copy(v_codes[KP - 1][:, part], tabs[KP - 1][:].bitcast(U32).indirect(entries(list1, part)))
 
@@ -194,6 +193,7 @@ def tile_list_dialogue_reply_ranker_kernel(tc, tab_words, tab_scales, offs, offs
         z_bf = {}
         for b in range(RP):
             for h in range(2):
+                x_bf[b, h] = at("x_bf%d%d" % (b, h), [P, HALF, PACK], BF16, AT_XBF + 4 * KB * (2 * b + h))
                 z_bf[b, h] = at("z_bf%d%d" % (b, h), [P, HALF, PACK], BF16, AT_ZBF + 4 * KB * (2 * b + h))
         staged = {}
 
@@ -247,26 +247,27 @@ def tile_list_dialogue_reply_ranker_kernel(tc, tab_words, tab_scales, offs, offs
             if i < SLICES - 3:
                 parked = at("parked%d" % i, [P, HALF], F32, staged_at(i + 3))
                 parts = [(cols(0), x_row(i + 1)[:, cols(0)]), (cols(1), parked[:])]
-                if i in (0, 3):
-                    ahead = at("ahead%d" % i, [P, QUARTER], F32, AT_WVBF if i else AT_XBF + 4 * KB - HALF)
+                if i == 3:
+                    ahead = at("ahead_of_wv", [P, QUARTER], F32, AT_WVBF)
                     parts = [parts[0], (slice(HALF, HALF + QUARTER), parked[:, :QUARTER]), (slice(HALF + QUARTER, M), ahead[:])]
             else:
                 parts = [(slice(QUARTER * k, QUARTER * (k + 1)), x_row(i + 1 + k)[:, P:P + QUARTER]) for k in range(2)]
                 parts.append((cols(1), x_f32[b][:, t + 1:, HALF:HALF + QUARTER]))
             for part, ge in parts:
                 gelu(i, part, ge)
-            for k, (part, ge) in enumerate(parts):
-                gain(i, z_bf[b, k][:, :, 0] if i == 1 else shaped(z_rows[b][:, t, part], ge), ge)
+            for part, ge in parts:
+                gain(i, shaped(z_rows[b][:, t, part], ge), ge)
 
-        def weave(copy, dst, src, b, h, t0, t1, part=slice(0, HALF)):
-            copy(dst[b, h][:, part, t0:t1].rearrange("p (c i) t -> p c t i", i=4),
-                 src[b][:, t0:t1, cols(h)][:, :, part].rearrange("p t (c i) -> p c t i", i=4))
+        def weave(copy, dst, src, b, h, part=slice(0, HALF), t0=0):
+            copy(dst[b, h][:, part, t0:].rearrange("p (c i) t -> p c t i", i=4),
+                 src[b][:, t0:, cols(h)][:, :, part].rearrange("p t (c i) -> p c t i", i=4))
 
         def weave_wv(wv_bf, b):
             nc.scalar.activation(
                 wv_bf[:, b * N * PACK:(b + 1) * N * PACK].rearrange("p (c i j) -> p c j i", i=4, j=PACK),
                 wv_raw[:, b].rearrange("p j (c i) -> p c j i", i=4), ACT.Copy, scale=0.5)
 
+        by_vector = ((0, slice(P, HALF)), (1, slice(0, HALF)))
         project(0)
         project(1)
         deal_w4(1, 1, PACK, AT_W4 + 3 * KB + 2 * P * KP - 64)
@@ -300,23 +301,19 @@ def tile_list_dialogue_reply_ranker_kernel(tc, tab_words, tab_scales, offs, offs
                 load_page(i + 1 + PACK)
             if i == 0:
                 nc.sync.dma_start(gin_rest, gin_cols[:, :, 1:])
-            if i < RP:
-                for h in range(2):
-                    x_bf[i, h] = at("x_bf%d%d" % (i, h), [P, HALF, PACK], BF16, AT_XBF + 4 * KB * (2 * i + h))
-                    nc.scalar.copy(x_bf[i, h][:, :, 0], x_row(i)[:, cols(h)])
-            if i == 2:
-                for h in range(2):
-                    weave(nc.scalar.copy, z_bf, z_rows, 0, h, 0, 2)
+            if i == 1:
+                for h, part in by_vector:
+                    nc.scalar.copy(x_bf[1, h][:, part, 0], x_row(i)[:, cols(h)][:, part])
             if i == 3:
                 wv_bf = at("wv_bf", [P, RP * N * PACK], BF16, AT_WVBF)
                 for b in range(RP):
                     weave_wv(wv_bf, b)
             if i == 4:
                 for h in range(2):
-                    weave(nc.scalar.copy, x_bf, x_f32, 0, h, 1, PACK)
-                weave(nc.scalar.copy, z_bf, z_rows, 0, 0, 2, PACK)
+                    weave(nc.scalar.copy, x_bf, x_f32, 0, h)
             if i == 5:
-                weave(nc.scalar.copy, z_bf, z_rows, 0, 1, 2, PACK)
+                for h in range(2):
+                    weave(nc.scalar.copy, z_bf, z_rows, 0, h)
 
         pair = (SLICES - 2, SLICES - 1)
         quarters = (first, slice(QUARTER, HALF))
@@ -339,7 +336,8 @@ def tile_list_dialogue_reply_ranker_kernel(tc, tab_words, tab_scales, offs, offs
             nc.vector.quantize_mx(out=codes[b, h][:].bitcast(FP8X4), scales=scales[:, b, cols(h)],
                                   in_=src[b, h][:].rearrange("p m t -> p (m t)"))
 
-        ge = {(i, h): at("ge%d%d" % (i, h), [P, HALF], F32, at_page(5) + 2 * KB * (2 * h + i % 2))
+        ge = {(i, h): at("ge%d%d" % (i, h), [P, HALF], F32,
+                         AT_TAIL if (i, h) == (7, 1) else at_page(5) + 2 * KB * (2 * h + i % 2))
               for h in range(2) for i in pair}
 
         def last_gelu(i, h):
@@ -353,17 +351,18 @@ def tile_list_dialogue_reply_ranker_kernel(tc, tab_words, tab_scales, offs, offs
         for part in quarters:
             gain(6, z_rows[1][:, 2, part], ge[6, 0][:, part])
         last_gelu(7, 0)
-        weave(nc.scalar.copy, x_bf, x_f32, 1, 0, 1, PACK)
+        weave(nc.scalar.copy, x_bf, x_f32, 1, 0, slice(0, P))
         last_gain(7, 0)
         last_gelu(6, 1)
-        weave(nc.scalar.copy, z_bf, z_rows, 1, 0, 1, PACK)
+        weave(nc.scalar.copy, z_bf, z_rows, 1, 0)
         last_gelu(7, 1)
         last_gain(6, 1)
         last_gain(7, 1)
-        weave(nc.scalar.copy, z_bf, z_rows, 1, 1, 1, PACK)
+        weave(nc.scalar.copy, z_bf, z_rows, 1, 1)
 
         quantize(x_codes, x_sc, x_bf, 0, 0)
-        weave(nc.vector.tensor_copy, x_bf, x_f32, 1, 1, 1, PACK)
+        for h, part in by_vector:
+            weave(nc.vector.tensor_copy, x_bf, x_f32, 1, h, part, 1)
         quantize(x_codes, x_sc, x_bf, 1, 0)
         quantize(x_codes, x_sc, x_bf, 0, 1)
         quantize(x_codes, x_sc, x_bf, 1, 1)
@@ -393,10 +392,11 @@ def tile_list_dialogue_reply_ranker_kernel(tc, tab_words, tab_scales, offs, offs
         for b in range(RP):
             for n, h in order:
                 gate_pass(gate[n, h], n, b, h)
+        th_all = at("th_all", [P, len(order), HALF], F32, AT_TAIL)
         th = {}
         for k, (n, h) in enumerate(order):
-            th[n, h] = at("th%d" % k, [P, HALF], F32, AT_TAIL + 2 * KB * k)
-            nc.scalar.activation(th[n, h][:], gate[n, h][:], ACT.Tanh, scale=0.5)
+            th[n, h] = th_all[:, k]
+            nc.scalar.activation(th[n, h], gate[n, h][:], ACT.Tanh, scale=0.5)
         for k, (n, h) in enumerate(order):
             value = bank((6 + k) % 8)
             for b in range(RP):

@@ -21,7 +21,7 @@ PACK = 4
 KP = K // (P * PACK)
 RP = H // (P * PACK)
 SLICES = RP * PACK
-ORDER = (0, 4, 1, 2, 3, 5, 6, 7)
+LAST = SLICES - 1
 HALF = 512
 QUARTER = 256
 NT = N // P
@@ -29,29 +29,36 @@ QUADS = (0, 2, 1, 3)
 EARLY = 2 * P
 LATE = H - EARLY
 ROWS0 = 48
+PAGES = 5
+X_BY_SCALAR = 48
 KB = 1024
+LAP = 256
 
-SHIFT = KB // 4
-AT_TABS = (4 * KB, 20 * KB + SHIFT, 36 * KB + SHIFT)
-AT_PAGES = (8 * KB, AT_TABS[2] + 64, AT_TABS[2] - 8 * KB + 64, 64, 8 * KB + 64)
-AT_WGS0 = 16 * KB + 64
-AT_W4_LATE = AT_TABS[0]
-AT_LATER = AT_TABS[2] + 16 * KB - 64
-AT_W8 = AT_TABS[2] + 28 * KB
-AT_WV = AT_TABS[2] + 32 * KB
-AT_V = 81 * KB
-AT_PLANES = 93 * KB
-AT_W4 = 98 * KB
-AT_XBF = 104 * KB
-AT_ZBF = 120 * KB
-AT_ZROWS = 136 * KB
-AT_X = 152 * KB
-AT_STAGED = 184 * KB
-AT_TAIL = 196 * KB
-AT_WVBF = 208 * KB
-AT_SC = 214 * KB
-AT_HEAD = 220 * KB
-AT_GAINS = 235 * KB
+AT_LATEST = 0
+AT_TAB1 = 16 * KB - LAP
+AT_WGS1 = 24 * KB
+AT_LATE_PLANES = 28 * KB
+AT_X0 = 30 * KB + LAP
+AT_TAB2 = 54 * KB
+AT_WGS2 = 62 * KB + LAP
+AT_W8 = 66 * KB + LAP
+AT_GAINS = 69 * KB + LAP
+AT_TAB0 = 78 * KB - LAP
+AT_PAGES = (AT_TAB0, 16 * KB, AT_TAB2 + LAP - 8 * KB, AT_TAB2 + LAP, AT_TAB0 - 8 * KB)
+AT_WVBF = AT_TAB0 + 8 * KB
+AT_V = AT_TAB0 + 16 * KB
+AT_PLANES = AT_V + 12 * KB
+AT_W4 = AT_PLANES + 4 * KB - LAP
+AT_W4_RAW = AT_W4 + 6 * KB
+AT_ROWS = AT_W4_RAW + 3 * KB
+AT_WGS0 = AT_ROWS + 2 * KB
+AT_STAGED = (AT_WGS0 + 12 * KB, AT_WGS0 + 4 * KB, AT_WGS0 + 8 * KB)
+AT_XBF = AT_WGS0 + 16 * KB
+AT_ZBF = AT_XBF + 16 * KB
+AT_X1 = AT_ZBF + 16 * KB
+AT_ZROWS = AT_X1 + 16 * KB
+AT_SC = AT_ZROWS + 14 * KB
+AT_CLK = AT_SC + 6 * KB
 
 
 def tile_list_dialogue_reply_ranker_kernel(tc, tab_words, tab_scales, offs, offs2, offs3, w4_words, w4_scales,
@@ -63,7 +70,7 @@ def tile_list_dialogue_reply_ranker_kernel(tc, tab_words, tab_scales, offs, offs
         psum = ctx.enter_context(tc.psum_pool(name="psum", bufs=1))
 
         def at(name, shape, dtype, offset):
-            return mem.tile(shape, dtype, name=name, align_bytes=64, offset=offset)
+            return mem.tile(shape, dtype, name=name, align_bytes=LAP, offset=offset)
 
         def bank(n):
             return psum.tile([P, HALF], F32, name="bank%d" % n)
@@ -77,145 +84,127 @@ def tile_list_dialogue_reply_ranker_kernel(tc, tab_words, tab_scales, offs, offs
         list1 = lists.tile([P, S // 16], U16)
         list2 = lists.tile([P, S // 16], U16)
         list3 = lists.tile([P, M // 16], U16)
+        whole = slice(0, S)
+        ramp = (slice(0, QUARTER), slice(QUARTER, HALF), cols(1))
 
-        tabs = {}
+        tab_rows = [tab_words[a].rearrange("p t i -> p (t i)").bitcast(I32) for a in range(KP)]
+        tabs = {0: at("tab0", [P, T], I32, AT_TAB0)}
         ts_win = at("ts_win", [P, T], U8, AT_V)
-        w4s_raw = at("w4s_raw", [P, H], U8, AT_HEAD + 4 * KB)
-        ts_got = at("ts_got", [P, S], U8, AT_TABS[KP - 1])
-        early_rows = at("early_rows", [P, S + EARLY], U8, AT_HEAD + 6 * KB)
-        late_planes = at("late_planes", [P, KP, LATE], U8, AT_HEAD + 12 * KB)
-        w4_raw = {0: at("w4_raw0", [P, KP, 2 * HALF], U8, AT_HEAD + 9 * KB)}
-        w4_slice = {}
+        w4s_raw = at("w4s_raw", [P, H], U8, AT_TAB2 + 2 * KB)
+        rows = at("rows", [P, S + H], U8, AT_ROWS)
         planes = at("planes", [P, KP, S + EARLY], U8, AT_PLANES)
-        weights = {}
-        wv_sc = at("wv_sc", [P, RP * N], U8, AT_SC + KB)
-        x_sc = at("x_sc", [P, RP, M], U8, AT_SC + 2 * KB)
-        z_sc = at("z_sc", [P, RP, M], U8, AT_SC + 4 * KB)
-
-        def load_table(a):
-            tabs[a] = at("tab%d" % a, [P, T], I32, AT_TABS[a])
-            nc.sync.dma_start(tabs[a][:], tab_words[a].rearrange("p t i -> p (t i)").bitcast(I32))
+        weights = {0: at("wgs0", [P, S], F32, AT_WGS0)[:]}
+        w4_raw = {0: at("w4_raw0", [P, KP, 2 * HALF], U8, AT_W4_RAW)}
+        w4_dealt = {}
 
         def load_scale_rows(tile, scales):
             nc.sync.dma_start(tile[ROWS0:2 * ROWS0, :].bitcast(I32), scales.rearrange("a q c -> q a c").bitcast(I32))
             nc.vector.memset(tile[0:ROWS0, :].bitcast(I32), 0)
             nc.vector.memset(tile[2 * ROWS0:P, :].bitcast(I32), 0)
 
-        def move_scale_rows(queue, dst, src, quads=QUADS):
+        def move_scale_rows(queue, dst, part, quads):
             for q in quads:
                 row = ROWS0 + 4 * KP * q
                 queue.dma_start(dst[32 * q:32 * q + 4].rearrange("p a c -> p (a c)").bitcast(I32),
-                                src[row:row + 4 * KP, :].bitcast(I32))
+                                rows[row:row + 4 * KP, part].bitcast(I32))
 
         w4_rows = w4_words.rearrange("a p c -> p a c")
 
-        def load_w4(queue, b):
-            queue.dma_start(w4_raw[b][:].bitcast(I32), w4_rows[:, :, 2 * HALF * b:2 * HALF * (b + 1)].bitcast(I32))
+        def load_w4(b):
+            nc.sync.dma_start(w4_raw[b][:].bitcast(I32), w4_rows[:, :, 2 * HALF * b:2 * HALF * (b + 1)].bitcast(I32))
 
-        def deal_w4(b, t0, t1, offset):
-            dealt = at("w4_dealt%d%d" % (b, t0), [P, t1 - t0, KP, 2 * P], U8, offset)
-            nc.scalar.copy(dealt[:].bitcast(U16).rearrange("p t a (c i) -> p a c t i", i=8),
-                           w4_raw[b][:].bitcast(U16).rearrange("p a (c i t) -> p a c t i", t=PACK, i=8)[:, :, :, t0:t1])
-            for t in range(t0, t1):
-                w4_slice[PACK * b + t] = dealt[:, t - t0]
+        def deal_w4(b):
+            w4_dealt[b] = at("w4_dealt%d" % b, [P, PACK, KP, 2 * P], U8, AT_W4 + 3 * KB * b)
+            nc.scalar.copy(w4_dealt[b][:].bitcast(U16).rearrange("p t a (c i) -> p a c t i", i=8),
+                           w4_raw[b][:].bitcast(U16).rearrange("p a (c i t) -> p a c t i", t=PACK, i=8))
 
         wgs_rows = wgs.rearrange("(q t) j -> q t j", t=PACK)
 
-        def load_weights(queue, t, part):
+        def load_weights(t):
             for q in QUADS:
-                queue.dma_start(weights[t][32 * q:32 * q + 32, part], wgs_rows[:, t, part])
+                nc.sync.dma_start(weights[t][32 * q:32 * q + 32, :], wgs_rows[:, t, :])
 
         page_rows = page0.rearrange("(b p t) c -> b t p c", p=P, t=PACK)
         pages = {}
 
-        def at_page(i):
-            return AT_PAGES[i if i <= PACK else i - PACK]
-
         def load_page(k):
-            pages[k] = at("page%d" % k, [P, T2], F32, at_page(k))
-            nc.sync.dma_start(pages[k][:], page_rows[ORDER[k] // PACK, ORDER[k] % PACK])
+            pages[k] = at("page%d" % k, [P, T2], F32, AT_PAGES[k % PAGES])
+            nc.sync.dma_start(pages[k][:], page_rows[k // PACK, k % PACK])
 
-        first, rest = slice(0, QUARTER), slice(QUARTER, S)
-        load_table(0)
+        nc.sync.dma_start(tabs[0][:, :T // 2], tab_rows[0][:, :T // 2])
         nc.sync.dma_start(list1[:], offs)
         load_scale_rows(ts_win, tab_scales)
         load_scale_rows(w4s_raw, w4_scales)
-        load_w4(nc.sync, 0)
-        load_table(1)
+        nc.sync.dma_start(tabs[0][:, T // 2:], tab_rows[0][:, T // 2:])
+        nc.sync.dma_start(weights[0][0:32, :], wgs_rows[:, 0, :])
+        load_w4(0)
+        tabs[1] = at("tab1", [P, T], I32, AT_TAB1)
+        nc.sync.dma_start(tabs[1][:], tab_rows[1])
         nc.sync.dma_start(list2[:], offs2)
         nc.sync.dma_start(list3[:], offs3)
         nc.vector.memset(planes[:].bitcast(I32), 0)
-        nc.vector.memset(late_planes[:].bitcast(I32), 0)
 
+        nc.vector.tensor_copy(rows[:, S:].rearrange("p (b t m) -> p b t m", b=RP, t=PACK),
+                              w4s_raw[:].rearrange("p (b m t) -> p b t m", b=RP, t=PACK))
+        ts_got = at("ts_got", [P, S], U8, AT_TAB2 + 2 * KB)
         nc.vector.tensor_copy(ts_got[:], ts_win[:].indirect(list1[:]))
-        as_given = w4s_raw[:].rearrange("p (b m t) -> p b t m", b=RP, t=PACK)
-        nc.vector.tensor_copy(early_rows[:, S:].rearrange("p (b m) -> p b m", b=RP), as_given[:, :, 0])
-        nc.vector.tensor_copy(early_rows[:, :S].bitcast(I32), ts_got[:].bitcast(I32))
-        move_scale_rows(nc.scalar, planes, early_rows, QUADS[:2])
-        move_scale_rows(nc.sync, planes, early_rows, QUADS[2:])
-        load_table(KP - 1)
-        deal_w4(0, 0, PACK, AT_W4)
+        nc.vector.tensor_copy(rows[:, :S].bitcast(I32), ts_got[:].bitcast(I32))
+        move_scale_rows(nc.scalar, planes, slice(0, S + EARLY), QUADS[:2])
+        move_scale_rows(nc.sync, planes, slice(0, S + EARLY), QUADS[2:])
+        tabs[2] = at("tab2", [P, T], I32, AT_TAB2)
+        nc.sync.dma_start(tabs[2][:], tab_rows[2])
+        deal_w4(0)
 
         v_codes = [at("v_codes%d" % a, [P, S], U32, AT_V + 4 * KB * a) for a in range(KP)]
-        first_parts = (first, slice(QUARTER, HALF), cols(1))
-        for a in range(KP - 1):
-            nc.vector.tensor_copy(v_codes[a][:], tabs[a][:].bitcast(U32).indirect(list1[:]))
-            if a == 0:
-                late_rows = at("late_rows", [P, LATE], U8, AT_W4_LATE + 3 * KB)
-                nc.vector.tensor_copy(late_rows[:].rearrange("p (b t m) -> p b t m", b=RP, m=P), as_given[:, :, 1:])
-        for part in first_parts:
-            nc.vector.tensor_copy(v_codes[KP - 1][:, part], tabs[KP - 1][:].bitcast(U32).indirect(entries(list1, part)))
 
-        whole = slice(0, S)
-        weights[0] = at("wgs0", [P, S], F32, AT_WGS0)[:]
-        load_weights(nc.sync, 0, first)
+        def look_up(a, part):
+            nc.vector.tensor_copy(v_codes[a][:, part], tabs[a][:].bitcast(U32).indirect(entries(list1, part)))
+
+        look_up(0, whole)
+        nc.vector.tensor_copy(weights[0][32:64, :].bitcast(I32), weights[0][0:32, :].bitcast(I32))
+        nc.vector.tensor_copy(weights[0][64:128, :].bitcast(I32), weights[0][0:64, :].bitcast(I32))
+        look_up(1, whole)
+        late_planes = at("late_planes", [P, KP, LATE], U8, AT_LATE_PLANES)
+        nc.vector.memset(late_planes[:].bitcast(I32), 0)
+        for part in ramp:
+            look_up(2, part)
+
         load_page(0)
-        load_weights(nc.sync, 0, rest)
-        w4_raw[1] = at("w4_raw1", [P, KP, 2 * HALF], U8, AT_W4_LATE)
-        load_w4(nc.sync, 1)
-        move_scale_rows(nc.sync, late_planes, late_rows)
-        later = at("later", [P, (PACK - 1) * S + RP * PACK], F32, AT_LATER)
-        gin_first = later[:, (PACK - 1) * S:(PACK - 1) * S + RP]
-        gin_cols = gin.rearrange("(b p t) -> p b t", p=P, t=PACK)
-        for i in range(1, PACK):
-            weights[i] = later[:, S * (i - 1):S * i]
         load_page(1)
-        load_weights(nc.sync, 1, whole)
+        weights[1] = at("wgs1", [P, S], F32, AT_WGS1)[:]
+        load_weights(1)
+        move_scale_rows(nc.sync, late_planes, slice(S + EARLY, S + H), QUADS)
+        w4_raw[1] = at("w4_raw1", [P, KP, 2 * HALF], U8, AT_X0)
+        load_w4(1)
         load_page(2)
-        with nc.allow_non_contiguous_dma(reason="one gain a partition and pass"):
-            nc.sync.dma_start(gin_first, gin_cols[:, :, 0])
-        load_weights(nc.sync, 2, whole)
-        deal_w4(1, 0, 1, AT_W4 + 3 * KB)
+        weights[2] = at("wgs2", [P, S], F32, AT_WGS2)[:]
+        load_weights(2)
+        gains = at("gains", [P, 2, RP, PACK], F32, AT_GAINS)
+        nc.sync.dma_start(gains[:, 0], gin.rearrange("(b p t) -> p b t", p=P, t=PACK))
+        load_page(3)
+        latest = at("latest", [P, S + RP * PACK * N], F32, AT_LATEST)
+        weights[3] = latest[:, :S]
+        load_weights(3)
+        load_page(4)
+        nc.sync.dma_start(gains[:, 1], gout.rearrange("(b p t) -> p b t", p=P, t=PACK))
 
-        x_f32 = [at("x_f32_%d" % b, [P, PACK, M], F32, AT_X + 16 * KB * b) for b in range(RP)]
-        z_rows = [at("z_rows%d" % b, [P, PACK, M], BF16, AT_ZROWS + 8 * KB * b) for b in range(RP)]
-        x_bf = {}
-        z_bf = {}
-        for b in range(RP):
-            for h in range(2):
-                x_bf[b, h] = at("x_bf%d%d" % (b, h), [P, HALF, PACK], BF16, AT_XBF + 4 * KB * (2 * b + h))
-                z_bf[b, h] = at("z_bf%d%d" % (b, h), [P, HALF, PACK], BF16, AT_ZBF + 4 * KB * (2 * b + h))
+        x_f32 = [at("x_f32_%d" % b, [P, PACK * M], F32, (AT_X0, AT_X1)[b]) for b in range(RP)]
+        z_rows = at("z_rows", [P, LAST, M], BF16, AT_ZROWS)
         staged = {}
 
-        def staged_at(i):
-            return AT_STAGED + 4 * KB * (i % 3)
-
         def x_row(i):
-            return x_f32[ORDER[i] // PACK][:, ORDER[i] % PACK]
+            return x_f32[i // PACK][:, M * (i % PACK):M * (i % PACK + 1)]
 
         def project(i):
-            staged[i] = at("staged%d" % i, [P, S], F32, staged_at(i) if i else AT_WV - 2 * KB)
-            if i == 0:
-                groups = zip(first_parts, (7, 6, 5))
-            else:
-                groups = zip((cols(0), cols(1)), (7 - (2 * i + 1) % 3, 7 - (2 * i + 2) % 3))
+            staged[i] = at("staged%d" % i, [P, S], F32, AT_STAGED[i % 3])
+            groups = zip(ramp, range(3)) if i == 0 else zip((cols(0), cols(1)), ((2 * i + 1) % 8, (2 * i + 2) % 8))
             for part, n in groups:
                 acc = bank(n)
                 width = part.stop - part.start
                 for a in range(KP):
                     nc.tensor.matmul_mx(
                         out=acc[:, :width],
-                        lhsT=w4_slice[ORDER[i]][:, a].bitcast(FP4X4),
+                        lhsT=w4_dealt[i // PACK][:, i % PACK, a].bitcast(FP4X4),
                         lhsT_scale=(planes[:, a, S + P * i:S + P * (i + 1)] if P * i < EARLY
                                     else late_planes[:, a, P * i - EARLY:P * (i + 1) - EARLY]),
                         rhs=v_codes[a][:, part].bitcast(FP8X4),
@@ -224,185 +213,155 @@ def tile_list_dialogue_reply_ranker_kernel(tc, tab_words, tab_scales, offs, offs
                 nc.scalar.copy(staged[i][:, part], acc[:, :width])
 
         def scatter(i):
-            for part in (first, rest) if i == 0 else (whole,):
+            for part in (cols(0), cols(1)) if i == 0 else (whole,):
                 nc.vector.tensor_tensor(pages[i][:].indirect(entries(list2, part)), staged[i][:, part],
-                                        weights[ORDER[i] % PACK][:, part], ALU.mult)
+                                        weights[i % PACK][:, part], ALU.mult)
 
         def fetch(i, part):
             nc.vector.tensor_copy(x_row(i)[:, part], pages[i][:].indirect(entries(list3, part)))
 
-        def shaped(row, like):
-            return row if like.ndim == 2 else row.rearrange("p (r c) -> p r c", r=like.shape[1])
-
         def gelu(i, part, ge):
-            b, t = divmod(ORDER[i], PACK)
-            nc.scalar.activation(ge, shaped(x_row(i)[:, part], ge), ACT.Gelu_apprx_tanh, scale=gin_rest[:, b, t - 1:t] if t else gin_first[:, b:b + 1])
+            b, t = divmod(i, PACK)
+            nc.scalar.activation(ge, x_row(i)[:, part], ACT.Gelu_apprx_tanh, scale=gains[:, 0, b, t:t + 1])
 
         def gain(i, dst, ge):
-            b, t = divmod(ORDER[i], PACK)
-            nc.scalar.activation(dst, ge, ACT.Copy, scale=gout_t[:, b, t:t + 1])
+            b, t = divmod(i, PACK)
+            nc.scalar.activation(dst, ge, ACT.Copy, scale=gains[:, 1, b, t:t + 1])
 
         def make_z(i):
-            b, t = divmod(ORDER[i], PACK)
-            if i < SLICES - 3:
-                parked = at("parked%d" % i, [P, HALF], F32, staged_at(i + 3))
-                parts = [(cols(0), x_row(i + 1)[:, cols(0)]), (cols(1), parked[:])]
-                if i == 3:
-                    ahead = at("ahead_of_wv", [P, QUARTER], F32, AT_WVBF)
-                    parts = [parts[0], (slice(HALF, HALF + QUARTER), parked[:, :QUARTER]), (slice(HALF + QUARTER, M), ahead[:])]
+            if i + 3 < SLICES:
+                shift = 3 * KB if i == PACK - 1 else 0
+                parked = at("parked%d" % i, [P, HALF], F32, AT_STAGED[i % 3] + shift)
+                parts = [(cols(1), parked[:]), (cols(0), x_row(i + 1)[:, cols(0)])]
+                if i == PACK - 1:
+                    parts = [(ramp[0], latest[:, S:S + QUARTER]), parts[0], (ramp[1], x_row(i + 1)[:, ramp[0]])]
+                if i == PACK:
+                    parts[1] = (cols(0), x_f32[1][:, 2 * M - QUARTER:2 * M + QUARTER])
             else:
-                parts = [(slice(QUARTER * k, QUARTER * (k + 1)), x_row(i + 1 + k)[:, P:P + QUARTER]) for k in range(2)]
-                parts.append((cols(1), x_f32[b][:, t + 1:, HALF:HALF + QUARTER]))
+                ge_row = at("ge%d" % i, [P, M], F32, AT_XBF + 8 * KB + 4 * KB * (LAST - 1 - i))
+                parts = [(cols(h), ge_row[:, cols(h)]) for h in range(2)]
             for part, ge in parts:
                 gelu(i, part, ge)
             for part, ge in parts:
-                gain(i, shaped(z_rows[b][:, t, part], ge), ge)
+                gain(i, z_rows[:, i, part], ge)
 
-        def weave(copy, dst, src, b, h, part=slice(0, HALF), t0=0):
-            copy(dst[b, h][:, part, t0:].rearrange("p (c i) t -> p c t i", i=4),
-                 src[b][:, t0:, cols(h)][:, :, part].rearrange("p t (c i) -> p c t i", i=4))
+        def weave(copy, dst, src):
+            copy(dst.rearrange("p (c i) t -> p c t i", i=4), src.rearrange("p t (c i) -> p c t i", i=4))
 
-        def weave_wv(wv_bf, b):
-            nc.scalar.activation(
-                wv_bf[:, b * N * PACK:(b + 1) * N * PACK].rearrange("p (c i j) -> p c j i", i=4, j=PACK),
-                wv_raw[:, b].rearrange("p j (c i) -> p c j i", i=4), ACT.Copy, scale=0.5)
+        def x_rows(b):
+            return x_f32[b][:].rearrange("p (t m) -> p t m", t=PACK)
 
-        by_vector = ((0, slice(P, HALF)), (1, slice(0, HALF)))
         project(0)
         project(1)
-        deal_w4(1, 1, PACK, AT_W4 + 3 * KB + 2 * P * KP - 64)
-        scatter(0)
         project(2)
-        fetch(0, whole)
-        latest = at("latest", [P, RP * PACK * (N + 2)], F32, AT_WV)
-        gout_t = latest[:, :RP * PACK].rearrange("p (b t) -> p b t", t=PACK)
-        gin_rest = latest[:, RP * PACK:RP * (2 * PACK - 1)].rearrange("p (b t) -> p b t", b=RP)
-        wv_raw = latest[:, 2 * RP * PACK:].rearrange("p (b j n) -> p b j n", b=RP, j=PACK)
-        load_page(3)
-        nc.sync.dma_start(gout_t, gout.rearrange("(b p t) -> p b t", p=P, t=PACK))
-        load_weights(nc.sync, 3, whole)
-        load_page(4)
+        deal_w4(1)
         w8_codes = at("w8_codes", [P, RP, N], U32, AT_W8)
-        w8_sc = w4_slice[0].rearrange("p a c -> p (a c)").rearrange("p (b c) -> p b c", b=RP)
+        w8_sc = w4_dealt[0][:, 0].rearrange("p a c -> p (a c)").rearrange("p (b c) -> p b c", b=RP)
         for q in QUADS:
             nc.sync.dma_start(w8_sc[32 * q:32 * q + 4, :, :].bitcast(I32),
                               w8_scales[:, 4 * q:4 * q + 4, :].rearrange("b r c -> r b c").bitcast(I32))
         nc.sync.dma_start(w8_codes[:].bitcast(I32), w8_words.rearrange("b p c i -> p b (c i)").bitcast(I32))
+        wv_raw = latest[:, S:].rearrange("p (b j n) -> p b j n", b=RP, j=PACK)
         nc.sync.dma_start(wv_raw, wv.rearrange("(b p j) n -> p b j n", p=P, j=PACK))
-        scatter(1)
+
+        x_bf = {}
+        z_bf = {}
+        scatter(0)
         for i in range(SLICES - 2):
-            scatter(i + 2)
+            scatter(i + 1)
+            fetch(i, whole)
+            if i + PAGES < SLICES:
+                load_page(i + PAGES)
+            if i == SLICES - 3:
+                fetch(i + 1, whole)
             make_z(i)
             if i + 3 < SLICES:
                 project(i + 3)
-            if i + 1 < SLICES - 2:
-                fetch(i + 1, whole)
-            if i + 1 < PACK:
-                load_page(i + 1 + PACK)
-            if i == 0:
-                nc.sync.dma_start(gin_rest, gin_cols[:, :, 1:])
             if i == 1:
-                for h, part in by_vector:
-                    nc.scalar.copy(x_bf[1, h][:, part, 0], x_row(i)[:, cols(h)][:, part])
-            if i == 3:
                 wv_bf = at("wv_bf", [P, RP * N * PACK], BF16, AT_WVBF)
                 for b in range(RP):
-                    weave_wv(wv_bf, b)
-            if i == 4:
+                    nc.scalar.activation(
+                        wv_bf[:, b * N * PACK:(b + 1) * N * PACK].rearrange("p (c i j) -> p c j i", i=4, j=PACK),
+                        wv_raw[:, b].rearrange("p j (c i) -> p c j i", i=4), ACT.Copy, scale=0.5)
+            if i == PACK - 1:
+                x_bf[0] = at("x_bf0", [P, M, PACK], BF16, AT_XBF)
                 for h in range(2):
-                    weave(nc.scalar.copy, x_bf, x_f32, 0, h)
-            if i == 5:
+                    weave(nc.scalar.copy, x_bf[0][:, cols(h)], x_rows(0)[:, :, cols(h)])
+            if i == PACK:
+                z_bf[0] = at("z_bf0", [P, M, PACK], BF16, AT_ZBF)
                 for h in range(2):
-                    weave(nc.scalar.copy, z_bf, z_rows, 0, h)
+                    weave(nc.scalar.copy, z_bf[0][:, cols(h)], z_rows[:, :PACK, cols(h)])
+        make_z(LAST - 1)
+        for h in range(2):
+            x_bf[1, h] = at("x_bf1%d" % h, [P, HALF, PACK], BF16, AT_XBF + 8 * KB + 4 * KB * h)
+            z_bf[1, h] = at("z_bf1%d" % h, [P, HALF, PACK], BF16, AT_ZBF + 8 * KB + 4 * KB * h)
+            weave(nc.scalar.copy, z_bf[1, h][:, :, :PACK - 1], z_rows[:, PACK:, cols(h)])
+        scatter(LAST)
 
-        pair = (SLICES - 2, SLICES - 1)
-        quarters = (first, slice(QUARTER, HALF))
-        for part in quarters:
-            fetch(6, part)
-        fetch(7, cols(0))
-        for i in pair:
-            fetch(i, cols(1))
-        x_codes = {(0, 0): at("x_codes00", [P, HALF], U32, at_page(6) + 4 * KB),
-                   (0, 1): at("x_codes01", [P, HALF], U32, at_page(6) + 6 * KB),
-                   (1, 0): at("x_codes10", [P, HALF], U32, AT_V),
-                   (1, 1): at("x_codes11", [P, HALF], U32, AT_V + 2 * KB)}
-        z_codes = {(0, 0): at("z_codes00", [P, HALF], U32, at_page(6)),
-                   (0, 1): at("z_codes01", [P, HALF], U32, at_page(6) + 2 * KB),
-                   (1, 0): at("z_codes10", [P, HALF], U32, AT_V + 4 * KB),
-                   (1, 1): at("z_codes11", [P, HALF], U32, AT_V + 6 * KB)}
-        wv_codes = at("wv_codes", [P, RP * N], U32, at_page(7))
+        x_codes = [at("x_codes%d" % b, [P, M], U32, AT_LATEST + 8 * KB * b) for b in range(RP)]
+        z_codes = [at("z_codes%d" % b, [P, M], U32, AT_LATEST + 8 * KB * b + 4 * KB) for b in range(RP)]
+        wv_codes = at("wv_codes", [P, RP * N], U32, AT_PAGES[(LAST - 1) % PAGES])
+        x_sc = at("x_sc", [P, RP, M], U8, AT_SC)
+        z_sc = at("z_sc", [P, RP, M], U8, AT_SC + 2 * KB)
+        wv_sc = at("wv_sc", [P, RP * N], U8, AT_SC + 4 * KB)
 
-        def quantize(codes, scales, src, b, h):
-            nc.vector.quantize_mx(out=codes[b, h][:].bitcast(FP8X4), scales=scales[:, b, cols(h)],
-                                  in_=src[b, h][:].rearrange("p m t -> p (m t)"))
+        def quantize(codes, scales, src):
+            nc.vector.quantize_mx(out=codes.bitcast(FP8X4), scales=scales, in_=src.rearrange("p m t -> p (m t)"))
 
-        ge = {(i, h): at("ge%d%d" % (i, h), [P, HALF], F32,
-                         AT_TAIL if (i, h) == (7, 1) else at_page(5) + 2 * KB * (2 * h + i % 2))
-              for h in range(2) for i in pair}
-
-        def last_gelu(i, h):
-            gelu(i, cols(h), ge[i, h][:])
-
-        def last_gain(i, h):
-            gain(i, z_rows[1][:, i % PACK, cols(h)], ge[i, h][:])
-
-        for part in quarters:
-            gelu(6, part, ge[6, 0][:, part])
-        for part in quarters:
-            gain(6, z_rows[1][:, 2, part], ge[6, 0][:, part])
-        last_gelu(7, 0)
-        weave(nc.scalar.copy, x_bf, x_f32, 1, 0, slice(0, P))
-        last_gain(7, 0)
-        last_gelu(6, 1)
-        weave(nc.scalar.copy, z_bf, z_rows, 1, 0)
-        last_gelu(7, 1)
-        last_gain(6, 1)
-        last_gain(7, 1)
-        weave(nc.scalar.copy, z_bf, z_rows, 1, 1)
-
-        quantize(x_codes, x_sc, x_bf, 0, 0)
-        for h, part in by_vector:
-            weave(nc.vector.tensor_copy, x_bf, x_f32, 1, h, part, 1)
-        quantize(x_codes, x_sc, x_bf, 1, 0)
-        quantize(x_codes, x_sc, x_bf, 0, 1)
-        quantize(x_codes, x_sc, x_bf, 1, 1)
-        for b in range(RP):
+        def quantize_wv(b):
             nc.vector.quantize_mx(out=wv_codes[:, b * N:(b + 1) * N].bitcast(FP8X4), scales=wv_sc[:, b * N:(b + 1) * N],
                                   in_=wv_bf[:, b * N * PACK:(b + 1) * N * PACK])
-        for b in range(RP):
-            for h in range(2):
-                quantize(z_codes, z_sc, z_bf, b, h)
+
+        quantize_wv(0)
+        for part in ramp:
+            fetch(LAST, part)
+        ge_last = at("ge_last", [P, M], F32, AT_ZROWS)
+        for part in ramp[:2]:
+            weave(nc.scalar.copy, x_bf[1, 0][:, part], x_rows(1)[:, :, part])
+        weave(nc.scalar.copy, x_bf[1, 1][:, :X_BY_SCALAR], x_rows(1)[:, :, HALF:HALF + X_BY_SCALAR])
+        for h in range(2):
+            gelu(LAST, cols(h), ge_last[:, cols(h)])
+        for h in range(2):
+            gain(LAST, z_bf[1, h][:, :, PACK - 1], ge_last[:, cols(h)])
+
+        quantize(x_codes[0][:], x_sc[:, 0], x_bf[0][:])
+        weave(nc.vector.tensor_copy, x_bf[1, 1][:, X_BY_SCALAR:], x_rows(1)[:, :, HALF + X_BY_SCALAR:])
+        quantize(x_codes[1][:, cols(0)], x_sc[:, 1, cols(0)], x_bf[1, 0][:])
+        quantize_wv(1)
+        quantize(x_codes[1][:, cols(1)], x_sc[:, 1, cols(1)], x_bf[1, 1][:])
+        quantize(z_codes[0][:], z_sc[:, 0], z_bf[0][:])
+        for h in range(2):
+            quantize(z_codes[1][:, cols(h)], z_sc[:, 1, cols(h)], z_bf[1, h][:])
 
         def gate_pass(acc, n, b, h):
             nc.tensor.matmul_mx(out=acc[:], lhsT=w8_codes[:, b, P * n:P * (n + 1)].bitcast(FP8X4),
                                 lhsT_scale=w8_sc[:, b, P * n:P * (n + 1)],
-                                rhs=x_codes[b, h][:].bitcast(FP8X4), rhs_scale=x_sc[:, b, cols(h)],
+                                rhs=x_codes[b][:, cols(h)].bitcast(FP8X4), rhs_scale=x_sc[:, b, cols(h)],
                                 start=(b == 0), stop=(b == RP - 1))
 
         def value_pass(acc, n, b, h):
             c0 = b * N + P * n
             nc.tensor.matmul_mx(out=acc[:], lhsT=wv_codes[:, c0:c0 + P].bitcast(FP8X4), lhsT_scale=wv_sc[:, c0:c0 + P],
-                                rhs=z_codes[b, h][:].bitcast(FP8X4), rhs_scale=z_sc[:, b, cols(h)],
+                                rhs=z_codes[b][:, cols(h)].bitcast(FP8X4), rhs_scale=z_sc[:, b, cols(h)],
                                 start=(b == 0), stop=(b == RP - 1))
 
         order = [(n, h) for h in range(2) for n in range(NT)]
         gate = {}
         for k, (n, h) in enumerate(order):
-            gate[n, h] = bank(k)
+            gate[n, h] = bank(1 + k)
         for b in range(RP):
             for n, h in order:
                 gate_pass(gate[n, h], n, b, h)
-        th_all = at("th_all", [P, len(order), HALF], F32, AT_TAIL)
-        th = {}
+        th_all = at("th_all", [P, len(order), HALF], F32, AT_ZROWS)
         for k, (n, h) in enumerate(order):
-            th[n, h] = th_all[:, k]
-            nc.scalar.activation(th[n, h], gate[n, h][:], ACT.Tanh, scale=0.5)
+            for part in ramp[:2] if k == len(order) - 1 else (cols(0),):
+                nc.scalar.activation(th_all[:, k, part], gate[n, h][:, part], ACT.Tanh, scale=0.5)
         for k, (n, h) in enumerate(order):
-            value = bank((6 + k) % 8)
+            value = bank((7 + k) % 8)
             for b in range(RP):
                 value_pass(value, n, b, h)
-            res = at("res%d" % k, [P, HALF], F32, AT_LATER + 2 * KB * k)
-            for part in (first, slice(QUARTER, HALF)) if k == len(order) - 1 else (cols(0),):
-                nc.vector.scalar_tensor_tensor(out=res[:, part], in0=th[n, h][:, part], scalar=1.0, in1=value[:, part],
+            res = at("res%d" % k, [P, HALF], F32, AT_PAGES[3] + 2 * KB * k)
+            for part in ramp[:2] if k == len(order) - 1 else (cols(0),):
+                nc.vector.scalar_tensor_tensor(out=res[:, part], in0=th_all[:, k, part], scalar=1.0, in1=value[:, part],
                                                op0=ALU.add, op1=ALU.mult)
                 nc.sync.dma_start(out[P * n:P * (n + 1), cols(h)][:, part], res[:, part])

@@ -30,7 +30,7 @@ EARLY = 2 * P
 LATE = H - EARLY
 ROWS0 = 48
 PAGES = 5
-X_BY_SCALAR = 48
+X_BY_SCALAR = 32
 KB = 1024
 LAP = 256
 
@@ -86,6 +86,7 @@ def tile_list_dialogue_reply_ranker_kernel(tc, tab_words, tab_scales, offs, offs
         list3 = lists.tile([P, M // 16], U16)
         whole = slice(0, S)
         ramp = (slice(0, QUARTER), slice(QUARTER, HALF), cols(1))
+        opening = (slice(0, QUARTER), slice(QUARTER, S - QUARTER), slice(S - QUARTER, S))
 
         tab_rows = [tab_words[a].rearrange("p t i -> p (t i)").bitcast(I32) for a in range(KP)]
         tabs = {0: at("tab0", [P, T], I32, AT_TAB0)}
@@ -166,7 +167,7 @@ def tile_list_dialogue_reply_ranker_kernel(tc, tab_words, tab_scales, offs, offs
         look_up(1, whole)
         late_planes = at("late_planes", [P, KP, LATE], U8, AT_LATE_PLANES)
         nc.vector.memset(late_planes[:].bitcast(I32), 0)
-        for part in ramp:
+        for part in opening:
             look_up(2, part)
 
         load_page(0)
@@ -197,7 +198,7 @@ def tile_list_dialogue_reply_ranker_kernel(tc, tab_words, tab_scales, offs, offs
 
         def project(i):
             staged[i] = at("staged%d" % i, [P, S], F32, AT_STAGED[i % 3])
-            groups = zip(ramp, range(3)) if i == 0 else zip((cols(0), cols(1)), ((2 * i + 1) % 8, (2 * i + 2) % 8))
+            groups = zip(opening, range(3)) if i == 0 else zip((cols(0), cols(1)), ((2 * i + 1) % 8, (2 * i + 2) % 8))
             for part, n in groups:
                 acc = bank(n)
                 width = part.stop - part.start
@@ -213,7 +214,7 @@ def tile_list_dialogue_reply_ranker_kernel(tc, tab_words, tab_scales, offs, offs
                 nc.scalar.copy(staged[i][:, part], acc[:, :width])
 
         def scatter(i):
-            for part in (cols(0), cols(1)) if i == 0 else (whole,):
+            for part in (ramp[0], slice(QUARTER, S)) if i == 0 else (whole,):
                 nc.vector.tensor_tensor(pages[i][:].indirect(entries(list2, part)), staged[i][:, part],
                                         weights[i % PACK][:, part], ALU.mult)
 
@@ -298,9 +299,15 @@ def tile_list_dialogue_reply_ranker_kernel(tc, tab_words, tab_scales, offs, offs
             weave(nc.scalar.copy, z_bf[1, h][:, :, :PACK - 1], z_rows[:, PACK:, cols(h)])
         scatter(LAST)
 
-        x_codes = [at("x_codes%d" % b, [P, M], U32, AT_LATEST + 8 * KB * b) for b in range(RP)]
-        z_codes = [at("z_codes%d" % b, [P, M], U32, AT_LATEST + 8 * KB * b + 4 * KB) for b in range(RP)]
-        wv_codes = at("wv_codes", [P, RP * N], U32, AT_PAGES[(LAST - 1) % PAGES])
+        x_codes = {}
+        z_codes = {}
+        for b in range(RP):
+            for h in range(2):
+                x_codes[b, h] = at("x_codes%d%d" % (b, h), [P, HALF], U32,
+                                   AT_LATEST + 2 * KB * (2 * b + h) if b + h else AT_PAGES[(LAST - 1) % PAGES])
+                z_codes[b, h] = at("z_codes%d%d" % (b, h), [P, HALF], U32,
+                                   AT_ZROWS + 12 * KB if (b, h) == (0, 1) else AT_LATEST + 8 * KB + 2 * KB * (2 * b + h))
+        wv_codes = at("wv_codes", [P, RP * N], U32, AT_STAGED[LAST % 3])
         x_sc = at("x_sc", [P, RP, M], U8, AT_SC)
         z_sc = at("z_sc", [P, RP, M], U8, AT_SC + 2 * KB)
         wv_sc = at("wv_sc", [P, RP * N], U8, AT_SC + 4 * KB)
@@ -312,37 +319,39 @@ def tile_list_dialogue_reply_ranker_kernel(tc, tab_words, tab_scales, offs, offs
             nc.vector.quantize_mx(out=wv_codes[:, b * N:(b + 1) * N].bitcast(FP8X4), scales=wv_sc[:, b * N:(b + 1) * N],
                                   in_=wv_bf[:, b * N * PACK:(b + 1) * N * PACK])
 
-        quantize_wv(0)
+        quantize(x_codes[0, 0][:], x_sc[:, 0, cols(0)], x_bf[0][:, cols(0)])
         for part in ramp:
             fetch(LAST, part)
-        ge_last = at("ge_last", [P, M], F32, AT_ZROWS)
+        ge_last = [at("ge_last%d" % h, [P, HALF], F32, AT_ZROWS + 12 * KB * (1 - h)) for h in range(2)]
         for part in ramp[:2]:
             weave(nc.scalar.copy, x_bf[1, 0][:, part], x_rows(1)[:, :, part])
         weave(nc.scalar.copy, x_bf[1, 1][:, :X_BY_SCALAR], x_rows(1)[:, :, HALF:HALF + X_BY_SCALAR])
         for h in range(2):
-            gelu(LAST, cols(h), ge_last[:, cols(h)])
+            gelu(LAST, cols(h), ge_last[h][:])
         for h in range(2):
-            gain(LAST, z_bf[1, h][:, :, PACK - 1], ge_last[:, cols(h)])
+            gain(LAST, z_bf[1, h][:, :, PACK - 1], ge_last[h][:])
 
-        quantize(x_codes[0][:], x_sc[:, 0], x_bf[0][:])
+        quantize(x_codes[0, 1][:], x_sc[:, 0, cols(1)], x_bf[0][:, cols(1)])
+        for b in range(RP):
+            quantize_wv(b)
+        quantize(z_codes[0, 0][:], z_sc[:, 0, cols(0)], z_bf[0][:, cols(0)])
         weave(nc.vector.tensor_copy, x_bf[1, 1][:, X_BY_SCALAR:], x_rows(1)[:, :, HALF + X_BY_SCALAR:])
-        quantize(x_codes[1][:, cols(0)], x_sc[:, 1, cols(0)], x_bf[1, 0][:])
-        quantize_wv(1)
-        quantize(x_codes[1][:, cols(1)], x_sc[:, 1, cols(1)], x_bf[1, 1][:])
-        quantize(z_codes[0][:], z_sc[:, 0], z_bf[0][:])
-        for h in range(2):
-            quantize(z_codes[1][:, cols(h)], z_sc[:, 1, cols(h)], z_bf[1, h][:])
+        quantize(x_codes[1, 0][:], x_sc[:, 1, cols(0)], x_bf[1, 0][:])
+        quantize(x_codes[1, 1][:], x_sc[:, 1, cols(1)], x_bf[1, 1][:])
+        quantize(z_codes[1, 0][:], z_sc[:, 1, cols(0)], z_bf[1, 0][:])
+        quantize(z_codes[0, 1][:], z_sc[:, 0, cols(1)], z_bf[0][:, cols(1)])
+        quantize(z_codes[1, 1][:], z_sc[:, 1, cols(1)], z_bf[1, 1][:])
 
         def gate_pass(acc, n, b, h):
             nc.tensor.matmul_mx(out=acc[:], lhsT=w8_codes[:, b, P * n:P * (n + 1)].bitcast(FP8X4),
                                 lhsT_scale=w8_sc[:, b, P * n:P * (n + 1)],
-                                rhs=x_codes[b][:, cols(h)].bitcast(FP8X4), rhs_scale=x_sc[:, b, cols(h)],
+                                rhs=x_codes[b, h][:].bitcast(FP8X4), rhs_scale=x_sc[:, b, cols(h)],
                                 start=(b == 0), stop=(b == RP - 1))
 
         def value_pass(acc, n, b, h):
             c0 = b * N + P * n
             nc.tensor.matmul_mx(out=acc[:], lhsT=wv_codes[:, c0:c0 + P].bitcast(FP8X4), lhsT_scale=wv_sc[:, c0:c0 + P],
-                                rhs=z_codes[b][:, cols(h)].bitcast(FP8X4), rhs_scale=z_sc[:, b, cols(h)],
+                                rhs=z_codes[b, h][:].bitcast(FP8X4), rhs_scale=z_sc[:, b, cols(h)],
                                 start=(b == 0), stop=(b == RP - 1))
 
         order = [(n, h) for h in range(2) for n in range(NT)]

@@ -30,21 +30,21 @@ EARLY = 2 * P
 LATE = H - EARLY
 ROWS0 = 48
 PAGES = 5
-X_BY_SCALAR = 32
+X_BY_SCALAR = 64
 KB = 1024
 LAP = 256
 
 AT_LATEST = 0
-AT_TAB1 = 16 * KB - LAP
-AT_WGS1 = 24 * KB
-AT_LATE_PLANES = 28 * KB
-AT_X0 = 30 * KB + LAP
-AT_TAB2 = 54 * KB
-AT_WGS2 = 62 * KB + LAP
-AT_W8 = 66 * KB + LAP
-AT_GAINS = 69 * KB + LAP
-AT_TAB0 = 78 * KB - LAP
-AT_PAGES = (AT_TAB0, 16 * KB, AT_TAB2 + LAP - 8 * KB, AT_TAB2 + LAP, AT_TAB0 - 8 * KB)
+AT_TAB1 = 20 * KB - LAP
+AT_WGS1 = 28 * KB
+AT_LATE_PLANES = 32 * KB
+AT_X0 = 34 * KB + LAP
+AT_TAB2 = 58 * KB
+AT_WGS2 = 66 * KB + LAP
+AT_W8 = 70 * KB + LAP
+AT_GAINS = 73 * KB + LAP
+AT_TAB0 = 82 * KB - LAP
+AT_PAGES = (AT_TAB0, 20 * KB, AT_TAB2 + LAP - 8 * KB, AT_TAB2 + LAP, AT_TAB0 - 8 * KB)
 AT_WVBF = AT_TAB0 + 8 * KB
 AT_V = AT_TAB0 + 16 * KB
 AT_PLANES = AT_V + 12 * KB
@@ -86,7 +86,7 @@ def tile_list_dialogue_reply_ranker_kernel(tc, tab_words, tab_scales, offs, offs
         list3 = lists.tile([P, M // 16], U16)
         whole = slice(0, S)
         ramp = (slice(0, QUARTER), slice(QUARTER, HALF), cols(1))
-        opening = (slice(0, QUARTER), slice(QUARTER, S - QUARTER), slice(S - QUARTER, S))
+        closing = (slice(0, HALF - P), slice(HALF - P, HALF))
 
         tab_rows = [tab_words[a].rearrange("p t i -> p (t i)").bitcast(I32) for a in range(KP)]
         tabs = {0: at("tab0", [P, T], I32, AT_TAB0)}
@@ -94,9 +94,10 @@ def tile_list_dialogue_reply_ranker_kernel(tc, tab_words, tab_scales, offs, offs
         w4s_raw = at("w4s_raw", [P, H], U8, AT_TAB2 + 2 * KB)
         rows = at("rows", [P, S + H], U8, AT_ROWS)
         planes = at("planes", [P, KP, S + EARLY], U8, AT_PLANES)
-        weights = {0: at("wgs0", [P, S], F32, AT_WGS0)[:]}
-        w4_raw = {0: at("w4_raw0", [P, KP, 2 * HALF], U8, AT_W4_RAW)}
-        w4_dealt = {}
+        weights = {}
+        opening = at("opening", [P, 2, HALF], F32, AT_WGS0)
+        w4_raw = {0: at("w4_raw0", [P, KP - 1, 2 * HALF], U8, AT_W4_RAW)}
+        w4_dealt = [at("w4_dealt%d" % b, [P, PACK, KP, 2 * P], U8, AT_W4 + 3 * KB * b) for b in range(RP)]
 
         def load_scale_rows(tile, scales):
             nc.sync.dma_start(tile[ROWS0:2 * ROWS0, :].bitcast(I32), scales.rearrange("a q c -> q a c").bitcast(I32))
@@ -111,19 +112,19 @@ def tile_list_dialogue_reply_ranker_kernel(tc, tab_words, tab_scales, offs, offs
 
         w4_rows = w4_words.rearrange("a p c -> p a c")
 
-        def load_w4(b):
-            nc.sync.dma_start(w4_raw[b][:].bitcast(I32), w4_rows[:, :, 2 * HALF * b:2 * HALF * (b + 1)].bitcast(I32))
+        def load_w4(b, passes):
+            nc.sync.dma_start(w4_raw[b][:, passes].bitcast(I32), w4_rows[:, passes, 2 * HALF * b:2 * HALF * (b + 1)].bitcast(I32))
 
-        def deal_w4(b):
-            w4_dealt[b] = at("w4_dealt%d" % b, [P, PACK, KP, 2 * P], U8, AT_W4 + 3 * KB * b)
-            nc.scalar.copy(w4_dealt[b][:].bitcast(U16).rearrange("p t a (c i) -> p a c t i", i=8),
-                           w4_raw[b][:].bitcast(U16).rearrange("p a (c i t) -> p a c t i", t=PACK, i=8))
+        def deal_w4(b, passes):
+            nc.scalar.copy(w4_dealt[b][:].bitcast(U16).rearrange("p t a (c i) -> p a c t i", i=8)[:, passes],
+                           w4_raw[b][:].bitcast(U16).rearrange("p a (c i t) -> p a c t i", t=PACK, i=8)[:, passes])
 
         wgs_rows = wgs.rearrange("(q t) j -> q t j", t=PACK)
 
-        def load_weights(t):
-            for q in QUADS:
-                nc.sync.dma_start(weights[t][32 * q:32 * q + 32, :], wgs_rows[:, t, :])
+        def load_weights(t, part):
+            for q in range(2):
+                nc.sync.dma_start(weights[t][32 * q:32 * q + 32, part], wgs_rows[:, t, part])
+            nc.scalar.copy(weights[t][64:128, part], weights[t][0:64, part])
 
         page_rows = page0.rearrange("(b p t) c -> b t p c", p=P, t=PACK)
         pages = {}
@@ -137,8 +138,8 @@ def tile_list_dialogue_reply_ranker_kernel(tc, tab_words, tab_scales, offs, offs
         load_scale_rows(ts_win, tab_scales)
         load_scale_rows(w4s_raw, w4_scales)
         nc.sync.dma_start(tabs[0][:, T // 2:], tab_rows[0][:, T // 2:])
-        nc.sync.dma_start(weights[0][0:32, :], wgs_rows[:, 0, :])
-        load_w4(0)
+        nc.sync.dma_start(opening[0:32], wgs_rows[:, 0:2, cols(0)])
+        load_w4(0, slice(0, KP - 1))
         tabs[1] = at("tab1", [P, T], I32, AT_TAB1)
         nc.sync.dma_start(tabs[1][:], tab_rows[1])
         nc.sync.dma_start(list2[:], offs2)
@@ -154,7 +155,7 @@ def tile_list_dialogue_reply_ranker_kernel(tc, tab_words, tab_scales, offs, offs
         move_scale_rows(nc.sync, planes, slice(0, S + EARLY), QUADS[2:])
         tabs[2] = at("tab2", [P, T], I32, AT_TAB2)
         nc.sync.dma_start(tabs[2][:], tab_rows[2])
-        deal_w4(0)
+        deal_w4(0, slice(0, KP - 1))
 
         v_codes = [at("v_codes%d" % a, [P, S], U32, AT_V + 4 * KB * a) for a in range(KP)]
 
@@ -162,32 +163,13 @@ def tile_list_dialogue_reply_ranker_kernel(tc, tab_words, tab_scales, offs, offs
             nc.vector.tensor_copy(v_codes[a][:, part], tabs[a][:].bitcast(U32).indirect(entries(list1, part)))
 
         look_up(0, whole)
-        nc.vector.tensor_copy(weights[0][32:64, :].bitcast(I32), weights[0][0:32, :].bitcast(I32))
-        nc.vector.tensor_copy(weights[0][64:128, :].bitcast(I32), weights[0][0:64, :].bitcast(I32))
+        nc.vector.tensor_copy(opening[32:64].bitcast(I32), opening[0:32].bitcast(I32))
+        nc.vector.tensor_copy(opening[64:128].bitcast(I32), opening[0:64].bitcast(I32))
         look_up(1, whole)
         late_planes = at("late_planes", [P, KP, LATE], U8, AT_LATE_PLANES)
         nc.vector.memset(late_planes[:].bitcast(I32), 0)
-        for part in opening:
+        for part in ramp:
             look_up(2, part)
-
-        load_page(0)
-        load_page(1)
-        weights[1] = at("wgs1", [P, S], F32, AT_WGS1)[:]
-        load_weights(1)
-        move_scale_rows(nc.sync, late_planes, slice(S + EARLY, S + H), QUADS)
-        w4_raw[1] = at("w4_raw1", [P, KP, 2 * HALF], U8, AT_X0)
-        load_w4(1)
-        load_page(2)
-        weights[2] = at("wgs2", [P, S], F32, AT_WGS2)[:]
-        load_weights(2)
-        gains = at("gains", [P, 2, RP, PACK], F32, AT_GAINS)
-        nc.sync.dma_start(gains[:, 0], gin.rearrange("(b p t) -> p b t", p=P, t=PACK))
-        load_page(3)
-        latest = at("latest", [P, S + RP * PACK * N], F32, AT_LATEST)
-        weights[3] = latest[:, :S]
-        load_weights(3)
-        load_page(4)
-        nc.sync.dma_start(gains[:, 1], gout.rearrange("(b p t) -> p b t", p=P, t=PACK))
 
         x_f32 = [at("x_f32_%d" % b, [P, PACK * M], F32, (AT_X0, AT_X1)[b]) for b in range(RP)]
         z_rows = at("z_rows", [P, LAST, M], BF16, AT_ZROWS)
@@ -198,7 +180,7 @@ def tile_list_dialogue_reply_ranker_kernel(tc, tab_words, tab_scales, offs, offs
 
         def project(i):
             staged[i] = at("staged%d" % i, [P, S], F32, AT_STAGED[i % 3])
-            groups = zip(opening, range(3)) if i == 0 else zip((cols(0), cols(1)), ((2 * i + 1) % 8, (2 * i + 2) % 8))
+            groups = zip(ramp, range(3)) if i == 0 else zip((cols(0), cols(1)), ((2 * i + 1) % 8, (2 * i + 2) % 8))
             for part, n in groups:
                 acc = bank(n)
                 width = part.stop - part.start
@@ -213,10 +195,9 @@ def tile_list_dialogue_reply_ranker_kernel(tc, tab_words, tab_scales, offs, offs
                         start=(a == 0), stop=(a == KP - 1))
                 nc.scalar.copy(staged[i][:, part], acc[:, :width])
 
-        def scatter(i):
-            for part in (ramp[0], slice(QUARTER, S)) if i == 0 else (whole,):
-                nc.vector.tensor_tensor(pages[i][:].indirect(entries(list2, part)), staged[i][:, part],
-                                        weights[i % PACK][:, part], ALU.mult)
+        def scatter(i, part, factors):
+            nc.vector.tensor_tensor(pages[i][:].indirect(entries(list2, part)), staged[i][:, part],
+                                    factors, ALU.mult)
 
         def fetch(i, part):
             nc.vector.tensor_copy(x_row(i)[:, part], pages[i][:].indirect(entries(list3, part)))
@@ -235,7 +216,7 @@ def tile_list_dialogue_reply_ranker_kernel(tc, tab_words, tab_scales, offs, offs
                 parked = at("parked%d" % i, [P, HALF], F32, AT_STAGED[i % 3] + shift)
                 parts = [(cols(1), parked[:]), (cols(0), x_row(i + 1)[:, cols(0)])]
                 if i == PACK - 1:
-                    parts = [(ramp[0], latest[:, S:S + QUARTER]), parts[0], (ramp[1], x_row(i + 1)[:, ramp[0]])]
+                    parts = [(ramp[0], latest[:, 2 * S:2 * S + QUARTER]), parts[0], (ramp[1], x_row(i + 1)[:, ramp[0]])]
                 if i == PACK:
                     parts[1] = (cols(0), x_f32[1][:, 2 * M - QUARTER:2 * M + QUARTER])
             else:
@@ -252,24 +233,54 @@ def tile_list_dialogue_reply_ranker_kernel(tc, tab_words, tab_scales, offs, offs
         def x_rows(b):
             return x_f32[b][:].rearrange("p (t m) -> p t m", t=PACK)
 
+        w4_last = at("w4_last", [P, 2 * HALF], U8, AT_WVBF)
+        nc.sync.dma_start(w4_last[:].bitcast(I32), w4_rows[:, KP - 1, :2 * HALF].bitcast(I32))
+        nc.scalar.copy(w4_dealt[0][:, :, KP - 1].bitcast(U16).rearrange("p t (c i) -> p c t i", i=8),
+                       w4_last[:].bitcast(U16).rearrange("p (c i t) -> p c t i", t=PACK, i=8))
+        load_page(0)
+        load_page(1)
+        latest = at("latest", [P, 2 * S + RP * PACK * N], F32, AT_LATEST)
+        weights[0] = latest[:, S:2 * S]
+        load_weights(0, cols(1))
+        weights[1] = at("wgs1", [P, S], F32, AT_WGS1)[:]
+        load_weights(1, cols(1))
+        for t in range(2):
+            nc.scalar.copy(weights[t][:, cols(0)], opening[:, t])
+        move_scale_rows(nc.sync, late_planes, slice(S + EARLY, S + H), QUADS)
+        w4_raw[1] = at("w4_raw1", [P, KP, 2 * HALF], U8, AT_X0)
+        load_w4(1, slice(0, KP))
+        load_page(2)
+        weights[2] = at("wgs2", [P, S], F32, AT_WGS2)[:]
+        load_weights(2, whole)
+        gains = at("gains", [P, 2, RP, PACK], F32, AT_GAINS)
+        nc.sync.dma_start(gains[:, 0], gin.rearrange("(b p t) -> p b t", p=P, t=PACK))
+        load_page(3)
+        weights[3] = latest[:, :S]
+        load_weights(3, whole)
+        load_page(4)
+        nc.sync.dma_start(gains[:, 1], gout.rearrange("(b p t) -> p b t", p=P, t=PACK))
+
         project(0)
         project(1)
         project(2)
-        deal_w4(1)
+        deal_w4(1, slice(0, KP))
         w8_codes = at("w8_codes", [P, RP, N], U32, AT_W8)
         w8_sc = w4_dealt[0][:, 0].rearrange("p a c -> p (a c)").rearrange("p (b c) -> p b c", b=RP)
         for q in QUADS:
             nc.sync.dma_start(w8_sc[32 * q:32 * q + 4, :, :].bitcast(I32),
                               w8_scales[:, 4 * q:4 * q + 4, :].rearrange("b r c -> r b c").bitcast(I32))
         nc.sync.dma_start(w8_codes[:].bitcast(I32), w8_words.rearrange("b p c i -> p b (c i)").bitcast(I32))
-        wv_raw = latest[:, S:].rearrange("p (b j n) -> p b j n", b=RP, j=PACK)
+        wv_raw = latest[:, 2 * S:].rearrange("p (b j n) -> p b j n", b=RP, j=PACK)
         nc.sync.dma_start(wv_raw, wv.rearrange("(b p j) n -> p b j n", p=P, j=PACK))
 
         x_bf = {}
         z_bf = {}
-        scatter(0)
+        for i in range(2):
+            scatter(i, cols(0), opening[:, i])
+        scatter(0, cols(1), weights[0][:, cols(1)])
         for i in range(SLICES - 2):
-            scatter(i + 1)
+            part = whole if i else cols(1)
+            scatter(i + 1, part, weights[(i + 1) % PACK][:, part])
             fetch(i, whole)
             if i + PAGES < SLICES:
                 load_page(i + PAGES)
@@ -297,7 +308,7 @@ def tile_list_dialogue_reply_ranker_kernel(tc, tab_words, tab_scales, offs, offs
             x_bf[1, h] = at("x_bf1%d" % h, [P, HALF, PACK], BF16, AT_XBF + 8 * KB + 4 * KB * h)
             z_bf[1, h] = at("z_bf1%d" % h, [P, HALF, PACK], BF16, AT_ZBF + 8 * KB + 4 * KB * h)
             weave(nc.scalar.copy, z_bf[1, h][:, :, :PACK - 1], z_rows[:, PACK:, cols(h)])
-        scatter(LAST)
+        scatter(LAST, whole, weights[LAST % PACK])
 
         x_codes = {}
         z_codes = {}
@@ -306,7 +317,7 @@ def tile_list_dialogue_reply_ranker_kernel(tc, tab_words, tab_scales, offs, offs
                 x_codes[b, h] = at("x_codes%d%d" % (b, h), [P, HALF], U32,
                                    AT_LATEST + 2 * KB * (2 * b + h) if b + h else AT_PAGES[(LAST - 1) % PAGES])
                 z_codes[b, h] = at("z_codes%d%d" % (b, h), [P, HALF], U32,
-                                   AT_ZROWS + 12 * KB if (b, h) == (0, 1) else AT_LATEST + 8 * KB + 2 * KB * (2 * b + h))
+                                   AT_ZROWS + KB if (b, h) == (0, 1) else AT_LATEST + 8 * KB + 2 * KB * (2 * b + h))
         wv_codes = at("wv_codes", [P, RP * N], U32, AT_STAGED[LAST % 3])
         x_sc = at("x_sc", [P, RP, M], U8, AT_SC)
         z_sc = at("z_sc", [P, RP, M], U8, AT_SC + 2 * KB)
@@ -320,10 +331,11 @@ def tile_list_dialogue_reply_ranker_kernel(tc, tab_words, tab_scales, offs, offs
                                   in_=wv_bf[:, b * N * PACK:(b + 1) * N * PACK])
 
         quantize(x_codes[0, 0][:], x_sc[:, 0, cols(0)], x_bf[0][:, cols(0)])
-        for part in ramp:
+        last_parts = (slice(0, P), slice(P, HALF), cols(1))
+        for part in last_parts:
             fetch(LAST, part)
-        ge_last = [at("ge_last%d" % h, [P, HALF], F32, AT_ZROWS + 12 * KB * (1 - h)) for h in range(2)]
-        for part in ramp[:2]:
+        ge_last = [at("ge_last%d" % h, [P, HALF], F32, AT_ZROWS + 4 * KB * h) for h in range(2)]
+        for part in last_parts[:2]:
             weave(nc.scalar.copy, x_bf[1, 0][:, part], x_rows(1)[:, :, part])
         weave(nc.scalar.copy, x_bf[1, 1][:, :X_BY_SCALAR], x_rows(1)[:, :, HALF:HALF + X_BY_SCALAR])
         for h in range(2):
@@ -361,16 +373,16 @@ def tile_list_dialogue_reply_ranker_kernel(tc, tab_words, tab_scales, offs, offs
         for b in range(RP):
             for n, h in order:
                 gate_pass(gate[n, h], n, b, h)
-        th_all = at("th_all", [P, len(order), HALF], F32, AT_ZROWS)
+        th_all = at("th_all", [P, len(order), HALF], F32, AT_ZROWS - 11 * KB)
         for k, (n, h) in enumerate(order):
-            for part in ramp[:2] if k == len(order) - 1 else (cols(0),):
+            for part in closing if k == len(order) - 1 else (cols(0),):
                 nc.scalar.activation(th_all[:, k, part], gate[n, h][:, part], ACT.Tanh, scale=0.5)
         for k, (n, h) in enumerate(order):
             value = bank((7 + k) % 8)
             for b in range(RP):
                 value_pass(value, n, b, h)
             res = at("res%d" % k, [P, HALF], F32, AT_PAGES[3] + 2 * KB * k)
-            for part in ramp[:2] if k == len(order) - 1 else (cols(0),):
+            for part in closing if k == len(order) - 1 else (cols(0),):
                 nc.vector.scalar_tensor_tensor(out=res[:, part], in0=th_all[:, k, part], scalar=1.0, in1=value[:, part],
                                                op0=ALU.add, op1=ALU.mult)
                 nc.sync.dma_start(out[P * n:P * (n + 1), cols(h)][:, part], res[:, part])

from contextlib import ExitStack

import concourse.mybir as mybir

K, H, N, T, S, T2, M = 1536, 1024, 384, 4096, 1024, 2048, 1024
FLOPS = 2 * K * H * S + 4 * H * N * M

F32 = mybir.dt.float32
BF16 = mybir.dt.bfloat16
I32 = mybir.dt.int32
U32 = mybir.dt.uint32
U16 = mybir.dt.uint16
U8 = mybir.dt.uint8
FP8X4 = mybir.dt.float8_e4m3fn_x4
FP4X4 = mybir.dt.float4_e2m1fn_x4
ACT = mybir.ActivationFunctionType
ALU = mybir.AluOpType

P = 128
PACK = 4
KP = K // (P * PACK)
RP = H // (P * PACK)
SLICES = RP * PACK
LAST = SLICES - 1
HALF = 512
QUARTER = 256
NT = N // P
QUADS = (0, 2, 1, 3)
EARLY = 2 * P
LATE = H - EARLY
ROWS0 = 48
PAGES = 5
X_BY_SCALAR = 64
KB = 1024
LAP = 256

AT_LATEST = 0
AT_TAB1 = 20 * KB - LAP
AT_WGS1 = 28 * KB
AT_LATE_PLANES = 32 * KB
AT_X0 = 34 * KB + LAP
AT_TAB2 = 58 * KB
AT_WGS2 = 66 * KB + LAP
AT_W8 = 70 * KB + LAP
AT_GAINS = 73 * KB + LAP
AT_TAB0 = 82 * KB - LAP
AT_PAGES = (AT_TAB0, 20 * KB, AT_TAB2 + LAP - 8 * KB, AT_TAB2 + LAP, AT_TAB0 - 8 * KB)
AT_WVBF = AT_TAB0 + 8 * KB
AT_V = AT_TAB0 + 16 * KB
AT_PLANES = AT_V + 12 * KB
AT_W4 = AT_PLANES + 4 * KB - LAP
AT_W4_RAW = AT_W4 + 6 * KB
AT_ROWS = AT_W4_RAW + 3 * KB
AT_WGS0 = AT_ROWS + 2 * KB
AT_STAGED = (AT_WGS0 + 12 * KB, AT_WGS0 + 4 * KB, AT_WGS0 + 8 * KB)
AT_XBF = AT_WGS0 + 16 * KB
AT_ZBF = AT_XBF + 16 * KB
AT_X1 = AT_ZBF + 16 * KB
AT_ZROWS = AT_X1 + 16 * KB
AT_SC = AT_ZROWS + 14 * KB
AT_CLK = AT_SC + 6 * KB


def tile_list_dialogue_reply_ranker_kernel(tc, tab_words, tab_scales, offs, offs2, offs3, w4_words, w4_scales,
                                                        w8_words, w8_scales, wv, page0, wgs, gin, gout, out):
    nc = tc.nc
    with ExitStack() as ctx:
        lists = ctx.enter_context(tc.tile_pool(name="lists", bufs=1))
        mem = ctx.enter_context(tc.tile_pool(name="mem", bufs=1))
        psum = ctx.enter_context(tc.psum_pool(name="psum", bufs=1))

        def at(name, shape, dtype, offset):
            return mem.tile(shape, dtype, name=name, align_bytes=LAP, offset=offset)

        def bank(n):
            return psum.tile([P, HALF], F32, name="bank%d" % n)

        def cols(h):
            return slice(h * HALF, (h + 1) * HALF)

        def entries(lst, part):
            return lst[:, part.start // 16:part.stop // 16]

        list1 = lists.tile([P, S // 16], U16)
        list2 = lists.tile([P, S // 16], U16)
        list3 = lists.tile([P, M // 16], U16)
        whole = slice(0, S)
        ramp = (slice(0, QUARTER), slice(QUARTER, HALF), cols(1))
        closing = (slice(0, HALF - P), slice(HALF - P, HALF))

        tab_rows = [tab_words[a].rearrange("p t i -> p (t i)").bitcast(I32) for a in range(KP)]
        tabs = {0: at("tab0", [P, T], I32, AT_TAB0)}
        ts_win = at("ts_win", [P, T], U8, AT_V)
        w4s_raw = at("w4s_raw", [P, H], U8, AT_TAB2 + 2 * KB)
        rows = at("rows", [P, S + H], U8, AT_ROWS)
        planes = at("planes", [P, KP, S + EARLY], U8, AT_PLANES)
        weights = {}
        opening = at("opening", [P, 2, HALF], F32, AT_WGS0)
        w4_raw = {0: at("w4_raw0", [P, KP - 1, 2 * HALF], U8, AT_W4_RAW)}
        w4_dealt = [at("w4_dealt%d" % b, [P, PACK, KP, 2 * P], U8, AT_W4 + 3 * KB * b) for b in range(RP)]

        def load_scale_rows(tile, scales):
            nc.sync.dma_start(tile[ROWS0:2 * ROWS0, :].bitcast(I32), scales.rearrange("a q c -> q a c").bitcast(I32))
            nc.vector.memset(tile[0:ROWS0, :].bitcast(I32), 0)
            nc.vector.memset(tile[2 * ROWS0:P, :].bitcast(I32), 0)

        def move_scale_rows(queue, dst, part, quads):
            for q in quads:
                row = ROWS0 + 4 * KP * q
                queue.dma_start(dst[32 * q:32 * q + 4].rearrange("p a c -> p (a c)").bitcast(I32),
                                rows[row:row + 4 * KP, part].bitcast(I32))

        w4_rows = w4_words.rearrange("a p c -> p a c")

        def load_w4(b, passes):
            nc.sync.dma_start(w4_raw[b][:, passes].bitcast(I32), w4_rows[:, passes, 2 * HALF * b:2 * HALF * (b + 1)].bitcast(I32))

        def deal_w4(b, passes):
            nc.scalar.copy(w4_dealt[b][:].bitcast(U16).rearrange("p t a (c i) -> p a c t i", i=8)[:, passes],
                           w4_raw[b][:].bitcast(U16).rearrange("p a (c i t) -> p a c t i", t=PACK, i=8)[:, passes])

        wgs_rows = wgs.rearrange("(q t) j -> q t j", t=PACK)

        def load_weights(t, part):
            for q in range(2):
                nc.sync.dma_start(weights[t][32 * q:32 * q + 32, part], wgs_rows[:, t, part])
            nc.scalar.copy(weights[t][64:128, part], weights[t][0:64, part])

        page_rows = page0.rearrange("(b p t) c -> b t p c", p=P, t=PACK)
        pages = {}

        def load_page(k):
            pages[k] = at("page%d" % k, [P, T2], F32, AT_PAGES[k % PAGES])
            nc.sync.dma_start(pages[k][:], page_rows[k // PACK, k % PACK])

        nc.sync.dma_start(tabs[0][:, :T // 2], tab_rows[0][:, :T // 2])
        nc.sync.dma_start(list1[:], offs)
        load_scale_rows(ts_win, tab_scales)
        load_scale_rows(w4s_raw, w4_scales)
        nc.sync.dma_start(tabs[0][:, T // 2:], tab_rows[0][:, T // 2:])
        nc.sync.dma_start(opening[0:32], wgs_rows[:, 0:2, cols(0)])
        load_w4(0, slice(0, KP - 1))
        tabs[1] = at("tab1", [P, T], I32, AT_TAB1)
        nc.sync.dma_start(tabs[1][:], tab_rows[1])
        nc.sync.dma_start(list2[:], offs2)
        nc.sync.dma_start(list3[:], offs3)
        nc.vector.memset(planes[:].bitcast(I32), 0)

        nc.vector.tensor_copy(rows[:, S:].rearrange("p (b t m) -> p b t m", b=RP, t=PACK),
                              w4s_raw[:].rearrange("p (b m t) -> p b t m", b=RP, t=PACK))
        ts_got = at("ts_got", [P, S], U8, AT_TAB2 + 2 * KB)
        nc.vector.tensor_copy(ts_got[:], ts_win[:].indirect(list1[:]))
        nc.vector.tensor_copy(rows[:, :S].bitcast(I32), ts_got[:].bitcast(I32))
        move_scale_rows(nc.scalar, planes, slice(0, S + EARLY), QUADS[:2])
        move_scale_rows(nc.sync, planes, slice(0, S + EARLY), QUADS[2:])
        tabs[2] = at("tab2", [P, T], I32, AT_TAB2)
        nc.sync.dma_start(tabs[2][:], tab_rows[2])
        deal_w4(0, slice(0, KP - 1))

        v_codes = [at("v_codes%d" % a, [P, S], U32, AT_V + 4 * KB * a) for a in range(KP)]

        def look_up(a, part):
            nc.vector.tensor_copy(v_codes[a][:, part], tabs[a][:].bitcast(U32).indirect(entries(list1, part)))

        look_up(0, whole)
        nc.vector.tensor_copy(opening[32:64].bitcast(I32), opening[0:32].bitcast(I32))
        nc.vector.tensor_copy(opening[64:128].bitcast(I32), opening[0:64].bitcast(I32))
        look_up(1, whole)
        late_planes = at("late_planes", [P, KP, LATE], U8, AT_LATE_PLANES)
        nc.vector.memset(late_planes[:].bitcast(I32), 0)
        for part in ramp:
            look_up(2, part)

        x_f32 = [at("x_f32_%d" % b, [P, PACK * M], F32, (AT_X0, AT_X1)[b]) for b in range(RP)]
        z_rows = at("z_rows", [P, LAST, M], BF16, AT_ZROWS)
        staged = {}

        def x_row(i):
            return x_f32[i // PACK][:, M * (i % PACK):M * (i % PACK + 1)]

        def project(i):
            staged[i] = at("staged%d" % i, [P, S], F32, AT_STAGED[i % 3])
            groups = zip(ramp, range(3)) if i == 0 else zip((cols(0), cols(1)), ((2 * i + 1) % 8, (2 * i + 2) % 8))
            for part, n in groups:
                acc = bank(n)
                width = part.stop - part.start
                for a in range(KP):
                    nc.tensor.matmul_mx(
                        out=acc[:, :width],
                        lhsT=w4_dealt[i // PACK][:, i % PACK, a].bitcast(FP4X4),
                        lhsT_scale=(planes[:, a, S + P * i:S + P * (i + 1)] if P * i < EARLY
                                    else late_planes[:, a, P * i - EARLY:P * (i + 1) - EARLY]),
                        rhs=v_codes[a][:, part].bitcast(FP8X4),
                        rhs_scale=planes[:, a, part],
                        start=(a == 0), stop=(a == KP - 1))
                nc.scalar.copy(staged[i][:, part], acc[:, :width])

        def scatter(i, part, factors):
            nc.vector.tensor_tensor(pages[i][:].indirect(entries(list2, part)), staged[i][:, part],
                                    factors, ALU.mult)

        def fetch(i, part):
            nc.vector.tensor_copy(x_row(i)[:, part], pages[i][:].indirect(entries(list3, part)))

        def gelu(i, part, ge):
            b, t = divmod(i, PACK)
            nc.scalar.activation(ge, x_row(i)[:, part], ACT.Gelu_apprx_tanh, scale=gains[:, 0, b, t:t + 1])

        def gain(i, dst, ge):
            b, t = divmod(i, PACK)
            nc.scalar.activation(dst, ge, ACT.Copy, scale=gains[:, 1, b, t:t + 1])

        def make_z(i):
            if i + 3 < SLICES:
                shift = 3 * KB if i == PACK - 1 else 0
                parked = at("parked%d" % i, [P, HALF], F32, AT_STAGED[i % 3] + shift)
                parts = [(cols(1), parked[:]), (cols(0), x_row(i + 1)[:, cols(0)])]
                if i == PACK - 1:
                    parts = [(ramp[0], latest[:, 2 * S:2 * S + QUARTER]), parts[0], (ramp[1], x_row(i + 1)[:, ramp[0]])]
                if i == PACK:
                    parts[1] = (cols(0), x_f32[1][:, 2 * M - QUARTER:2 * M + QUARTER])
            else:
                ge_row = at("ge%d" % i, [P, M], F32, AT_XBF + 8 * KB + 4 * KB * (LAST - 1 - i))
                parts = [(cols(h), ge_row[:, cols(h)]) for h in range(2)]
            for part, ge in parts:
                gelu(i, part, ge)
            for part, ge in parts:
                gain(i, z_rows[:, i, part], ge)

        def weave(copy, dst, src):
            copy(dst.rearrange("p (c i) t -> p c t i", i=4), src.rearrange("p t (c i) -> p c t i", i=4))

        def x_rows(b):
            return x_f32[b][:].rearrange("p (t m) -> p t m", t=PACK)

        w4_last = at("w4_last", [P, 2 * HALF], U8, AT_WVBF)
        nc.sync.dma_start(w4_last[:].bitcast(I32), w4_rows[:, KP - 1, :2 * HALF].bitcast(I32))
        nc.scalar.copy(w4_dealt[0][:, :, KP - 1].bitcast(U16).rearrange("p t (c i) -> p c t i", i=8),
                       w4_last[:].bitcast(U16).rearrange("p (c i t) -> p c t i", t=PACK, i=8))
        load_page(0)
        load_page(1)
        latest = at("latest", [P, 2 * S + RP * PACK * N], F32, AT_LATEST)
        weights[0] = latest[:, S:2 * S]
        load_weights(0, cols(1))
        weights[1] = at("wgs1", [P, S], F32, AT_WGS1)[:]
        load_weights(1, cols(1))
        for t in range(2):
            nc.scalar.copy(weights[t][:, cols(0)], opening[:, t])
        move_scale_rows(nc.sync, late_planes, slice(S + EARLY, S + H), QUADS)
        w4_raw[1] = at("w4_raw1", [P, KP, 2 * HALF], U8, AT_X0)
        load_w4(1, slice(0, KP))
        load_page(2)
        weights[2] = at("wgs2", [P, S], F32, AT_WGS2)[:]
        load_weights(2, whole)
        gains = at("gains", [P, 2, RP, PACK], F32, AT_GAINS)
        nc.sync.dma_start(gains[:, 0], gin.rearrange("(b p t) -> p b t", p=P, t=PACK))
        load_page(3)
        weights[3] = latest[:, :S]
        load_weights(3, whole)
        load_page(4)
        nc.sync.dma_start(gains[:, 1], gout.rearrange("(b p t) -> p b t", p=P, t=PACK))

        project(0)
        project(1)
        project(2)
        deal_w4(1, slice(0, KP))
        w8_codes = at("w8_codes", [P, RP, N], U32, AT_W8)
        w8_sc = w4_dealt[0][:, 0].rearrange("p a c -> p (a c)").rearrange("p (b c) -> p b c", b=RP)
        for q in QUADS:
            nc.sync.dma_start(w8_sc[32 * q:32 * q + 4, :, :].bitcast(I32),
                              w8_scales[:, 4 * q:4 * q + 4, :].rearrange("b r c -> r b c").bitcast(I32))
        nc.sync.dma_start(w8_codes[:].bitcast(I32), w8_words.rearrange("b p c i -> p b (c i)").bitcast(I32))
        wv_raw = latest[:, 2 * S:].rearrange("p (b j n) -> p b j n", b=RP, j=PACK)
        nc.sync.dma_start(wv_raw, wv.rearrange("(b p j) n -> p b j n", p=P, j=PACK))

        x_bf = {}
        z_bf = {}
        for i in range(2):
            scatter(i, cols(0), opening[:, i])
        scatter(0, cols(1), weights[0][:, cols(1)])
        for i in range(SLICES - 2):
            part = whole if i else cols(1)
            scatter(i + 1, part, weights[(i + 1) % PACK][:, part])
            fetch(i, whole)
            if i + PAGES < SLICES:
                load_page(i + PAGES)
            if i == SLICES - 3:
                fetch(i + 1, whole)
            make_z(i)
            if i + 3 < SLICES:
                project(i + 3)
            if i == 1:
                wv_bf = at("wv_bf", [P, RP * N * PACK], BF16, AT_WVBF)
                for b in range(RP):
                    nc.scalar.activation(
                        wv_bf[:, b * N * PACK:(b + 1) * N * PACK].rearrange("p (c i j) -> p c j i", i=4, j=PACK),
                        wv_raw[:, b].rearrange("p j (c i) -> p c j i", i=4), ACT.Copy, scale=0.5)
            if i == PACK - 1:
                x_bf[0] = at("x_bf0", [P, M, PACK], BF16, AT_XBF)
                for h in range(2):
                    weave(nc.scalar.copy, x_bf[0][:, cols(h)], x_rows(0)[:, :, cols(h)])
            if i == PACK:
                z_bf[0] = at("z_bf0", [P, M, PACK], BF16, AT_ZBF)
                for h in range(2):
                    weave(nc.scalar.copy, z_bf[0][:, cols(h)], z_rows[:, :PACK, cols(h)])
        make_z(LAST - 1)
        for h in range(2):
            x_bf[1, h] = at("x_bf1%d" % h, [P, HALF, PACK], BF16, AT_XBF + 8 * KB + 4 * KB * h)
            z_bf[1, h] = at("z_bf1%d" % h, [P, HALF, PACK], BF16, AT_ZBF + 8 * KB + 4 * KB * h)
            weave(nc.scalar.copy, z_bf[1, h][:, :, :PACK - 1], z_rows[:, PACK:, cols(h)])
        scatter(LAST, whole, weights[LAST % PACK])

        x_codes = {}
        z_codes = {}
        for b in range(RP):
            for h in range(2):
                x_codes[b, h] = at("x_codes%d%d" % (b, h), [P, HALF], U32,
                                   AT_LATEST + 2 * KB * (2 * b + h) if b + h else AT_PAGES[(LAST - 1) % PAGES])
                z_codes[b, h] = at("z_codes%d%d" % (b, h), [P, HALF], U32,
                                   AT_ZROWS + KB if (b, h) == (0, 1) else AT_LATEST + 8 * KB + 2 * KB * (2 * b + h))
        wv_codes = at("wv_codes", [P, RP * N], U32, AT_STAGED[LAST % 3])
        x_sc = at("x_sc", [P, RP, M], U8, AT_SC)
        z_sc = at("z_sc", [P, RP, M], U8, AT_SC + 2 * KB)
        wv_sc = at("wv_sc", [P, RP * N], U8, AT_SC + 4 * KB)

        def quantize(codes, scales, src):
            nc.vector.quantize_mx(out=codes.bitcast(FP8X4), scales=scales, in_=src.rearrange("p m t -> p (m t)"))

        def quantize_wv(b):
            nc.vector.quantize_mx(out=wv_codes[:, b * N:(b + 1) * N].bitcast(FP8X4), scales=wv_sc[:, b * N:(b + 1) * N],
                                  in_=wv_bf[:, b * N * PACK:(b + 1) * N * PACK])

        quantize(x_codes[0, 0][:], x_sc[:, 0, cols(0)], x_bf[0][:, cols(0)])
        last_parts = (slice(0, P), slice(P, HALF), cols(1))
        for part in last_parts:
            fetch(LAST, part)
        ge_last = [at("ge_last%d" % h, [P, HALF], F32, AT_ZROWS + 4 * KB * h) for h in range(2)]
        for part in last_parts[:2]:
            weave(nc.scalar.copy, x_bf[1, 0][:, part], x_rows(1)[:, :, part])
        weave(nc.scalar.copy, x_bf[1, 1][:, :X_BY_SCALAR], x_rows(1)[:, :, HALF:HALF + X_BY_SCALAR])
        for h in range(2):
            gelu(LAST, cols(h), ge_last[h][:])
        for h in range(2):
            gain(LAST, z_bf[1, h][:, :, PACK - 1], ge_last[h][:])

        quantize(x_codes[0, 1][:], x_sc[:, 0, cols(1)], x_bf[0][:, cols(1)])
        for b in range(RP):
            quantize_wv(b)
        quantize(z_codes[0, 0][:], z_sc[:, 0, cols(0)], z_bf[0][:, cols(0)])
        weave(nc.vector.tensor_copy, x_bf[1, 1][:, X_BY_SCALAR:], x_rows(1)[:, :, HALF + X_BY_SCALAR:])
        quantize(x_codes[1, 0][:], x_sc[:, 1, cols(0)], x_bf[1, 0][:])
        quantize(x_codes[1, 1][:], x_sc[:, 1, cols(1)], x_bf[1, 1][:])
        quantize(z_codes[1, 0][:], z_sc[:, 1, cols(0)], z_bf[1, 0][:])
        quantize(z_codes[0, 1][:], z_sc[:, 0, cols(1)], z_bf[0][:, cols(1)])
        quantize(z_codes[1, 1][:], z_sc[:, 1, cols(1)], z_bf[1, 1][:])

        def gate_pass(acc, n, b, h):
            nc.tensor.matmul_mx(out=acc[:], lhsT=w8_codes[:, b, P * n:P * (n + 1)].bitcast(FP8X4),
                                lhsT_scale=w8_sc[:, b, P * n:P * (n + 1)],
                                rhs=x_codes[b, h][:].bitcast(FP8X4), rhs_scale=x_sc[:, b, cols(h)],
                                start=(b == 0), stop=(b == RP - 1))

        def value_pass(acc, n, b, h):
            c0 = b * N + P * n
            nc.tensor.matmul_mx(out=acc[:], lhsT=wv_codes[:, c0:c0 + P].bitcast(FP8X4), lhsT_scale=wv_sc[:, c0:c0 + P],
                                rhs=z_codes[b, h][:].bitcast(FP8X4), rhs_scale=z_sc[:, b, cols(h)],
                                start=(b == 0), stop=(b == RP - 1))

        order = [(n, h) for h in range(2) for n in range(NT)]
        gate = {}
        for k, (n, h) in enumerate(order):
            gate[n, h] = bank(1 + k)
        for b in range(RP):
            for n, h in order:
                gate_pass(gate[n, h], n, b, h)
        th_all = at("th_all", [P, len(order), HALF], F32, AT_ZROWS - 11 * KB)
        for k, (n, h) in enumerate(order):
            for part in closing if k == len(order) - 1 else (cols(0),):
                nc.scalar.activation(th_all[:, k, part], gate[n, h][:, part], ACT.Tanh, scale=0.5)
        for k, (n, h) in enumerate(order):
            value = bank((7 + k) % 8)
            for b in range(RP):
                value_pass(value, n, b, h)
            res = at("res%d" % k, [P, HALF], F32, AT_PAGES[3] + 2 * KB * k)
            for part in closing if k == len(order) - 1 else (cols(0),):
                nc.vector.scalar_tensor_tensor(out=res[:, part], in0=th_all[:, k, part], scalar=1.0, in1=value[:, part],
                                               op0=ALU.add, op1=ALU.mult)
                nc.sync.dma_start(out[P * n:P * (n + 1), cols(h)][:, part], res[:, part])
